import numpy as np, ml_dtypes
CORES = [16,18,20,22]
N = 4
BF = ml_dtypes.bfloat16
def gentries(a):
    return np.ascontiguousarray(a.reshape(8, 16, -1).transpose(0, 2, 1)).reshape(8, -1)
def gtable(e):
    e = np.asarray(e); return np.ascontiguousarray(e.reshape(8, -1, 16).transpose(0, 2, 1)).reshape(128, -1).astype(np.int32)
W, S, U, H, C, R, TH, SH = 4096, 2048, 256, 2, 8, 4, 260, 8
B, LC = W // C, 3
def two(rng, lo, hi, shape):
    return np.where(rng.random(shape) < 0.5, lo, hi)
def pack(mu, fr, a, mix, s):
    return {"mu": np.ascontiguousarray(mu.reshape(N, 128, W)).astype(np.float32).astype(BF),
            "fr": np.ascontiguousarray(fr.reshape(N, 128, R * U)).astype(np.float32).astype(BF),
            "a0": np.ascontiguousarray(a.transpose(0, 1, 3, 2, 4)).reshape(N, 128, 16 * C).astype(np.float32).astype(BF),
            "mix": np.ascontiguousarray(mix.transpose(0, 1, 3, 2)).reshape(N, 128, S).astype(np.int32),
            "s0": np.stack([gtable(v) for v in s])}
def frames(rng, mu, mix, s):
    ri = np.arange(N)[:, None, None, None]; gi = np.arange(8)[None, :, None, None]
    st = (s[..., None] + (np.arange(R) * (H - 1)) // 2 + rng.integers(0, H, (N, 8, U, R))) & (S - 1)
    w = mix[ri, gi, st, rng.integers(0, 16, st.shape)]
    x = mu[ri, gi, :, w]
    x = np.where(rng.random((N, 8, U, R, 1)) < 0.5, np.clip(x + rng.integers(-3, 4, x.shape), -8, 7), rng.integers(-8, 8, x.shape))
    return np.ascontiguousarray(x.transpose(0, 1, 4, 3, 2))
def parts(rng):
    mu = rng.integers(-8, 8, (N, 8, 16, W))
    a = 64 * np.eye(16, dtype=np.int64) + rng.integers(-6, 7, (N, 8, C, 16, 16))
    wgt = np.exp2(rng.integers(0, 6, (8, C))); wgt[0] = 1.0; wgt[0, int(rng.integers(0, C))] = 32.0; wgt[1] = 1.0
    cum = np.add.accumulate(wgt, axis=1)
    v = rng.random((N, 8, S * 16, 1)) * cum[None, :, None, C - 1:]
    cl = np.minimum(np.add.reduce((v >= cum[None, :, None, :]).astype(np.int64), axis=-1), C - 1)
    mix = (cl * B + rng.integers(0, B, cl.shape)).reshape(N, 8, S, 16)
    s = rng.integers(0, S, (N, 8, U))
    return mu, a, mix, s
def setup_inputs(rng):
    mu, a, mix, s = parts(rng)
    return pack(mu, frames(rng, mu, mix, s), a, mix, s)
def setup_inputs_spread(rng):
    mu, a, mix, s = parts(rng)
    sz = np.array([1.0, 1.0, 0.5, 0.25, 0.125, 0.0])
    mu = np.floor(mu * rng.choice(sz, (N, 8, 1, W))).astype(np.int64)
    a = np.eye(16, dtype=np.int64) * rng.integers(16, 128, (N, 8, C, 1, 16)) + rng.integers(-127, 128, a.shape) * (rng.random(a.shape) < 0.0625)
    a = np.clip(a, -127, 127)
    mix[:, ::2] = np.minimum((W * rng.random((N, 4, S, 16)) ** 3).astype(np.int64), W - 1)
    s[:, 1::2] = np.minimum((S * rng.random((N, 4, U)) ** 4).astype(np.int64), S - 1)
    x = frames(rng, mu, mix, s)
    x = np.floor(x * rng.choice(sz, (N, 8, 1, R, U))).astype(np.int64)
    return pack(mu, x, a, mix, s)
def setup_inputs_ends(rng):
    mu = two(rng, -8, 7, (N, 8, 16, W)); x = two(rng, -8, 7, (N, 8, 16, R, U)); a = two(rng, -127, 127, (N, 8, C, 16, 16))
    kind = rng.integers(0, 3, (N, 8, S, 1))
    mix = np.where(kind == 0, 0, np.where(kind == 1, W - 1, two(rng, 0, W - 1, (N, 8, S, 16))))
    s = two(rng, 0, S - 1, (N, 8, U))
    mix[:, 7] = W - 1; mu[:, 7, :, W - 1] = -8; a[:, 7, C - 1] = 127; x[:, 7, :, 0::2] = 7; x[:, 7, :, 1::2] = -8
    mu[:, 6, :, 0] = -8; mu[:, 6, :, W - 1] = -8; a[:, 6, 0] = 127; a[:, 6, C - 1] = 127; x[:, 6] = two(rng, -8, 7, (N, 1, R, U))
    mix[:, 4] = W - 1; mu[:, 4, :, W - 1] = -8; a[:, 4, C - 1] = -127; x[:, 4] = -8
    return pack(mu, x, a, mix, s)
def setup_inputs_corners(rng):
    mu, a, mix, s = parts(rng); eye = 64 * np.eye(16, dtype=np.int64); low = (np.arange(16) < 8)[:, None]; slot = np.arange(16)[None, None, :]
    s[:, 2] = ((np.arange(N) & 1) * (S - 1))[:, None]
    mix[:, 3] = rng.choice(np.array([0, B - 1, B, W - 1]), (N, S, 1)); a[:, 3] = two(rng, -127, 127, (N, C, 16, 16))
    mix[:, 4] = rng.choice(np.concatenate([np.arange(C) * B, np.arange(C) * B + B - 1]), (N, S, 16))
    a[:, 5] = 0
    mu[:, 6] = rng.integers(-1, 2, (N, 16, W))
    s[:, 7] = rng.choice(np.array([0, 1, 2, 3, S - 2, S - 1]), (N, U))
    q = np.arange(W)[None, :] & 3
    mu[:, 0] = np.where(q == 0, 6, np.where(q == 1, -7, np.where(q == 2, np.where(low, 6, -8), np.where(low, -7, 7))))
    a[:, 0] = eye; ty = ((np.arange(S) // (H - 1)) & 1)[None, :, None]
    k = rng.integers(0, 16, (N, S, 1)); k[:, ::8] = 15; k[:, 3::8] = 0
    mix[:, 0] = 4 * rng.integers(0, W // 4, (N, S, 16)) + ty + 2 * (slot < k)
    s[:, 0] = (H - 1) * rng.integers(0, S // (H - 1), (N, U)); s[:, 0, :16] = S - (H - 1); s[:, 0, 16:32] = 0
    ft = rng.integers(0, 16, (N, 1, W))
    mu[:, 1] = -8 + ((np.arange(16)[None, :, None] == ft) & ((np.arange(W) & 1) == 1)[None, None, :]).astype(np.int64)
    a[:, 1] = eye; k = np.where(rng.random((N, S, 1)) < 0.5, rng.integers(1, 16, (N, S, 1)), 16)
    mix[:, 1] = 2 * rng.integers(0, W // 2, (N, S, 16)) + (slot < k)
    x = frames(rng, mu, mix, s)
    x[:, 6] = rng.integers(-1, 2, (N, 16, R, U)); x[:, 1] = -8
    cur = s[:, 0].copy(); u4 = (np.arange(U) & 3)[None, :]
    for t in range(R):
        mv = np.where(u4 == 0, 1, np.where(u4 == 1, 0, rng.integers(0, 2, (N, U))))
        x[:, 0, :, t] = np.where((((cur // (H - 1)) + mv) & 1) == 0, 7, -8)[:, None, :]
        cur = (cur + mv * (H - 1)) & (S - 1)
    return pack(mu, x, a, mix, s)
def setup_inputs_crowd(rng):
    mu, a, mix, s = parts(rng); T = N * U
    mix = ((np.arange(S) >> 4) & (C - 1))[None, None, :, None] * B + rng.integers(0, B, (N, 8, S, 16))
    kinds = [(1, TH - 1), (2, TH - 2), (3, TH - 3), (0, TH), (1, TH - 2)]
    for g in range(8):
        n = np.zeros((C // 2, 2), np.int64)
        if g == 0: n[C // 2 - 1, 1] = T
        elif g == 1: n[0, 0] = T - 1; n[C // 2 - 1, 1] = 1
        elif g == 2: n[0] = (TH, TH - 1); n[C // 2 - 1, 1] = T - 2 * TH + 1
        elif g in (3, 4):
            v = TH - 1 if g == 3 else TH; b = 2 * int(rng.integers(0, C // 4))
            h = v // 2 + int(rng.integers(-(v // 4), v // 4 + 1)); i = int(rng.integers(1, h)); j = int(rng.integers(1, v - h))
            n[b] = (i, h - i); n[b + 1] = (j, v - h - j)
            n[(b + C // 4) % (C // 2) + int(rng.integers(0, 2)), int(rng.integers(0, 2))] = T - v
        else:
            p = rng.permutation(C // 2)
            for i in range(3):
                v = kinds[(g + i) % 5]; n[p[i]] = v if rng.random() < 0.5 else v[::-1]
            n[p[3], int(rng.integers(0, 2))] = T - int(np.add.reduce(n.reshape(-1)))
        cl = rng.permutation(np.repeat(np.arange(C), n.reshape(-1))).reshape(N, U)
        s[:, g] = 16 * (cl + C * rng.integers(0, S // (16 * C), (N, U))) + rng.integers(0, 16 - R * (H - 1), (N, U))
    return pack(mu, frames(rng, mu, mix, s), a, mix, s)
def setup_inputs_tally(rng):
    mu, a, mix, s = parts(rng); T = N * U
    mix = ((np.arange(S) >> 4) & (C - 1))[None, None, :, None] * B + rng.integers(0, B, (N, 8, S, 16))
    for g in range(8):
        n = np.zeros(C, np.int64)
        if g in (0, 1, 2, 3, 7):
            q = N - 1 if g == 7 else int(rng.integers(0, N))
            c = C - 1 if g == 7 else 2 * int(rng.integers(0, C // 2)) + (1, 0, 0, 1)[g]
            m = TH - U - 1 if g == 3 else TH - U
            v = rng.choice(np.array([i for i in range(C) if i != c and (g != 3 or i != (c ^ 1))]), (N - 1) * U)
            v[:m] = c
            if g == 3: v[m] = c ^ 1
            v = rng.permutation(v).reshape(N - 1, U)
            cl = np.concatenate([v[:q], np.full((1, U), c, np.int64), v[q:]], axis=0)
        elif g == 4:
            o = 4 * int(rng.integers(0, C // 4)); p = (o + 4) % C; b = o + 2 * int(rng.integers(0, 2)); k = T - 2 * TH + 2
            n[b + int(rng.integers(0, 2))] = TH - 1; n[b ^ 2] = k // 2; n[(b ^ 2) + 1] = k - k // 2
            i = int(rng.integers(1, TH // 3)); j = int(rng.integers(1, TH // 3))
            n[p:p + 4] = rng.permutation(np.array([0, i, j, TH - 1 - i - j]))
            cl = rng.permutation(np.repeat(np.arange(C), n)).reshape(N, U)
        elif g == 5:
            p = rng.permutation(C // 2); k = TH // 15 + 1; left = T - 45 * k
            for i in range(3): n[2 * p[i]] = 7 * k; n[2 * p[i] + 1] = 8 * k
            n[2 * p[3]] = 7 * left // 15; n[2 * p[3] + 1] = left - 7 * left // 15
            cl = rng.permutation(np.repeat(np.arange(C), n)).reshape(N, U)
        else: cl = rng.integers(0, C, (N, U))
        s[:, g] = 16 * (cl + C * rng.integers(0, S // (16 * C), (N, U))) + rng.integers(0, 16 - R * (H - 1), (N, U))
    odd = ((np.arange(W) // B) & 1) == 1
    mu[:, 5] = np.where(odd[None, None, :], two(rng, 6, 7, (N, 16, W)), two(rng, -8, -7, (N, 16, W)))
    a[:, 5] = np.where((np.arange(C) & 1) == 1, -127, 127)[None, :, None, None]
    mu[:, 6, :14] = rng.integers(-8, -3, (N, 14, W)); a[:, 6, :, :14] = 127
    x = frames(rng, mu, mix, s)
    x[:, 5] = two(rng, 6, 7, (N, 16, R, U))
    x[:, 6, :14] = np.where(rng.random((N, 1, R, U)) < 0.5, 7, x[:, 6, :14])
    return pack(mu, x, a, mix, s)
def check_inputs(d):
    bad = []
    for k, lo, hi in (("mu", -8, 7), ("fr", -8, 7), ("a0", -127, 127), ("mix", 0, W - 1), ("s0", 0, S - 1)):
        v = np.asarray(d[k]).astype(np.float64)
        if not (np.min(v) >= lo and np.max(v) <= hi): bad.append("range of " + k)
        elif np.any(v != np.floor(v)): bad.append("whole numbers in " + k)
    return bad
def reference(mu, fr, a0, mix, s0):
    mi = mu.astype(np.float32).astype(np.int32).reshape(N, 8, 16, W)
    mf = np.ascontiguousarray(mi.reshape(N, 8, 16, C, B).transpose(0, 1, 3, 2, 4)).astype(np.float64)
    x = fr.astype(np.float32).astype(np.int32).reshape(N, 8, 16, R, U)
    a = a0.astype(np.float32).astype(np.int64).reshape(N, 8, 16, C, 16).transpose(0, 1, 3, 2, 4)
    lst = mix.astype(np.int64).reshape(N, 8, 16, S)
    s = np.stack([gentries(v) for v in s0]).astype(np.int64)
    yw = np.zeros((N, 8, R, U), np.float32)
    gi = np.arange(8)[:, None, None, None]; si = np.arange(16)[None, None, :, None]
    for t in range(R):
        z = np.matmul(a.astype(np.float64), mf).astype(np.int64)
        M = np.clip((z + 32) >> 6, -8, 7).astype(np.int32).transpose(0, 1, 3, 2, 4).reshape(N, 8, 16, W)
        G = np.zeros((8, C, 16, 16), np.int64); n = np.zeros((8, C), np.int64); new = []
        for r in range(N):
            st = (s[r][:, None, :] + np.arange(H)[None, :, None]) & (S - 1)
            cand = lst[r][gi, si, st[:, :, None, :]].reshape(8, 16 * H, U)
            mc = np.take_along_axis(M[r], cand.reshape(8, 1, 16 * H * U), 2).reshape(8, 16, 16 * H, U)
            xt = x[r, :, :, t]
            score = np.add.reduce(mc * (2 * xt[:, :, None, :] - mc), axis=1)
            k = np.argmax(score, axis=1)
            w = np.take_along_axis(cand, k[:, None, :], 1)[:, 0]
            e = xt - np.take_along_axis(M[r], w[:, None, :], 2)
            v = np.take_along_axis(mi[r], w[:, None, :], 2)
            hit = (w >> 9)[:, None, :] == np.arange(C)[None, :, None]
            left = (hit[:, :, None, :] * e[:, None]).astype(np.float64)
            G = G + np.matmul(left, v.transpose(0, 2, 1)[:, None].astype(np.float64)).astype(np.int64)
            n = n + np.add.reduce(hit.astype(np.int64), axis=2)
            yw[r, :, t] = w
            new.append((s[r] + (k >> 4)) & (S - 1))
        s = np.stack(new)
        took = np.zeros((8, C), bool); D = np.zeros_like(G)
        for l in range(LC + 1):
            gs = np.repeat(np.add.reduce(G.reshape(8, C >> l, 1 << l, 16, 16), axis=2), 1 << l, axis=1)
            ns = np.repeat(np.add.reduce(n.reshape(8, C >> l, 1 << l), axis=2), 1 << l, axis=1)
            now = (ns >= TH) & ~took
            D = np.where(now[:, :, None, None], gs, D); took = took | now
        a = np.clip(a + np.clip(D >> SH, -2, 2)[None], -127, 127)
    ya = np.ascontiguousarray(a.transpose(0, 1, 3, 2, 4)).reshape(N, 128, 16 * C)
    return {"ya": ya.astype(np.float32), "ys": s.astype(np.float32), "yw": yw.reshape(N, 8, R * U)}

@@ -1,0 +1,547 @@
+from concourse.bass import DstId, RemoteDMATransfer
+from concourse.mybir import AluOpType, ActivationFunctionType
+
+R = 4
+_B = {
+    "bfloat16": dict(MU=4096, FR=1024, XO=1024, XR0=4096, XR1=4096, XR2=4096, XR3=4096, AN=128, AB=128, L=1024,
+                     MW=4096, MG=2048, D=8192, CS=256, SG=256, VG=256, EG=256, ZR=480, I16=16, J=64, WB=144,
+                     ONE=136, NEG=136, ID=128, NID=128, E1=136, E2=136, Q64=64, BL=128, BR=512),
+    "float32": dict(AM=128, CF=512, SW=256, NL=64, NJ=8, NS=4, RK=48, OK=48, M1=16, M2=16, OWN=128, C1=128,
+                    C2=128, CUM=144, H=128, T2=128, YW=1024, YS=256, YA=128, PC=16, CI=144, C16=128, LOC=48, KA=48,
+                    KB=48, VC=48, SC1=128, SC2=128, SC3=128, ONF=128, BT=128, BF=128, IW=2056),
+    "int32": dict(MX=2056, S=16, SK=512, RI=16, HS=16, TI=128, IP=4, SLI=8),
+    "uint16": dict(S2=32, CL=512, RL=16, WL=16, GS=512, GL=1536, LH=16, SL=8, SLB=4),
+    "float16": dict(CM=512, BH=128),
+}
+SCRATCH = {}
+for _d in _B:
+    for _n in _B[_d]:
+        SCRATCH[_n] = ("sbuf", [128, _B[_d][_n]], _d)
+SCRATCH["D2"] = ("sbuf", [128, 32, 256], "bfloat16")
+SCRATCH["TT"] = ("sbuf", [128, 16, 136], "bfloat16")
+SCRATCH["VP"] = ("sbuf", [128, 16, 240], "bfloat16")
+for _k in range(8):
+    SCRATCH["P%d" % _k] = ("psum", [128, 512], "float32")
+
+NDMA = 24
+SEMAPHORES = (["pe", "dve", "act", "pool", "sent"] + ["d%d" % k for k in range(NDMA)]
+              + ["nar%d" % t for t in range(R)] + ["gar%d" % t for t in range(R)])
+
+A = AluOpType
+F = ActivationFunctionType
+
+PLAN = """g 1 4 6|g 1 2 4|g 0 2 4|g 0 6 8|g 1 6 8|c 0 0 2|c 1 0 2|c 0 8 9|s 1 2 4|q 0|q 1|g 0 4 6|g 0 9 12|g 1 9 12|
+g 1 14 15|s 0 2 4|m 2 0 4|z 2 0 4|c 1 8 9|s 1 6 8|s 0 4 6|g 1 12 14|g 0 12 14|s 0 6 8|g 0 14 16|s 1 4 6|m 3 4 8|q 8|
+g 1 15 16 0 8|s 0 9 12|s 1 9 12|m 2 8 12|z 2 8 12|z 3 4 8|s 1 12 14|s 1 14 15|g 1 15 16 8 16|a 1|f 0|s 0 12 14|
+s 0 14 16|m 2 12 14|f 2|a 2|s 1 15 16 0 8|m 3 14 16 0 8|s 1 15 16 8 16|m 3 14 16 8 16|f 1|a 3|a 4|z 2 12 14|
+z 3 14 16|a 7|f 3|b 1|a 5|a 6|b 2|a 9|b 3|b 4|a 10|a 11|b 7|a 13|b 5|b 6|h 0|b 9|a 12|b 11|a 14|b 10|a 15|a 17|b 12|
+a 16|b 14|b 15|b 13|h 1|a 8|b 8|b 16|a 18|b 17|p 0|b 18|p 1|h 2"""
+MORDER = "A0:2 D2:4 A4:6 C0:2 D6:8 A8:10 C4:6 D10:12 A12:14 C8:10 A14:16 C12:16"
+VCLS = (1, 3, 5)
+CBANK = (0, 1, 6, 7)
+ONACT = ((1, 16),)
+XPOOL = 7
+
+
+def _norm(rs):
+    out = []
+    for r in rs:
+        out.append((r, 0, 1 << 30) if isinstance(r, str) else r)
+    return out
+
+
+def make_sched(g, T):
+    queues = {"pe": g.tensor, "dve": g.vector, "act": g.scalar, "pool": g, "sync": g.sync}
+    known = {q: {} for q in queues}
+    count = {}
+    hist = {}
+    ndma = [0]
+
+    def wait_for(q, src, n, clock):
+        if known[q].get(src, 0) >= n:
+            return
+        queues[q].wait_ge(T.sem[src], n)
+        known[q][src] = n
+        for k, v in clock.items():
+            if known[q].get(k, 0) < v:
+                known[q][k] = v
+
+    def op(q, fn, r=(), w=(), dma=False, ext=None, track=True):
+        r = _norm(r)
+        w = _norm(w)
+        need = {}
+        for (regs, writing) in ((r, False), (w, True)):
+            for (name, lo, hi) in regs:
+                bank = name[0] == "P" and name[1:].isdigit()
+                for (plo, phi, pw, src, n, clock) in hist.get(name, ()):
+                    if src == "pe" and q == "pe":
+                        continue
+                    over = plo < hi and lo < phi
+                    if (over and (pw or writing)) or (bank and src != q):
+                        if need.get(src, (0, None))[0] < n:
+                            need[src] = (n, clock)
+        for src in sorted(need):
+            implied = False
+            for other in need:
+                if other != src and need[other][1].get(src, 0) >= need[src][0]:
+                    implied = True
+            if not implied:
+                wait_for(q, src, need[src][0], need[src][1])
+        if ext is not None:
+            wait_for(q, ext[0], ext[1], {})
+        ins = fn()
+        if not track:
+            return
+        if dma:
+            src = "d%d" % ndma[0]
+            ndma[0] += 1
+            step = 16
+        else:
+            src = q
+            step = 1
+        ins.then_inc(T.sem[src], step)
+        count[src] = count.get(src, 0) + step
+        clock = dict(known[q])
+        clock[src] = count[src]
+        for (regs, writing) in ((r, False), (w, True)):
+            for (name, lo, hi) in regs:
+                lst = hist.setdefault(name, [])
+                bank = name[0] == "P" and name[1:].isdigit()
+                lst[:] = [e for e in lst if not (lo <= e[0] and e[1] <= hi and (
+                    (writing and not bank) or (e[3] == src and (writing or not e[2]))))]
+                lst.append((lo, hi, writing, src, count[src], clock))
+
+    def finish(q):
+        for src in count:
+            wait_for(q, src, count[src], {})
+
+    return op, finish
+
+
+def rank_program(g, core, T, topo):
+    rank = T.rank_of(core)
+    if rank is None:
+        return
+    cores = list(T.cores)
+    n = len(cores)
+    op, finish = make_sched(g, T)
+    V, S_, PE = g.vector, g.scalar, g.tensor
+    P = [T["P%d" % k] for k in range(8)]
+    XR = [T["XR%d" % t] for t in range(R)]
+
+    def ts(out, in0, s1, s2, o0, o1, r, w, ext=None):
+        if o1 is None:
+            op("dve", lambda: V.tensor_scalar(out, in0, s1, None, o0), r, w, ext=ext)
+        else:
+            op("dve", lambda: V.tensor_scalar(out, in0, s1, s2, o0, o1), r, w, ext=ext)
+
+    def tt(out, in0, in1, o, r, w):
+        op("dve", lambda: V.tensor_tensor(out, in0, in1, o), r, w)
+
+    def cp(out, in_, r, w):
+        op("dve", lambda: V.tensor_copy(out, in_), r, w)
+
+    def ms(ap, c, w):
+        op("dve", lambda: V.memset(ap, c), (), w)
+
+    def act(out, in_, f, r, w, bias=0.0, scale=1.0, acc=None, ext=None):
+        op("act", lambda: S_.activation(out, in_, f, bias=bias, scale=scale, accum_out=acc), r, w, ext=ext)
+
+    def mm(out, lhsT, rhs, st, sp, r, w):
+        op("pe", lambda: PE.matmul(out, lhsT, rhs, st, sp), r, w)
+
+    def dma(q, out, in_, r, w):
+        eng = g.sync if q == "sync" else g.scalar
+        op(q, lambda: eng.dma_start(out, in_), r, w, dma=True)
+
+    def iota(out, pat, base, cm, w, flt=True):
+        if flt:
+            op("pool", lambda: g.iota(out, pat, base, cm, allow_small_or_imprecise_dtypes=True), (), w)
+        else:
+            op("pool", lambda: g.iota(out, pat, base, cm), (), w)
+
+    def sel(out, in_, pat, cmp, fill, base, cm, r, w):
+        op("pool", lambda: g.affine_select(out, in_, pat, cmp, fill, base, cm), r, w)
+
+    peers = [cores[(rank + k) % n] for k in range(1, n)]
+    mask = topo.mask(core, peers[0])
+    for c in peers[1:]:
+        mask &= topo.mask(core, c)
+    neng = bin(mask).count("1")
+    ids = [DstId(rid=topo.addr(c)[0], pnc=topo.addr(c)[1]) for c in peers]
+    sends = [0]
+
+    def send(src, dsts, sem, r):
+        def fn():
+            tr = RemoteDMATransfer(dst_ids=ids, dma_engine_mask=mask, remote_sem=T.sem[sem], src=src, dsts=dsts)
+            return g.remote_dma_fused([tr], local_sem=T.sem.sent)
+        op("pool", fn, r, (), track=False)
+        sends[0] += neng
+
+    def rg(name, a, b):
+        return (name, a, b)
+
+    dma("sync", T.AN[:], T.a0[:], (), ["AN"])
+    dma("act", T.FR[:, 0:256], T.fr[:, 0:256], (), [("FR", 0, 256)])
+    dma("act", T.S[:], T.s0[:], (), ["S"])
+    dma("act", T.MX[:, 2048:2056], T.mix[:, 0:8], (), [("MX", 2048, 2056)])
+    for k in range(4):
+        dma("sync", T.MU[:, 1024 * k:1024 * (k + 1)], T.mu[:, 1024 * k:1024 * (k + 1)], (),
+            [("MU", 1024 * k, 1024 * (k + 1))])
+    dma("sync", T.MX[:, 0:2048], T.mix[:], (), [("MX", 0, 2048)])
+    dma("sync", T.FR[:, 256:1024], T.fr[:, 256:1024], (), [("FR", 256, 1024)])
+
+    iota(T.IP[:, 0:1], [[0, 1]], 0, 1, [("IP", 0, 1)], flt=False)
+    iota(T.SLI[:], [[128, 8]], 0, 1, ["SLI"], flt=False)
+    iota(T.CI[:], [[1, 144]], 0, 0, ["CI"])
+    iota(T.C16[:], [[0, 8], [1, 16]], 0, 0, ["C16"])
+
+    ms(T.ZR[:], 0.0, ["ZR"])
+    ms(T.ONE[:], 1.0, ["ONE"])
+    ms(T.NEG[:], -1.0, ["NEG"])
+    ms(T.L[:], 0.0, ["L"])
+    for k in range(8):
+        act(T.VP[:, 2 * k:2 * k + 2, :], T.ZR[:], F.Identity, ["ZR"], ["VP0", "VP1"] if k == 7 else ["VPz%d" % k])
+    act(T.XO[:, 0:256], T.FR[:, 0:256], F.Identity, [("FR", 0, 256)], [("XO", 0, 256)], bias=192.0)
+    ts(T.IP[:, 1:2], T.IP[:, 0:1], 15, None, A.bitwise_and, None, [("IP", 0, 1)], [("IP", 1, 2)])
+    cp(T.SL[:], T.SLI[:], ["SLI"], ["SL"])
+    ts(T.SLB[:], T.SLI[:, 4:8], -512.0, None, A.add, None, ["SLI"], ["SLB"])
+    cp(T.PC[:, 0:2], T.IP[:, 0:2], [("IP", 0, 2)], [("PC", 0, 2)])
+    ms(T.ONF[:], 1.0, ["ONF"])
+    ms(T.CUM[:, 128:144], float(n * 128), [("CUM", 128, 144)])
+    PF, PM = T.PC[:, 0:1], T.PC[:, 1:2]
+    col = lambda k: T.PC[:, k:k + 1]
+    pr = [("PC", 0, 2)]
+    ts(T.I16[:], T.CI[:, 0:16], PM, 64.0, A.is_equal, A.mult, pr + ["CI"], ["I16"])
+    ms(T.Q64[:], 1.0 / 64, ["Q64"])
+    ms(T.BL[0:2, :], 1.0 / 128, ["BL"])
+    ms(T.BR[0:2, :], 1.0, ["BR"])
+    ms(T.BL[0:1, :], 192.0, ["BL"])
+    pc = [("PC", 0, 10)]
+
+    def columns():
+        ts(col(3), PM, -1.0, 15.0, A.mult, A.add, pr, [("PC", 3, 4)])
+        ts(col(7), PM, 15.0, 8192.0, A.is_equal, A.mult, pr, [("PC", 7, 8)])
+        ts(col(2), PM, -1.0, 31.0, A.mult, A.add, pr, [("PC", 2, 3)])
+        ts(col(4), PM, 1.0, None, A.add, None, pr, [("PC", 4, 5)])
+        ts(col(5), PM, -512.0, 2048.5, A.mult, A.add, pr, [("PC", 5, 6)])
+        tt(col(9), PF, col(3), A.add, pr + [("PC", 3, 4)], [("PC", 9, 10)])
+        ts(col(8), col(7), -6144.0, None, A.add, None, [("PC", 7, 8)], [("PC", 8, 9)])
+
+    def masks():
+        ts(T.SC2[:], T.C16[:], PM, -1.0e9, A.is_equal, A.mult, pc + ["C16"], ["SC2"])
+        ts(T.SC3[:], T.C16[:], col(4), 8192.0, A.is_equal, A.mult, pc + ["C16"], ["SC3"])
+        ts(T.WB[:], T.CI[:], col(9), -32.0, A.is_equal, A.mult, pc + ["CI"], ["WB"])
+        ts(T.J[:, 0:32], T.CI[:, 0:32], col(2), None, A.is_equal, None, pc + ["CI"], [("J", 0, 32)])
+        ts(T.J[:, 32:64], T.CI[:, 0:32], col(3), None, A.is_equal, None, pc + ["CI"], [("J", 32, 64)])
+        tt(T.SC2[:], T.SC2[:], T.SC3[:], A.add, ["SC2", "SC3"], ["SC2"])
+
+    def xr_names(t):
+        return ["XR%d#%d" % (t, i) for i in range(16)]
+
+    def xrep(t, i0, i1):
+        for i in range(i0, i1):
+            sel(XR[t][:, i:4096:16], T.FR[:, 256 * t:256 * t + 256], [[0, 256]], A.is_equal, 0.0, 0, 0,
+                [("FR", 256 * t, 256 * t + 256)], [xr_names(t)[i]])
+
+    def spread(hv, src, name):
+        lst, ln = (T.SL[:, 0:4], "SL") if hv == 0 else (T.SLB[:, 0:4], "SLB")
+        tt(T.L[:, 512 * hv:512 * hv + 512].indirect(lst), src[:, 64 * hv:64 * hv + 64], T.Q64[:], A.mult,
+           [rg(name, 64 * hv, 64 * hv + 64), ln, "Q64"], [rg("L", 512 * hv, 512 * hv + 512)])
+
+    def preload():
+        for c in VCLS:
+            mm(P[c][:], T.BL[0:2, :], T.BR[0:2, :], True, False, ["BL", "BR"], ["P%d" % c])
+
+    def turn(c, bank):
+        mm(P[bank][:, 16 * c:16 * c + 16], T.L[:, 128 * c:128 * c + 128], T.I16[:], True, True,
+           [rg("L", 128 * c, 128 * c + 128), "I16"], ["P%d" % bank])
+
+    sel(T.ID[:], T.ONE[:, 0:128], [[-1, 128]], A.is_equal, 0.0, 0, 1, ["ONE"], ["ID"])
+    sel(T.NID[:], T.NEG[:, 0:128], [[-1, 128]], A.is_equal, 0.0, 0, 1, ["NEG"], ["NID"])
+    xrep(0, 0, XPOOL)
+    sel(T.SC1[:], T.ONF[:], [[0, 4], [1, 32]], A.not_equal, -1.0e9, 0, 0, ["ONF"], ["SC1"])
+    sel(T.BT[:], T.ONF[:], [[-16, 8], [0, 16]], A.is_ge, 0.0, 0, 1, ["ONF"], ["BT"])
+    sel(T.E1[:], T.NEG[:], [[-16, 8], [-1, 17]], A.is_equal, 0.0, 0, 1, ["NEG"], ["E1"])
+    sel(T.BF[:], T.BT[:], [[16, 8], [0, 16]], A.is_ge, 0.0, 15, -1, ["BT"], ["BF"])
+    sel(T.E2[:], T.ONE[:], [[-16, 8], [0, 17]], A.is_equal, 0.0, 0, 1, ["ONE"], ["E2"])
+    iota(T.E1[:, 16:136:17], [[0, 8]], 0, 0, ["E1"])
+    iota(T.LOC[:, 0:16], [[0, 2], [1, 8]], 0, 0, [("LOC", 0, 16)])
+    iota(T.LOC[:, 16:32], [[0, 2], [2, 4], [0, 2]], 0, 0, [("LOC", 16, 32)])
+    iota(T.LOC[:, 32:48], [[0, 2], [4, 2], [0, 4]], 0, 0, [("LOC", 32, 48)])
+    xrep(1, 0, 16)
+
+    preload()
+    for hv in range(2):
+        spread(hv, T.AN, "AN")
+        for c in range(4 * hv, 4 * hv + 4):
+            turn(c, 6 + hv)
+    for hv in range(2):
+        cp(T.AB[:, 64 * hv:64 * hv + 64], P[6 + hv][:, 64 * hv:64 * hv + 64], ["P%d" % (6 + hv)],
+           [rg("AB", 64 * hv, 64 * hv + 64)])
+    for hv in range(2):
+        spread(hv, T.AB, "AB")
+
+    def lists():
+        cp(T.S2[:, 0:16], T.S[:], ["S"], [("S2", 0, 16)])
+        ts(T.S2[:, 16:32], T.S[:], 1.0, None, A.add, None, ["S"], [("S2", 16, 32)])
+
+    def cands():
+        op("dve", lambda: V.tensor_copy(T.CL[:], T.MX[:, 0:2056].indirect(T.S2[:, 0:32])), ["MX", "S2"], ["CL"])
+
+    def cands_f(k, nk=1):
+        a, b = 128 * k, 128 * (k + nk)
+        ts(T.CF[:, a:b], T.CL[:, a:b], -2048.0, None, A.add, None, ["CL"], [rg("CF", a, b)])
+
+    def tree_consts():
+        ts(col(10), PM, 1.0, None, A.subtract, None, pr, [("PC", 10, 11)])
+        ts(col(11), PM, 2.0, None, A.subtract, None, pr, [("PC", 11, 12)])
+        ts(col(12), PM, 4.0, None, A.subtract, None, pr, [("PC", 12, 13)])
+        ts(col(13), PM, 128.0, None, A.add, None, pr, [("PC", 13, 14)])
+        ts(T.KA[:], T.LOC[:], PM, None, A.is_equal, None, pr + ["LOC"], ["KA"])
+        for l in range(3):
+            ts(T.VC[:, 16 * l:16 * l + 8], T.LOC[:, 16 * l:16 * l + 8], 16.0, None, A.mult, None,
+               ["LOC"], [("VC", 16 * l, 16 * l + 8)])
+            ts(T.VC[:, 16 * l + 8:16 * l + 16], T.LOC[:, 16 * l + 8:16 * l + 16], -16.0, 128.0 - 16.0 * (1 << l),
+               A.mult, A.add, ["LOC"], [("VC", 16 * l + 8, 16 * l + 16)])
+            ts(T.KB[:, 16 * l:16 * l + 16], T.LOC[:, 16 * l:16 * l + 16], col(10 + l), None, A.is_equal, None,
+               [("PC", 10, 13), "LOC"], [("KB", 16 * l, 16 * l + 16)])
+        tt(T.KA[:], T.KA[:], T.KB[:], A.subtract, ["KA", "KB"], ["KA"])
+
+    for i in range(XPOOL, 16):
+        cp(XR[0][:, i:4096:16], T.FR[:, 0:256], [("FR", 0, 256)], [xr_names(0)[i]])
+    BIAS = 192.0 + 1.0 / 128
+    win = T.MW[:, 0:4096]
+
+    for t in range(R):
+        xr = xr_names(t)
+        for c in range(8):
+            mm(P[c][:], T.L[:, 128 * c:128 * c + 128], T.MU[:, 512 * c:512 * c + 512], c not in VCLS, True,
+               [rg("L", 128 * c, 128 * c + 128), rg("MU", 512 * c, 512 * c + 512)], ["P%d" % c])
+        toks = MORDER.split()
+        for tok in toks:
+            lo, hi = [256 * int(v) for v in tok[1:].split(":")]
+            c = lo // 512
+            a, b = lo - 512 * c, hi - 512 * c
+            if tok[0] == "A":
+                act(T.MW[:, lo:hi], P[c][:, a:b], F.Identity, ["P%d" % c], [rg("MW", lo, hi)],
+                    bias=0.0 if c in VCLS else BIAS)
+            elif tok[0] == "D":
+                ts(T.MW[:, lo:hi], P[c][:, a:b], 184.0, 199.0, A.max, A.min, ["P%d" % c], [rg("MW", lo, hi)])
+            else:
+                ts(T.MW[:, lo:hi], T.MW[:, lo:hi], 184.0, 199.0, A.max, A.min, [rg("MW", lo, hi)], [rg("MW", lo, hi)])
+        if t == 0:
+            lists()
+            columns()
+            masks()
+            cands()
+
+        slot = {}
+
+        def d2(j, h, p0=0, p1=16):
+            return rg("D2", 32 * j + 16 * h + p0, 32 * j + 16 * h + p1)
+
+        def cgath(h, j0, j1):
+            for j in range(j0, j1):
+                slot.setdefault(j, len(slot))
+            a = 1024 * h + 256 * slot[j0]
+            b = a + 256 * (j1 - j0)
+            act(T.MG[:, a:b], win.indirect(T.CL[:, 256 * h + 16 * j0:256 * h + 16 * j1]), F.Identity,
+                ["MW", "CL"], [rg("MG", a, b)])
+            for j in range(j0, j1):
+                bank = CBANK[slot[j]]
+                o = P[bank][:, 256 * h:256 * h + 256]
+                m0 = 1024 * h + 256 * slot[j]
+                mm(o, T.NID[:], XR[t][:, 256 * j:256 * j + 256], True, False, ["NID"] + xr, ["P%d" % bank])
+                mm(o, T.ID[:], T.MG[:, m0:m0 + 256], False, True, ["ID", rg("MG", m0, m0 + 256)], ["P%d" % bank])
+
+        def csq(j):
+            bank = CBANK[slot[j]]
+            act(T.D2[:, 2 * j:2 * j + 2, :], P[bank][:], F.Square, ["P%d" % bank], [d2(j, 0), d2(j, 1)], bias=-192.0)
+
+        def gath(h, j0, j1, p0=0, p1=16):
+            e0, e1 = 16 * j0 + p0, 16 * (j1 - 1) + p1
+            a, b = 4096 * h + 16 * e0, 4096 * h + 16 * e1
+            tt(T.D[:, a:b], win.indirect(T.CL[:, 256 * h + e0:256 * h + e1]), XR[t][:, 16 * e0:16 * e1],
+               A.subtract, ["MW", "CL"] + xr, [rg("D", a, b)])
+
+        def sq(h, j0, j1, p0=0, p1=16):
+            e0, e1 = 16 * j0 + p0, 16 * (j1 - 1) + p1
+            a, b = 4096 * h + 16 * e0, 4096 * h + 16 * e1
+            act(T.D2[:, 2 * j0 + h:2 * j1:2, 16 * p0:16 * p1], T.D[:, a:b], F.Square, [rg("D", a, b)],
+                [d2(j, h, p0, p1) for j in range(j0, j1)], bias=-192.0)
+
+        def score(bank, j0, j1, p0=0, p1=16):
+            for p in range(p0, p1):
+                mm(P[bank][:, 0:32 * (j1 - j0)], T.WB[:, 15 - p:143 - p], T.D2[:, 2 * j0:2 * j1, 16 * p:16 * p + 16],
+                   p == 0, p == 15, ["WB"] + [d2(j, h, p, p + 1) for j in range(j0, j1) for h in range(2)],
+                   ["P%d" % bank])
+
+        def scan(bank, j0, j1):
+            w = 32 * (j1 - j0)
+            op("dve", lambda: V.tensor_tensor_scan(T.SK[:, 32 * j0:32 * j1], T.SC1[:, 0:w], P[bank][:, 0:w], 0.0,
+                                                   A.add, A.max),
+               ["SC1", "P%d" % bank], [rg("SK", 32 * j0, 32 * j1)])
+
+        tn = lambda k: ("TT", k, k + 1)
+        nown = rg("NL", 16 * t + 8, 16 * t + 10)
+
+        def step(hf, k):
+            j0, j1 = 8 * hf, 8 * hf + 8
+            u0, u1 = 128 * hf, 128 * hf + 128
+            bx, by, bv = (4, 5, 2) if hf == 0 else (0, 1, 3)
+            px, py = "P%d" % bx, "P%d" % by
+            if k == 1:
+                ts(T.RI[:, j0:j1], T.SK[:, 32 * j0 + 31:32 * j1:32], 31, None, A.bitwise_and, None,
+                   [rg("SK", 32 * j0, 32 * j1)], [rg("RI", j0, j1)])
+            elif k == 2:
+                cp(T.RL[:, j0:j1], T.RI[:, j0:j1], [rg("RI", j0, j1)], [rg("RL", j0, j1)])
+                if t == 0 and hf == 0:
+                    cp(T.BH[:], T.BF[:], ["BF"], ["BH"])
+            elif k in (3, 4):
+                h = k - 3
+                a, b = 256 * h + u0, 256 * h + u1
+                tt(T.CM[:, a:b], T.J[:, 32 * h:32 * h + 32].indirect(T.RL[:, j0:j1]), T.CF[:, a:b], A.mult,
+                   ["J", rg("RL", j0, j1), rg("CF", a, b)], [rg("CM", a, b)])
+                for bank in (bx, by):
+                    mm(P[bank][:, 0:128], T.BH[:], T.CM[:, a:b], h == 0, h == 1, ["BH", rg("CM", a, b)],
+                       ["P%d" % bank])
+            elif k == 5:
+                op("dve", lambda: V.tensor_tensor_scan(T.SW[:, u0:u1], T.SC2[:], P[bx][:, 0:128], 0.0, A.add, A.max),
+                   ["SC2", px], [rg("SW", u0, u1)])
+            elif k == 6:
+                act(T.CS[:, u0:u1], P[by][:, 0:128], F.Identity, [py], [rg("CS", u0, u1)],
+                    bias=6144.0 + 128.0 - 255.5 / 16, scale=1.0 / 16)
+                mm(P[bx][:, 0:136], T.CS[:, u0:u1], T.E2[:], True, False, [rg("CS", u0, u1), "E2"], [px])
+            elif k == 7:
+                act(T.SG[:, u0:u1], P[by][:, 0:128], F.Sign, [py] + pc,
+                    [rg("SG", u0, u1), rg("NL", 16 * t + 8 + hf, 16 * t + 9 + hf)], bias=col(5),
+                    acc=T.NL[:, 16 * t + 8 + hf:16 * t + 9 + hf])
+                if t == 0:
+                    send(T.NL[:, 8 + hf:9 + hf], [T.NL[:, 2 * k2 + hf:2 * k2 + hf + 1] for k2 in range(1, n)], "nar0",
+                         [rg("NL", 8 + hf, 9 + hf)])
+                elif hf == 1:
+                    send(T.NL[:, 16 * t + 8:16 * t + 10],
+                         [T.NL[:, 16 * t + 2 * k2:16 * t + 2 * k2 + 2] for k2 in range(1, n)], "nar%d" % t, [nown])
+            elif k == 8:
+                a = 256 * t + u0
+                act(T.YW[:, a:a + 128], P[by][:, 0:128], F.Identity, [py], [rg("YW", a, a + 128)], bias=2048.0)
+                if hf == 1:
+                    dma("sync", T.yw[:, 256 * t:256 * t + 256], T.YW[0:128:16, 256 * t:256 * t + 256],
+                        [rg("YW", 256 * t, 256 * t + 256)], ())
+            elif k == 9:
+                ts(T.WL[:, j0:j1], T.SW[:, u0 + 15:u1:16], col(8), None, A.add, None, [rg("SW", u0, u1)] + pc,
+                   [rg("WL", j0, j1)])
+            elif k == 10:
+                act(T.VG[:, u0:u1], T.MU[:, 0:4096].indirect(T.WL[:, j0:j1]), F.Identity, ["MU", rg("WL", j0, j1)],
+                    [rg("VG", u0, u1)])
+                mm(P[bv][:, 0:128], T.VG[:, u0:u1], T.ID[:], True, True, [rg("VG", u0, u1), "ID"], ["P%d" % bv])
+            elif k == 11:
+                tt(T.EG[:, u0:u1], win.indirect(T.WL[:, j0:j1]), T.XO[:, 256 * t + u0:256 * t + u1], A.subtract,
+                   ["MW", rg("WL", j0, j1), rg("XO", 256 * t, 256 * t + 256)], [rg("EG", u0, u1)])
+                mm(P[bx][:, 0:136], T.EG[:, u0:u1], T.E1[:], False, True, [rg("EG", u0, u1), "E1"], [px])
+            elif k == 12:
+                if (hf, k) in ONACT:
+                    act(T.TT[:, j0, :], P[bx][:, 0:136], F.Identity, [px], [tn(j0)], bias=16.0 - 6144.0)
+                else:
+                    ts(T.TT[:, j0, :], P[bx][:, 0:136], 16.0 - 6144.0, None, A.add, None, [px], [tn(j0)])
+            elif k == 13:
+                act(T.VP[:, j0:j1, 112:128], P[bv][:, 0:128], F.Identity, ["P%d" % bv], ["VP%d" % hf])
+            elif k in (14, 15, 16):
+                for c in ((1, 2, 3), (4, 5), (6, 7))[k - 14]:
+                    if (hf, k) in ONACT:
+                        act(T.TT[:, j0 + c, :], T.TT[:, j0, :], F.Relu, [tn(j0)], [tn(j0 + c)], bias=-32.0 * c)
+                    else:
+                        ts(T.TT[:, j0 + c, :], T.TT[:, j0, :], -32.0 * c, 0.0, A.add, A.max, [tn(j0)], [tn(j0 + c)])
+            elif k in (17, 18):
+                cv = k - 17
+                for s in range(8):
+                    mm(P[6 + cv][:, 0:68], T.VP[:, j0 + s, 112 - 16 * s:240 - 16 * s],
+                       T.TT[:, j0 + 4 * cv:j0 + 4 * cv + 4, 17 * s:17 * s + 17], hf == 0 and s == 0,
+                       hf == 1 and s == 7, ["VP%d" % hf, rg("TT", j0 + 4 * cv, j0 + 4 * cv + 4)], ["P%d" % (6 + cv)])
+
+        def state(k):
+            if k == 0:
+                ts(T.HS[:], T.RI[:], 16.0, None, A.is_lt, None, ["RI"], ["HS"])
+            elif k == 1:
+                tt(T.S[:], T.S[:], T.HS[:], A.add, ["S", "HS"], ["S"])
+            else:
+                lists()
+
+        def pack(cv):
+            for c in range(4 * cv, 4 * cv + 4):
+                a = 128 * t + 16 * c
+                bank, c0 = 6 + cv, 17 * (c % 4)
+                ts(T.GS[:, a:a + 16], P[bank][:, c0:c0 + 16], P[bank][:, c0 + 16:c0 + 17], 32768.0,
+                   A.subtract, A.add, ["P%d" % bank], [rg("GS", a, a + 16)])
+
+        calls = {"c": cgath, "q": csq, "g": gath, "s": sq, "m": score, "z": scan, "a": lambda k: step(0, k),
+                 "b": lambda k: step(1, k), "h": state, "p": pack, "f": cands_f}
+        for tok in PLAN.replace("\n", "").split("|"):
+            f = tok.split()
+            calls[f[0]](*[int(v) for v in f[1:]])
+        gs = rg("GS", 128 * t, 128 * t + 128)
+        send(T.GS[:, 128 * t:128 * t + 128],
+             [T.GL[:, 384 * t + 128 * k:384 * t + 128 * k + 128] for k in range(n - 1)], "gar%d" % t, [gs])
+        if t + 2 < R:
+            xrep(t + 2, 0, 16)
+        if t == 2:
+            iota(T.IW[:, 0:2048], [[1, 2048]], 0, 0, [("IW", 0, 2048)])
+            iota(T.IW[:, 2048:2056], [[1, 8]], 0, 0, [("IW", 2048, 2056)])
+
+        if t == 0:
+            tree_consts()
+            act(T.XO[:, 256:1024], T.FR[:, 256:1024], F.Identity, ["FR"], [("XO", 256, 1024)], bias=192.0)
+        if t == R - 1:
+            act(T.YS[:], T.IW[:, 0:2056].indirect(T.S2[:, 0:16]), F.Identity, ["IW", "S2"], ["YS"])
+            dma("sync", T.ys[:], T.YS[0:128:16, :], ["YS"], ())
+        act(T.AM[:], T.AB[:], F.Identity, ["AB"], ["AM"], bias=-127.5 / 256)
+        if t < R - 1:
+            preload()
+        act(T.NJ[:], T.NL[:, 16 * t + 2:16 * t + 10], F.Identity, [nown], ["NJ", "NS"], acc=T.NS[:, 0:1],
+            ext=("nar%d" % t, neng * (n - 1) * (2 if t == 0 else 1)))
+        act(T.RK[:], T.KA[:], F.Identity, ["KA", "NS"], ["RK"], scale=T.NS[:, 0:1])
+        mm(P[4][:, 0:48], T.BF[:], T.RK[:], True, True, ["BF", "RK"], ["P4"])
+        ts(T.OWN[:], T.GS[:, 128 * t:128 * t + 128], 1.0 / 256, None, A.mult, None, [gs], ["OWN"])
+        ts(P[2][:, 0:128], T.AB[:], -2.0, -127.0, A.add, A.max, ["AB"], [("P2", 0, 128)])
+        ts(P[2][:, 128:256], T.AB[:], 2.0, 127.0, A.add, A.min, ["AB"], [("P2", 128, 256)])
+        if t < R - 1:
+            cands()
+        ts(T.OK[:], P[4][:, 0:48], 519.0, None, A.is_ge, None, ["P4"], ["OK"])
+        tt(T.OK[:], T.OK[:], T.VC[:], A.mult, ["OK", "VC"], ["OK"])
+        tt(T.M1[:], T.OK[:, 0:16], T.OK[:, 16:32], A.max, ["OK"], ["M1"])
+        tt(T.M2[:], T.M1[:], T.OK[:, 32:48], A.max, ["OK", "M1"], ["M2"])
+        ts(T.LH[:, 0:8], T.M2[:, 0:8], PM, None, A.add, None, ["M2", "PC"], [("LH", 0, 8)])
+        ts(T.LH[:, 8:16], T.M2[:, 8:16], -1.0, col(13), A.mult, A.add, ["M2", "PC"], [("LH", 8, 16)])
+        ts(P[0][:, 0:256], T.GL[:, 384 * t:384 * t + 256], 1.0 / 256, None, A.mult, None, [], [rg("P0", 0, 256)],
+           ext=("gar%d" % t, neng * (n - 1)))
+        ts(T.C2[:], T.GL[:, 384 * t + 256:384 * t + 384], 1.0 / 256, None, A.mult, None, [], ["C2"])
+        tt(T.C1[:], P[0][:, 0:128], T.OWN[:], A.add, [rg("P0", 0, 128), "OWN"], ["C1"])
+        hv2 = [(0, 64), (64, 128)]
+        for (a, b) in hv2:
+            tt(P[0][:, 256 + a:256 + b], P[0][:, 128 + a:128 + b], T.C2[:, a:b], A.add,
+               [rg("P0", 128 + a, 128 + b), "C2"], [rg("P0", 256 + a, 256 + b)])
+        for (a, b) in hv2:
+            tt(T.CUM[:, a:b], P[0][:, 256 + a:256 + b], T.C1[:, a:b], A.add, [rg("P0", 256 + a, 256 + b), "C1"],
+               [rg("CUM", a, b)])
+        cw = T.CUM[:, 0:144]
+        for hv, (a, b) in enumerate(hv2):
+            tt(T.H[:, a:b], cw.indirect(T.LH[:, 8 + 4 * hv:12 + 4 * hv]), T.AM[:, a:b], A.subtract,
+               ["CUM", "LH", "AM"], [rg("H", a, b)])
+        for hv, (a, b) in enumerate(hv2):
+            tt(T.TI[:, a:b], cw.indirect(T.LH[:, 4 * hv:4 * hv + 4]), T.H[:, a:b], A.subtract,
+               ["CUM", "LH", rg("H", a, b)], [rg("TI", a, b)])
+        for (a, b) in hv2:
+            tt(T.T2[:, a:b], T.TI[:, a:b], P[2][:, a:b], A.max, [rg("TI", a, b), "P2"], [rg("T2", a, b)])
+        for (a, b) in hv2:
+            tt(T.AB[:, a:b], T.T2[:, a:b], P[2][:, 128 + a:128 + b], A.min, [rg("T2", a, b), "P2"], [rg("AB", a, b)])
+        for hv in range(2):
+            spread(hv, T.AB, "AB")
+
+    for c in range(8):
+        turn(c, 4 + c // 4)
+    act(T.YA[:, 0:64], P[4][:, 0:64], F.Identity, ["P4"], [rg("YA", 0, 64)])
+    cp(T.YA[:, 64:128], P[5][:, 64:128], ["P5"], [rg("YA", 64, 128)])
+    dma("sync", T.ya[:], T.YA[:], ["YA"], ())
+    g.wait_ge(T.sem.sent, sends[0])
+    finish("sync")

@@ -6,7 +6,7 @@ _B = {
     "bfloat16": dict(MU=4096, FR=1024, XO=1024, XR0=4096, XR1=4096, XR2=4096, XR3=4096, AN=128, AB=128, L=1024,
                      MW=4096, MG=2048, D=8192, CS=256, SG=256, VG=256, EG=256, ZR=480, I16=16, J=64, WB=144,
                      ONE=136, NEG=136, ID=128, NID=128, E1=136, E2=136, Q64=64, BL=128, BR=512),
-    "float32": dict(AM=128, CF=512, SW=256, NL=64, NJ=8, NS=4, RK=48, OK=48, M1=16, M2=16, OWN=128, C1=128,
+    "float32": dict(AM=128, CF=512, SW=256, NL=64, NJ=8, NS=4, RK=48, OK=48, M1=16, M2=16, OWN=144, C1=128,
                     C2=128, CUM=144, H=128, T2=128, YW=1024, YS=256, YA=128, PC=16, CI=144, C16=128, LOC=48, KA=48,
                     KB=48, VC=48, SC1=128, SC2=128, SC3=128, ONF=128, BT=128, BF=128, IW=2056),
     "int32": dict(MX=2056, S=16, SK=512, RI=16, HS=16, TI=128, IP=4, SLI=8),
@@ -35,12 +35,17 @@ g 1 14 15|s 0 2 4|m 2 0 4|z 2 0 4|c 1 8 9|s 1 6 8|s 0 4 6|g 1 12 14|g 0 12 14|s 
 g 1 15 16 0 8|s 0 9 12|s 1 9 12|m 2 8 12|z 2 8 12|z 3 4 8|s 1 12 14|s 1 14 15|g 1 15 16 8 16|a 1|f 0|s 0 12 14|
 s 0 14 16|m 2 12 14|f 2|a 2|s 1 15 16 0 8|m 3 14 16 0 8|s 1 15 16 8 16|m 3 14 16 8 16|f 1|a 3|a 4|z 2 12 14|
 z 3 14 16|a 7|f 3|b 1|a 5|a 6|b 2|a 9|b 3|b 4|a 10|a 11|b 7|a 13|b 5|b 6|h 0|b 9|a 12|b 11|a 14|b 10|a 15|a 17|b 12|
-a 16|b 14|b 15|b 13|h 1|a 8|b 8|b 16|a 18|b 17|p 0|b 18|p 1|h 2"""
-MORDER = "A0:2 D2:4 A4:6 C0:2 D6:8 A8:10 C4:6 D10:12 A12:14 C8:10 A14:16 C12:16"
+a 16|b 14|b 15|b 13|h 1|a 8|b 8|b 16|a 18|b 17|h 2|l 0|p 0|b 18|p 1|l 1"""
+PLAN0 = PLAN
+MORDER = "A0:2 D2:4 A4:6 D6:8 A8:10 C0:2 D10:12 C4:6 A12:14 C8:10 A14:16 C12:14 C14:16"
 VCLS = (1, 3, 5)
 CBANK = (0, 1, 6, 7)
+CUT = (0, 4, 8)
 ONACT = ((1, 16),)
 XPOOL = 7
+XACT = 5
+VACT = 5
+XLATE = 6
 
 
 def _norm(rs):
@@ -194,50 +199,50 @@ def rank_program(g, core, T, topo):
     iota(T.IP[:, 0:1], [[0, 1]], 0, 1, [("IP", 0, 1)], flt=False)
     iota(T.SLI[:], [[128, 8]], 0, 1, ["SLI"], flt=False)
     iota(T.CI[:], [[1, 144]], 0, 0, ["CI"])
-    iota(T.C16[:], [[0, 8], [1, 16]], 0, 0, ["C16"])
 
     ms(T.ZR[:], 0.0, ["ZR"])
     ms(T.ONE[:], 1.0, ["ONE"])
     ms(T.NEG[:], -1.0, ["NEG"])
     ms(T.L[:], 0.0, ["L"])
-    for k in range(8):
-        act(T.VP[:, 2 * k:2 * k + 2, :], T.ZR[:], F.Identity, ["ZR"], ["VP0", "VP1"] if k == 7 else ["VPz%d" % k])
-    act(T.XO[:, 0:256], T.FR[:, 0:256], F.Identity, [("FR", 0, 256)], [("XO", 0, 256)], bias=192.0)
+
+    def xr_names(t):
+        return ["XR%d#%d" % (t, i) for i in range(16)]
+
+    for k in range(VACT):
+        act(T.VP[:, 2 * k:2 * k + 2, :], T.ZR[:], F.Identity, ["ZR"], [rg("VP", 2 * k, 2 * k + 2)])
+    for i in range(16 - XACT, 16):
+        act(XR[0][:, i:4096:16], T.FR[:, 0:256], F.Identity, [("FR", 0, 256)], [xr_names(0)[i]])
     ts(T.IP[:, 1:2], T.IP[:, 0:1], 15, None, A.bitwise_and, None, [("IP", 0, 1)], [("IP", 1, 2)])
     cp(T.SL[:], T.SLI[:], ["SLI"], ["SL"])
     ts(T.SLB[:], T.SLI[:, 4:8], -512.0, None, A.add, None, ["SLI"], ["SLB"])
     cp(T.PC[:, 0:2], T.IP[:, 0:2], [("IP", 0, 2)], [("PC", 0, 2)])
-    ms(T.ONF[:], 1.0, ["ONF"])
-    ms(T.CUM[:, 128:144], float(n * 128), [("CUM", 128, 144)])
+    ms(T.Q64[:], 1.0 / 64, ["Q64"])
+    ms(T.BL[0:2, :], 1.0 / 128, ["BL"])
     PF, PM = T.PC[:, 0:1], T.PC[:, 1:2]
     col = lambda k: T.PC[:, k:k + 1]
     pr = [("PC", 0, 2)]
+    pc = [("PC", 0, 10)]
     ts(T.I16[:], T.CI[:, 0:16], PM, 64.0, A.is_equal, A.mult, pr + ["CI"], ["I16"])
-    ms(T.Q64[:], 1.0 / 64, ["Q64"])
-    ms(T.BL[0:2, :], 1.0 / 128, ["BL"])
     ms(T.BR[0:2, :], 1.0, ["BR"])
     ms(T.BL[0:1, :], 192.0, ["BL"])
-    pc = [("PC", 0, 10)]
+    ts(col(3), PM, -1.0, 15.0, A.mult, A.add, pr, [("PC", 3, 4)])
+    ts(col(7), PM, 15.0, 8192.0, A.is_equal, A.mult, pr, [("PC", 7, 8)])
+    ts(col(2), PM, -1.0, 31.0, A.mult, A.add, pr, [("PC", 2, 3)])
+    tt(col(9), PF, col(3), A.add, pr + [("PC", 3, 4)], [("PC", 9, 10)])
+    ms(T.ONF[:], 1.0, ["ONF"])
 
-    def columns():
-        ts(col(3), PM, -1.0, 15.0, A.mult, A.add, pr, [("PC", 3, 4)])
-        ts(col(7), PM, 15.0, 8192.0, A.is_equal, A.mult, pr, [("PC", 7, 8)])
-        ts(col(2), PM, -1.0, 31.0, A.mult, A.add, pr, [("PC", 2, 3)])
-        ts(col(4), PM, 1.0, None, A.add, None, pr, [("PC", 4, 5)])
-        ts(col(5), PM, -512.0, 2048.5, A.mult, A.add, pr, [("PC", 5, 6)])
-        tt(col(9), PF, col(3), A.add, pr + [("PC", 3, 4)], [("PC", 9, 10)])
-        ts(col(8), col(7), -6144.0, None, A.add, None, [("PC", 7, 8)], [("PC", 8, 9)])
-
-    def masks():
-        ts(T.SC2[:], T.C16[:], PM, -1.0e9, A.is_equal, A.mult, pc + ["C16"], ["SC2"])
-        ts(T.SC3[:], T.C16[:], col(4), 8192.0, A.is_equal, A.mult, pc + ["C16"], ["SC3"])
-        ts(T.WB[:], T.CI[:], col(9), -32.0, A.is_equal, A.mult, pc + ["CI"], ["WB"])
-        ts(T.J[:, 0:32], T.CI[:, 0:32], col(2), None, A.is_equal, None, pc + ["CI"], [("J", 0, 32)])
-        ts(T.J[:, 32:64], T.CI[:, 0:32], col(3), None, A.is_equal, None, pc + ["CI"], [("J", 32, 64)])
-        tt(T.SC2[:], T.SC2[:], T.SC3[:], A.add, ["SC2", "SC3"], ["SC2"])
-
-    def xr_names(t):
-        return ["XR%d#%d" % (t, i) for i in range(16)]
+    def masks(k):
+        if k == 0:
+            ts(col(4), PM, 1.0, None, A.add, None, pr, [("PC", 4, 5)])
+            ts(col(5), PM, -512.0, 2048.5, A.mult, A.add, pr, [("PC", 5, 6)])
+            ts(col(8), col(7), -6144.0, None, A.add, None, [("PC", 7, 8)], [("PC", 8, 9)])
+            ts(T.SC2[:], T.C16[:], PM, -1.0e9, A.is_equal, A.mult, pc + ["C16"], ["SC2"])
+            ts(T.SC3[:], T.C16[:], col(4), 8192.0, A.is_equal, A.mult, pc + ["C16"], ["SC3"])
+        else:
+            ts(T.J[:, 0:32], T.CI[:, 0:32], col(2), None, A.is_equal, None, pc + ["CI"], [("J", 0, 32)])
+            ts(T.J[:, 32:64], T.CI[:, 0:32], col(3), None, A.is_equal, None, pc + ["CI"], [("J", 32, 64)])
+            cp(T.BH[:], T.BF[:], ["BF"], ["BH"])
+            tt(T.SC2[:], T.SC2[:], T.SC3[:], A.add, ["SC2", "SC3"], ["SC2"])
 
     def xrep(t, i0, i1):
         for i in range(i0, i1):
@@ -259,6 +264,7 @@ def rank_program(g, core, T, topo):
 
     sel(T.ID[:], T.ONE[:, 0:128], [[-1, 128]], A.is_equal, 0.0, 0, 1, ["ONE"], ["ID"])
     sel(T.NID[:], T.NEG[:, 0:128], [[-1, 128]], A.is_equal, 0.0, 0, 1, ["NEG"], ["NID"])
+    iota(T.C16[:], [[0, 8], [1, 16]], 0, 0, ["C16"])
     xrep(0, 0, XPOOL)
     sel(T.SC1[:], T.ONF[:], [[0, 4], [1, 32]], A.not_equal, -1.0e9, 0, 0, ["ONF"], ["SC1"])
     sel(T.BT[:], T.ONF[:], [[-16, 8], [0, 16]], A.is_ge, 0.0, 0, 1, ["ONF"], ["BT"])
@@ -266,49 +272,55 @@ def rank_program(g, core, T, topo):
     sel(T.BF[:], T.BT[:], [[16, 8], [0, 16]], A.is_ge, 0.0, 15, -1, ["BT"], ["BF"])
     sel(T.E2[:], T.ONE[:], [[-16, 8], [0, 17]], A.is_equal, 0.0, 0, 1, ["ONE"], ["E2"])
     iota(T.E1[:, 16:136:17], [[0, 8]], 0, 0, ["E1"])
+    for k in range(VACT, 8):
+        iota(T.VP[:, 2 * k:2 * k + 2, :], [[0, 2], [0, 240]], 0, 0, [rg("VP", 2 * k, 2 * k + 2)])
     iota(T.LOC[:, 0:16], [[0, 2], [1, 8]], 0, 0, [("LOC", 0, 16)])
     iota(T.LOC[:, 16:32], [[0, 2], [2, 4], [0, 2]], 0, 0, [("LOC", 16, 32)])
     iota(T.LOC[:, 32:48], [[0, 2], [4, 2], [0, 4]], 0, 0, [("LOC", 32, 48)])
-    xrep(1, 0, 16)
+    xrep(1, 0, 16 - XLATE)
+
+    def lists():
+        cp(T.S2[:, 0:16], T.S[:], ["S"], [("S2", 0, 16)])
+        ts(T.S2[:, 16:32], T.S[:], 1.0, None, A.add, None, ["S"], [("S2", 16, 32)])
 
     preload()
     for hv in range(2):
         spread(hv, T.AN, "AN")
         for c in range(4 * hv, 4 * hv + 4):
             turn(c, 6 + hv)
-    for hv in range(2):
-        cp(T.AB[:, 64 * hv:64 * hv + 64], P[6 + hv][:, 64 * hv:64 * hv + 64], ["P%d" % (6 + hv)],
-           [rg("AB", 64 * hv, 64 * hv + 64)])
+    cp(T.AB[:, 0:64], P[6][:, 0:64], ["P6"], [rg("AB", 0, 64)])
+    lists()
+    cp(T.AB[:, 64:128], P[7][:, 64:128], ["P7"], [rg("AB", 64, 128)])
     for hv in range(2):
         spread(hv, T.AB, "AB")
-
-    def lists():
-        cp(T.S2[:, 0:16], T.S[:], ["S"], [("S2", 0, 16)])
-        ts(T.S2[:, 16:32], T.S[:], 1.0, None, A.add, None, ["S"], [("S2", 16, 32)])
+    ts(T.WB[:], T.CI[:], col(9), -32.0, A.is_equal, A.mult, pc + ["CI"], ["WB"])
 
     def cands():
         op("dve", lambda: V.tensor_copy(T.CL[:], T.MX[:, 0:2056].indirect(T.S2[:, 0:32])), ["MX", "S2"], ["CL"])
 
-    def cands_f(k, nk=1):
-        a, b = 128 * k, 128 * (k + nk)
+    def cands_f(k):
+        a, b = 128 * k, 128 * k + 128
         ts(T.CF[:, a:b], T.CL[:, a:b], -2048.0, None, A.add, None, ["CL"], [rg("CF", a, b)])
 
     def tree_consts():
+        ms(T.CUM[:, 128:144], float(n * 128), [("CUM", 128, 144)])
         ts(col(10), PM, 1.0, None, A.subtract, None, pr, [("PC", 10, 11)])
         ts(col(11), PM, 2.0, None, A.subtract, None, pr, [("PC", 11, 12)])
         ts(col(12), PM, 4.0, None, A.subtract, None, pr, [("PC", 12, 13)])
         ts(col(13), PM, 128.0, None, A.add, None, pr, [("PC", 13, 14)])
         ts(T.KA[:], T.LOC[:], PM, None, A.is_equal, None, pr + ["LOC"], ["KA"])
         for l in range(3):
-            ts(T.VC[:, 16 * l:16 * l + 8], T.LOC[:, 16 * l:16 * l + 8], 16.0, None, A.mult, None,
-               ["LOC"], [("VC", 16 * l, 16 * l + 8)])
-            ts(T.VC[:, 16 * l + 8:16 * l + 16], T.LOC[:, 16 * l + 8:16 * l + 16], -16.0, 128.0 - 16.0 * (1 << l),
-               A.mult, A.add, ["LOC"], [("VC", 16 * l + 8, 16 * l + 16)])
             ts(T.KB[:, 16 * l:16 * l + 16], T.LOC[:, 16 * l:16 * l + 16], col(10 + l), None, A.is_equal, None,
                [("PC", 10, 13), "LOC"], [("KB", 16 * l, 16 * l + 16)])
-        tt(T.KA[:], T.KA[:], T.KB[:], A.subtract, ["KA", "KB"], ["KA"])
+        for l in range(3):
+            ts(T.VC[:, 16 * l:16 * l + 8], T.LOC[:, 16 * l:16 * l + 8], 16.0, None, A.mult, None,
+               ["LOC"], [("VC", 16 * l, 16 * l + 8)])
+            if l == 0:
+                tt(T.KA[:], T.KA[:], T.KB[:], A.subtract, ["KA", "KB"], ["KA"])
+            ts(T.VC[:, 16 * l + 8:16 * l + 16], T.LOC[:, 16 * l + 8:16 * l + 16], -16.0, 128.0 - 16.0 * (1 << l),
+               A.mult, A.add, ["LOC"], [("VC", 16 * l + 8, 16 * l + 16)])
 
-    for i in range(XPOOL, 16):
+    for i in range(XPOOL, 16 - XACT):
         cp(XR[0][:, i:4096:16], T.FR[:, 0:256], [("FR", 0, 256)], [xr_names(0)[i]])
     BIAS = 192.0 + 1.0 / 128
     win = T.MW[:, 0:4096]
@@ -331,9 +343,7 @@ def rank_program(g, core, T, topo):
             else:
                 ts(T.MW[:, lo:hi], T.MW[:, lo:hi], 184.0, 199.0, A.max, A.min, [rg("MW", lo, hi)], [rg("MW", lo, hi)])
         if t == 0:
-            lists()
-            columns()
-            masks()
+            act(T.XO[:, 0:256], T.FR[:, 0:256], F.Identity, [("FR", 0, 256)], [("XO", 0, 256)], bias=192.0)
             cands()
 
         slot = {}
@@ -394,10 +404,11 @@ def rank_program(g, core, T, topo):
             if k == 1:
                 ts(T.RI[:, j0:j1], T.SK[:, 32 * j0 + 31:32 * j1:32], 31, None, A.bitwise_and, None,
                    [rg("SK", 32 * j0, 32 * j1)], [rg("RI", j0, j1)])
+                if t == 0 and hf == 0:
+                    masks(0)
+                    masks(1)
             elif k == 2:
                 cp(T.RL[:, j0:j1], T.RI[:, j0:j1], [rg("RI", j0, j1)], [rg("RL", j0, j1)])
-                if t == 0 and hf == 0:
-                    cp(T.BH[:], T.BF[:], ["BF"], ["BH"])
             elif k in (3, 4):
                 h = k - 3
                 a, b = 256 * h + u0, 256 * h + u1
@@ -446,7 +457,7 @@ def rank_program(g, core, T, topo):
                 else:
                     ts(T.TT[:, j0, :], P[bx][:, 0:136], 16.0 - 6144.0, None, A.add, None, [px], [tn(j0)])
             elif k == 13:
-                act(T.VP[:, j0:j1, 112:128], P[bv][:, 0:128], F.Identity, ["P%d" % bv], ["VP%d" % hf])
+                act(T.VP[:, j0:j1, 112:128], P[bv][:, 0:128], F.Identity, ["P%d" % bv], [rg("VP", j0, j1)])
             elif k in (14, 15, 16):
                 for c in ((1, 2, 3), (4, 5), (6, 7))[k - 14]:
                     if (hf, k) in ONACT:
@@ -455,10 +466,11 @@ def rank_program(g, core, T, topo):
                         ts(T.TT[:, j0 + c, :], T.TT[:, j0, :], -32.0 * c, 0.0, A.add, A.max, [tn(j0)], [tn(j0 + c)])
             elif k in (17, 18):
                 cv = k - 17
+                c0, c1 = CUT[cv], CUT[cv + 1]
                 for s in range(8):
-                    mm(P[6 + cv][:, 0:68], T.VP[:, j0 + s, 112 - 16 * s:240 - 16 * s],
-                       T.TT[:, j0 + 4 * cv:j0 + 4 * cv + 4, 17 * s:17 * s + 17], hf == 0 and s == 0,
-                       hf == 1 and s == 7, ["VP%d" % hf, rg("TT", j0 + 4 * cv, j0 + 4 * cv + 4)], ["P%d" % (6 + cv)])
+                    mm(P[6 + cv][:, 0:17 * (c1 - c0)], T.VP[:, j0 + s, 112 - 16 * s:240 - 16 * s],
+                       T.TT[:, j0 + c0:j0 + c1, 17 * s:17 * s + 17], hf == 0 and s == 0,
+                       hf == 1 and s == 7, [rg("VP", j0, j1), rg("TT", j0 + c0, j0 + c1)], ["P%d" % (6 + cv)])
 
         def state(k):
             if k == 0:
@@ -469,20 +481,34 @@ def rank_program(g, core, T, topo):
                 lists()
 
         def pack(cv):
-            for c in range(4 * cv, 4 * cv + 4):
+            for c in range(CUT[cv], CUT[cv + 1]):
                 a = 128 * t + 16 * c
-                bank, c0 = 6 + cv, 17 * (c % 4)
+                bank, c0 = 6 + cv, 17 * (c - CUT[cv])
                 ts(T.GS[:, a:a + 16], P[bank][:, c0:c0 + 16], P[bank][:, c0 + 16:c0 + 17], 32768.0,
                    A.subtract, A.add, ["P%d" % bank], [rg("GS", a, a + 16)])
 
-        calls = {"c": cgath, "q": csq, "g": gath, "s": sq, "m": score, "z": scan, "a": lambda k: step(0, k),
+        def part(k):
+            if t < R - 1:
+                op("dve", lambda: V.tensor_copy(T.CL[:, 128 * k:128 * k + 128],
+                                                T.MX[:, 0:2056].indirect(T.S2[:, 8 * k:8 * k + 8])),
+                   ["MX", "S2"], [rg("CL", 128 * k, 128 * k + 128)])
+
+        def bounds(k):
+            if k == 0:
+                ts(P[4][:, 0:128], T.AB[:], -2.0, -127.0, A.add, A.max, ["AB"], [("P4", 0, 128)])
+            else:
+                ts(P[4][:, 128:256], T.AB[:], 2.0, 127.0, A.add, A.min, ["AB"], [("P4", 128, 256)])
+
+        calls = {"k": part, "l": bounds, "c": cgath, "q": csq, "g": gath, "s": sq, "m": score, "z": scan, "a": lambda k: step(0, k),
                  "b": lambda k: step(1, k), "h": state, "p": pack, "f": cands_f}
-        for tok in PLAN.replace("\n", "").split("|"):
+        for tok in (PLAN0 if t == 0 else PLAN).replace("\n", "").split("|"):
             f = tok.split()
             calls[f[0]](*[int(v) for v in f[1:]])
         gs = rg("GS", 128 * t, 128 * t + 128)
         send(T.GS[:, 128 * t:128 * t + 128],
              [T.GL[:, 384 * t + 128 * k:384 * t + 128 * k + 128] for k in range(n - 1)], "gar%d" % t, [gs])
+        if t == 0:
+            xrep(1, 16 - XLATE, 16)
         if t + 2 < R:
             xrep(t + 2, 0, 16)
         if t == 2:
@@ -492,35 +518,49 @@ def rank_program(g, core, T, topo):
         if t == 0:
             tree_consts()
             act(T.XO[:, 256:1024], T.FR[:, 256:1024], F.Identity, ["FR"], [("XO", 256, 1024)], bias=192.0)
-        if t == R - 1:
-            act(T.YS[:], T.IW[:, 0:2056].indirect(T.S2[:, 0:16]), F.Identity, ["IW", "S2"], ["YS"])
-            dma("sync", T.ys[:], T.YS[0:128:16, :], ["YS"], ())
         act(T.AM[:], T.AB[:], F.Identity, ["AB"], ["AM"], bias=-127.5 / 256)
         if t < R - 1:
             preload()
         act(T.NJ[:], T.NL[:, 16 * t + 2:16 * t + 10], F.Identity, [nown], ["NJ", "NS"], acc=T.NS[:, 0:1],
             ext=("nar%d" % t, neng * (n - 1) * (2 if t == 0 else 1)))
         act(T.RK[:], T.KA[:], F.Identity, ["KA", "NS"], ["RK"], scale=T.NS[:, 0:1])
-        mm(P[4][:, 0:48], T.BF[:], T.RK[:], True, True, ["BF", "RK"], ["P4"])
-        ts(T.OWN[:], T.GS[:, 128 * t:128 * t + 128], 1.0 / 256, None, A.mult, None, [gs], ["OWN"])
-        ts(P[2][:, 0:128], T.AB[:], -2.0, -127.0, A.add, A.max, ["AB"], [("P2", 0, 128)])
-        ts(P[2][:, 128:256], T.AB[:], 2.0, 127.0, A.add, A.min, ["AB"], [("P2", 128, 256)])
-        if t < R - 1:
-            cands()
-        ts(T.OK[:], P[4][:, 0:48], 519.0, None, A.is_ge, None, ["P4"], ["OK"])
+        mm(P[2][:, 0:48], T.BF[:], T.RK[:], True, True, ["BF", "RK"], ["P2"])
+        if t == R - 1:
+            act(T.YS[:], T.IW[:, 0:2056].indirect(T.S2[:, 0:16]), F.Identity, ["IW", "S2"], ["YS"])
+            dma("sync", T.ys[:], T.YS[0:128:16, :], ["YS"], ())
+        ts(T.OWN[:, 0:128], T.GS[:, 128 * t:128 * t + 128], 1.0 / 256, None, A.mult, None, [gs], [("OWN", 0, 128)])
+        fill = [k for k in range(4) if ("k %d" % k) not in (PLAN0 if t == 0 else PLAN)]
+
+        def more():
+            if fill:
+                part(fill.pop(0))
+
+        more()
+        ts(T.OK[:], P[2][:, 0:48], 519.0, None, A.is_ge, None, ["P2"], ["OK"])
+        more()
         tt(T.OK[:], T.OK[:], T.VC[:], A.mult, ["OK", "VC"], ["OK"])
+        more()
         tt(T.M1[:], T.OK[:, 0:16], T.OK[:, 16:32], A.max, ["OK"], ["M1"])
+        more()
         tt(T.M2[:], T.M1[:], T.OK[:, 32:48], A.max, ["OK", "M1"], ["M2"])
-        ts(T.LH[:, 0:8], T.M2[:, 0:8], PM, None, A.add, None, ["M2", "PC"], [("LH", 0, 8)])
-        ts(T.LH[:, 8:16], T.M2[:, 8:16], -1.0, col(13), A.mult, A.add, ["M2", "PC"], [("LH", 8, 16)])
+
+        def late(k):
+            if k == 0:
+                ts(T.LH[:, 8:16], T.M2[:, 8:16], -1.0, col(13), A.mult, A.add, ["M2", "PC"], [("LH", 8, 16)])
+            elif k == 1:
+                ts(T.LH[:, 0:8], T.M2[:, 0:8], PM, None, A.add, None, ["M2", "PC"], [("LH", 0, 8)])
+
         ts(P[0][:, 0:256], T.GL[:, 384 * t:384 * t + 256], 1.0 / 256, None, A.mult, None, [], [rg("P0", 0, 256)],
            ext=("gar%d" % t, neng * (n - 1)))
+        late(0)
         ts(T.C2[:], T.GL[:, 384 * t + 256:384 * t + 384], 1.0 / 256, None, A.mult, None, [], ["C2"])
-        tt(T.C1[:], P[0][:, 0:128], T.OWN[:], A.add, [rg("P0", 0, 128), "OWN"], ["C1"])
+        late(1)
+        tt(T.C1[:], P[0][:, 0:128], T.OWN[:, 0:128], A.add, [rg("P0", 0, 128), "OWN"], ["C1"])
         hv2 = [(0, 64), (64, 128)]
         for (a, b) in hv2:
             tt(P[0][:, 256 + a:256 + b], P[0][:, 128 + a:128 + b], T.C2[:, a:b], A.add,
                [rg("P0", 128 + a, 128 + b), "C2"], [rg("P0", 256 + a, 256 + b)])
+        late(2)
         for (a, b) in hv2:
             tt(T.CUM[:, a:b], P[0][:, 256 + a:256 + b], T.C1[:, a:b], A.add, [rg("P0", 256 + a, 256 + b), "C1"],
                [rg("CUM", a, b)])
@@ -532,9 +572,9 @@ def rank_program(g, core, T, topo):
             tt(T.TI[:, a:b], cw.indirect(T.LH[:, 4 * hv:4 * hv + 4]), T.H[:, a:b], A.subtract,
                ["CUM", "LH", rg("H", a, b)], [rg("TI", a, b)])
         for (a, b) in hv2:
-            tt(T.T2[:, a:b], T.TI[:, a:b], P[2][:, a:b], A.max, [rg("TI", a, b), "P2"], [rg("T2", a, b)])
+            tt(T.T2[:, a:b], T.TI[:, a:b], P[4][:, a:b], A.max, [rg("TI", a, b), "P4"], [rg("T2", a, b)])
         for (a, b) in hv2:
-            tt(T.AB[:, a:b], T.T2[:, a:b], P[2][:, 128 + a:128 + b], A.min, [rg("T2", a, b), "P2"], [rg("AB", a, b)])
+            tt(T.AB[:, a:b], T.T2[:, a:b], P[4][:, 128 + a:128 + b], A.min, [rg("T2", a, b), "P4"], [rg("AB", a, b)])
         for hv in range(2):
             spread(hv, T.AB, "AB")
 

@@ -3,64 +3,158 @@ from concourse.mybir import AluOpType, ActivationFunctionType
 
 R = 4
 _B = {
-    "bfloat16": dict(MU=4096, FR=1024, XO=1024, XR0=4096, XR1=4096, XR2=4096, XR3=4096, AN=128, AB=128, L=1024,
-                     MW=4096, MG=2048, D=8192, CS=256, SG=256, VG=256, EG=256, ZR=480, I16=16, J=64, WB=144,
-                     ONE=136, NEG=136, ID=128, NID=128, E1=136, E2=136, Q64=64, BL=128, BR=512),
-    "float32": dict(AM=128, CF=512, SW=256, NL=64, NJ=8, NS=4, RK=48, OK=48, M1=16, M2=16, OWN=144, C1=128,
-                    C2=128, CUM=144, H=128, T2=128, YW=1024, YS=256, YA=128, PC=16, CI=144, C16=128, LOC=48, KA=48,
-                    KB=48, VC=48, SC1=128, SC2=128, SC3=128, ONF=128, BT=128, BF=128, IW=2056),
-    "int32": dict(MX=2056, S=16, SK=512, RI=16, HS=16, TI=128, IP=4, SLI=8),
-    "uint16": dict(S2=32, CL=512, RL=16, WL=16, GS=512, GL=1536, LH=16, SL=8, SLB=4),
+    "bfloat16": dict(MU=4096, FR=1024, FP=1024, FX=1024, XZ=1024, XR=16384, AN=128, AB=128, L=1024, LN=1024, MW=4096, D=8224,
+                     JB=256, JJ=4256, CS=256, SG=256, VG=256, EG=256, ZR=480, I16=16, WB=144,
+                     ONE=136, NEG=136, ID=128, NID=128, E1=136, E2=136, E3=136, Q64=64, BL=128, BR=512),
+    "float32": dict(AM=128, SW=256, NL=64, NJ=16, RK=64, OK=64, SM=64, OWN=128, C1=128, CF=512, MXF=2056,
+                    C2=128, CUM=144, H=128, T2=128, YW=1024, YS=256, YA=128, PC=16, CI=144, C16=128, LOC=64, HIC=64,
+                    KA=64, KB=64, VC=64, SCS=64, SC1=256, SC2=128, SC3=128, BT=128, BF=128, IW=2056, K16=16),
+    "int32": dict(MX=2056, S=16, SK=512, RO=16, HS=16, TI=128, IP=4, SLI=8),
+    "uint16": dict(S2=32, CL=512, RL=16, OF=16, WL=16, GS=512, GL=1536, LH=16, SL=8, SLB=4, PL=16),
     "float16": dict(CM=512, BH=128),
 }
 SCRATCH = {}
 for _d in _B:
     for _n in _B[_d]:
         SCRATCH[_n] = ("sbuf", [128, _B[_d][_n]], _d)
-SCRATCH["D2"] = ("sbuf", [128, 32, 256], "bfloat16")
+SCRATCH["D2"] = ("sbuf", [128, 512, 16], "bfloat16")
 SCRATCH["TT"] = ("sbuf", [128, 16, 136], "bfloat16")
 SCRATCH["VP"] = ("sbuf", [128, 16, 240], "bfloat16")
 for _k in range(8):
     SCRATCH["P%d" % _k] = ("psum", [128, 512], "float32")
 
-NDMA = 24
+NDMA = 48
 SEMAPHORES = (["pe", "dve", "act", "pool", "sent"] + ["d%d" % k for k in range(NDMA)]
               + ["nar%d" % t for t in range(R)] + ["gar%d" % t for t in range(R)])
 
 A = AluOpType
 F = ActivationFunctionType
 
-PLAN = """g 1 4 6|g 1 2 4|g 0 2 4|g 0 6 8|g 1 6 8|c 0 0 2|c 1 0 2|c 0 8 9|s 1 2 4|q 0|q 1|g 0 4 6|g 0 9 12|g 1 9 12|
-g 1 14 15|s 0 2 4|m 2 0 4|z 2 0 4|c 1 8 9|s 1 6 8|s 0 4 6|g 1 12 14|g 0 12 14|s 0 6 8|g 0 14 16|s 1 4 6|m 3 4 8|q 8|
-g 1 15 16 0 8|s 0 9 12|s 1 9 12|m 2 8 12|z 2 8 12|z 3 4 8|s 1 12 14|s 1 14 15|g 1 15 16 8 16|a 1|f 0|s 0 12 14|
-s 0 14 16|m 2 12 14|f 2|a 2|s 1 15 16 0 8|m 3 14 16 0 8|s 1 15 16 8 16|m 3 14 16 8 16|f 1|a 3|a 4|z 2 12 14|
-z 3 14 16|a 7|f 3|b 1|a 5|a 6|b 2|a 9|b 3|b 4|a 10|a 11|b 7|a 13|b 5|b 6|h 0|b 9|a 12|b 11|a 14|b 10|a 15|a 17|b 12|
-a 16|b 14|b 15|b 13|h 1|a 8|b 8|b 16|a 18|b 17|h 2|l 0|p 0|b 18|p 1|l 1"""
-PLAN0 = PLAN
-MORDER = "A0:2 D2:4 A4:6 D6:8 A8:10 C0:2 D10:12 C4:6 A12:14 C8:10 A14:16 C12:14 C14:16"
+MORDER = "A0:2 D2:4 A4:6 D6:8 A8:10 C0:2 D10:12 C4:6 A12:14 C8:10 A14:15 C12:14 A15:16 C14:15 C15:16"
 VCLS = (1, 3, 5)
-CBANK = (0, 1, 6, 7)
+PLAN = """c 0 0 4|c 1 0 4|c 0 4 8|c 1 4 8|g 0 8 11|g 1 8 11|g 0 11 14|v 0 8 11|v 1 8 11|m 8 11|q 0 0 4|q 1 0 4|m 0 4|
+g 1 11 14|g 0 14 16|v 0 11 14|v 1 11 14|m 11 14|q 0 4 8|q 1 4 8|m 4 8|g 1 14 16|v 0 14 16|s 1 14 16|m 14 16|
+c 0 16 19|c 1 16 19|c 0 19 22|g 0 22 26|w 0|g 1 22 26|q 0 16 19|c 1 19 22|g 0 26 29|v 0 22 26|q 1 16 19|m 16 19|
+s 1 22 26|m 22 26|g 1 26 29|q 0 19 22|v 0 26 29|q 1 19 22|m 19 22|g 0 29 32|u 0|s 1 26 29|m 26 29|g 1 29 31|
+s 0 29 32|g 1 31 32|v 1 29 31|m 29 31|s 1 31 32|m 31 32|w 1|u 1"""
+RAW = (8, 6)
+PLAN0 = PLAN
+for _g, _c in (("Z", "g 1 22 26"), ("L", "g 0 26 29"), ("C", "g 1 26 29"), ("B", "m 22 26"), ("S", "q 0 19 22")):
+    PLAN0 = PLAN0.replace(_c, _g + "|" + _c)
+X0 = 6
+CBANK = (0, 1, 4, 5, 0, 1, 7, 0)
+HBANK = ((2, 4, 5, 6), (3, 1, 2, 0))
 CUT = (0, 4, 8)
-ONACT = ((1, 16),)
-XPOOL = 7
-XACT = 5
-VACT = 5
-XLATE = 6
+RELU_ACT = ((6, 7), (7,))
+ON_VECTOR = ("", "VT")
+XENG = ("act", "pool", "pool")
+CYC, GAT, SCA, PEC, PE0, SEM, ACT0, DMA0, BPU = 0.0009, 1.4, 3.5, 0.00055, 0.0, 0.13, 0.015, 1.2, 550e3
+CALL1, CALL, FLY = 4.0, 0.5, 1.7
+PASSES = 2
 
 
 def _norm(rs):
-    out = []
-    for r in rs:
-        out.append((r, 0, 1 << 30) if isinstance(r, str) else r)
-    return out
+    return [(r, 0, 1 << 30) if isinstance(r, str) else r for r in rs]
 
 
-def make_sched(g, T):
+def link(calls):
+    hist, bank_last, seq_last = {}, {}, {}
+    for i, c in enumerate(calls):
+        pre = {}
+        for (regs, writing) in ((c["r"], False), (c["w"], True)):
+            for (name, lo, hi) in regs:
+                for (plo, phi, pw, k) in hist.get(name, ()):
+                    if plo < hi and lo < phi and (pw or writing):
+                        pre[k] = True
+                if name[0] == "P" and name[1:].isdigit() and name in bank_last:
+                    k = bank_last[name]
+                    pre[k] = pre.get(k, False) or calls[k]["q"] != c["q"]
+        if c["seq"] is not None:
+            if c["seq"] in seq_last:
+                pre.setdefault(seq_last[c["seq"]], False)
+            seq_last[c["seq"]] = i
+        for k in c["after"]:
+            pre.setdefault(k, False)
+        pre.pop(i, None)
+        c["pre"] = [(k, s and not (c["q"] == "pe" and calls[k]["q"] == "pe")) for k, s in pre.items()]
+        for (regs, writing) in ((c["r"], False), (c["w"], True)):
+            for (name, lo, hi) in regs:
+                lst = hist.setdefault(name, [])
+                if writing:
+                    lst[:] = [e for e in lst if not (lo <= e[0] and e[1] <= hi)]
+                lst.append((lo, hi, writing, i))
+                if name[0] == "P" and name[1:].isdigit():
+                    bank_last[name] = i
+
+
+def order(calls):
+    n = len(calls)
+    wire = 0.0
+    for c in calls:
+        if c["bytes"]:
+            wire = (wire if c["seq"] else 0.0) + c["bytes"] / BPU
+            c["late"] = DMA0 + wire
+    succ = [[] for _ in range(n)]
+    pred = [[] for _ in range(n)]
+    for i, c in enumerate(calls):
+        for (k, s) in c["pre"]:
+            d = (SEM + calls[k]["late"]) if s else 0.0
+            if c["ext"] is not None and calls[k]["send"]:
+                d = FLY
+            succ[k].append((i, d))
+            pred[i].append((k, d))
+
+    def place(before, after, rank, first):
+        left = [len(b) for b in before]
+        ready = sorted((rank[i], i) for i in range(n) if left[i] == 0)
+        busy = {}
+        end = [0.0] * n
+        while ready:
+            i = ready.pop(0)[1]
+            at = max([first[i]] + [end[k] + d for (k, d) in before[i]])
+            lst = busy.setdefault(calls[i]["q"], [])
+            k = len(lst)
+            while k > 0 and lst[k - 1][1] > at:
+                k -= 1
+            while k < len(lst) and lst[k][0] < at + calls[i]["us"] - 1e-9:
+                at = max(at, lst[k][1])
+                k += 1
+            end[i] = at + calls[i]["us"]
+            lst.insert(k, (at, end[i]))
+            for (j, d) in after[i]:
+                left[j] -= 1
+                if left[j] == 0:
+                    ready.append((rank[j], j))
+            ready.sort()
+        return end
+
+    late = [c["late"] for c in calls]
+    way = [0.0] * n
+    left = [len(s) for s in succ]
+    chain = [i for i in range(n) if left[i] == 0]
+    for i in chain:
+        way[i] = calls[i]["us"] + max([d + way[j] for (j, d) in succ[i]] + [late[i]])
+        for (k, d) in pred[i]:
+            left[k] -= 1
+            if left[k] == 0:
+                chain.append(k)
+    end = place(pred, succ, [-way[i] - calls[i]["lead"] for i in range(n)], [0.0] * n)
+    best = (max(end[i] + late[i] for i in range(n)), end)
+    for _ in range(PASSES):
+        back = place(succ, pred, [-end[i] - late[i] for i in range(n)], late)
+        end = place(pred, succ, [-back[i] for i in range(n)], [0.0] * n)
+        span = max(end[i] + late[i] for i in range(n))
+        if span < best[0]:
+            best = (span, end)
+    end = best[1]
+    return sorted(range(n), key=lambda i: (end[i] - calls[i]["us"], end[i]))
+
+
+def issue(g, T, calls):
     queues = {"pe": g.tensor, "dve": g.vector, "act": g.scalar, "pool": g, "sync": g.sync}
     known = {q: {} for q in queues}
     count = {}
-    hist = {}
-    ndma = [0]
+    ndma = 0
 
     def wait_for(q, src, n, clock):
         if known[q].get(src, 0) >= n:
@@ -71,56 +165,36 @@ def make_sched(g, T):
             if known[q].get(k, 0) < v:
                 known[q][k] = v
 
-    def op(q, fn, r=(), w=(), dma=False, ext=None, track=True):
-        r = _norm(r)
-        w = _norm(w)
+    link(calls)
+    for i in order(calls):
+        c = calls[i]
+        q = c["q"]
+        tag = c["tag"]
         need = {}
-        for (regs, writing) in ((r, False), (w, True)):
-            for (name, lo, hi) in regs:
-                bank = name[0] == "P" and name[1:].isdigit()
-                for (plo, phi, pw, src, n, clock) in hist.get(name, ()):
-                    if src == "pe" and q == "pe":
-                        continue
-                    over = plo < hi and lo < phi
-                    if (over and (pw or writing)) or (bank and src != q):
-                        if need.get(src, (0, None))[0] < n:
-                            need[src] = (n, clock)
+        for (k, s) in c["pre"]:
+            if s:
+                src, n, clock = calls[k]["done"]
+                if need.get(src, (0, None))[0] < n:
+                    need[src] = (n, clock)
         for src in sorted(need):
-            implied = False
-            for other in need:
-                if other != src and need[other][1].get(src, 0) >= need[src][0]:
-                    implied = True
-            if not implied:
+            if not any(o != src and need[o][1].get(src, 0) >= need[src][0] for o in need):
                 wait_for(q, src, need[src][0], need[src][1])
-        if ext is not None:
-            wait_for(q, ext[0], ext[1], {})
-        ins = fn()
-        if not track:
-            return
-        if dma:
-            src = "d%d" % ndma[0]
-            ndma[0] += 1
-            step = 16
-        else:
-            src = q
-            step = 1
+        if c["ext"] is not None:
+            wait_for(q, c["ext"][0], c["ext"][1], {})
+        ins = c["fn"]()
+        if c["send"]:
+            continue
+        src, step = q, 1
+        if c["bytes"]:
+            src, step = "d%d" % ndma, 16
+            ndma += 1
         ins.then_inc(T.sem[src], step)
         count[src] = count.get(src, 0) + step
         clock = dict(known[q])
         clock[src] = count[src]
-        for (regs, writing) in ((r, False), (w, True)):
-            for (name, lo, hi) in regs:
-                lst = hist.setdefault(name, [])
-                bank = name[0] == "P" and name[1:].isdigit()
-                lst[:] = [e for e in lst if not (lo <= e[0] and e[1] <= hi and (
-                    (writing and not bank) or (e[3] == src and (writing or not e[2]))))]
-                lst.append((lo, hi, writing, src, count[src], clock))
-
-    def finish(q):
-        for src in count:
-            wait_for(q, src, count[src], {})
-
-    return op, finish
+        c["done"] = (src, count[src], clock)
+    for src in count:
+        wait_for("sync", src, count[src], {})
 
 
 def rank_program(g, core, T, topo):
@@ -129,44 +203,59 @@ def rank_program(g, core, T, topo):
         return
     cores = list(T.cores)
     n = len(cores)
-    op, finish = make_sched(g, T)
     V, S_, PE = g.vector, g.scalar, g.tensor
-    P = [T["P%d" % k] for k in range(8)]
-    XR = [T["XR%d" % t] for t in range(R)]
+    calls = []
+    now = {"tag": "init", "seq": None, "lead": 0.0}
 
-    def ts(out, in0, s1, s2, o0, o1, r, w, ext=None):
+    def op(q, fn, us, r=(), w=(), ext=None, after=(), nbytes=0, send=False, late=0.0):
+        seq = now["seq"] and q != "pe" and (now["seq"], q) or None
+        calls.append(dict(q=q, fn=fn, us=us, r=_norm(r), w=_norm(w), ext=ext, after=list(after) + now.pop("gate", []),
+                          bytes=nbytes, send=send, late=late, seq=seq, tag=now["tag"], lead=now["lead"]))
+        return len(calls) - 1
+
+    def vec(cyc):
+        return max(64, cyc) * CYC
+
+    def gat(k):
+        return 0.05 + k * GAT * CYC
+
+    def ts(out, in0, s1, s2, o0, o1, r, w, us=vec(0), ext=None, after=()):
         if o1 is None:
-            op("dve", lambda: V.tensor_scalar(out, in0, s1, None, o0), r, w, ext=ext)
-        else:
-            op("dve", lambda: V.tensor_scalar(out, in0, s1, s2, o0, o1), r, w, ext=ext)
+            return op("dve", lambda: V.tensor_scalar(out, in0, s1, None, o0), us, r, w, ext, after)
+        return op("dve", lambda: V.tensor_scalar(out, in0, s1, s2, o0, o1), us, r, w, ext, after)
 
-    def tt(out, in0, in1, o, r, w):
-        op("dve", lambda: V.tensor_tensor(out, in0, in1, o), r, w)
+    def tt(out, in0, in1, o, r, w, us=vec(0)):
+        return op("dve", lambda: V.tensor_tensor(out, in0, in1, o), us, r, w)
 
-    def cp(out, in_, r, w):
-        op("dve", lambda: V.tensor_copy(out, in_), r, w)
+    def cp(out, in_, r, w, us=vec(0)):
+        return op("dve", lambda: V.tensor_copy(out, in_), us, r, w)
 
-    def ms(ap, c, w):
-        op("dve", lambda: V.memset(ap, c), (), w)
+    def ms(ap, c, w, us=vec(0)):
+        return op("dve", lambda: V.memset(ap, c), us, (), w)
 
-    def act(out, in_, f, r, w, bias=0.0, scale=1.0, acc=None, ext=None):
-        op("act", lambda: S_.activation(out, in_, f, bias=bias, scale=scale, accum_out=acc), r, w, ext=ext)
+    def scan(out, d0, d1, r, w, k):
+        return op("dve", lambda: V.tensor_tensor_scan(out, d0, d1, 0.0, A.add, A.max), vec(k), r, w)
 
-    def mm(out, lhsT, rhs, st, sp, r, w):
-        op("pe", lambda: PE.matmul(out, lhsT, rhs, st, sp), r, w)
+    def act(out, in_, f, r, w, k, bias=0.0, scale=1.0, acc=None, ext=None, after=(), gather=False):
+        us = gat(k) if gather else ACT0 + k * CYC
+        return op("act", lambda: S_.activation(out, in_, f, bias=bias, scale=scale, accum_out=acc), us, r, w, ext, after)
 
-    def dma(q, out, in_, r, w):
+    def mm(out, lhsT, rhs, st, sp, r, w, k, after=()):
+        return op("pe", lambda: PE.matmul(out, lhsT, rhs, st, sp), PE0 + max(64, k) * PEC, r, w, late=0.05, after=after)
+
+    def dma(q, out, in_, r, w, nbytes):
         eng = g.sync if q == "sync" else g.scalar
-        op(q, lambda: eng.dma_start(out, in_), r, w, dma=True)
+        return op(q, lambda: eng.dma_start(out, in_), 0.06, r, w, nbytes=nbytes)
 
-    def iota(out, pat, base, cm, w, flt=True):
+    def iota(out, pat, base, cm, w, k, flt=True, after=()):
+        us = 0.13 + 2 * k * CYC
         if flt:
-            op("pool", lambda: g.iota(out, pat, base, cm, allow_small_or_imprecise_dtypes=True), (), w)
+            op("pool", lambda: g.iota(out, pat, base, cm, allow_small_or_imprecise_dtypes=True), us, (), w, after=after)
         else:
-            op("pool", lambda: g.iota(out, pat, base, cm), (), w)
+            op("pool", lambda: g.iota(out, pat, base, cm), us, (), w, after=after)
 
-    def sel(out, in_, pat, cmp, fill, base, cm, r, w):
-        op("pool", lambda: g.affine_select(out, in_, pat, cmp, fill, base, cm), r, w)
+    def sel(out, in_, pat, cmp, fill, base, cm, r, w, k, after=()):
+        op("pool", lambda: g.affine_select(out, in_, pat, cmp, fill, base, cm), 0.17 + 2 * k * CYC, r, w, after=after)
 
     peers = [cores[(rank + k) % n] for k in range(1, n)]
     mask = topo.mask(core, peers[0])
@@ -180,408 +269,415 @@ def rank_program(g, core, T, topo):
         def fn():
             tr = RemoteDMATransfer(dst_ids=ids, dma_engine_mask=mask, remote_sem=T.sem[sem], src=src, dsts=dsts)
             return g.remote_dma_fused([tr], local_sem=T.sem.sent)
-        op("pool", fn, r, (), track=False)
         sends[0] += neng
+        return op("pool", fn, CALL if sends[0] > neng else CALL1, r, (), send=True)
+
+    def col(k):
+        return T.PC[:, k:k + 1]
+
+    def pc(*ks):
+        return [("PC", k, k + 1) for k in ks]
 
     def rg(name, a, b):
         return (name, a, b)
 
-    dma("sync", T.AN[:], T.a0[:], (), ["AN"])
-    dma("act", T.FR[:, 0:256], T.fr[:, 0:256], (), [("FR", 0, 256)])
-    dma("act", T.S[:], T.s0[:], (), ["S"])
-    dma("act", T.MX[:, 2048:2056], T.mix[:, 0:8], (), [("MX", 2048, 2056)])
-    for k in range(4):
-        dma("sync", T.MU[:, 1024 * k:1024 * (k + 1)], T.mu[:, 1024 * k:1024 * (k + 1)], (),
-            [("MU", 1024 * k, 1024 * (k + 1))])
-    dma("sync", T.MX[:, 0:2048], T.mix[:], (), [("MX", 0, 2048)])
-    dma("sync", T.FR[:, 256:1024], T.fr[:, 256:1024], (), [("FR", 256, 1024)])
+    P = [T["P%d" % k] for k in range(8)]
+    pn = lambda k, a=0, b=512: ("P%d" % k, a, b)
 
-    iota(T.IP[:, 0:1], [[0, 1]], 0, 1, [("IP", 0, 1)], flt=False)
-    iota(T.SLI[:], [[128, 8]], 0, 1, ["SLI"], flt=False)
-    iota(T.CI[:], [[1, 144]], 0, 0, ["CI"])
+    ms(T.ZR[:], 0.0, ["ZR"], vec(240))
+    now["seq"] = "load"
+    dma("sync", T.AN[:], T.a0[:], (), ["AN"], 32768)
+    dma("act", T.FR[:, 0:256], T.fr[:, 0:256], (), [("FR", 0, 256)], 65536)
+    dma("act", T.S[:], T.s0[:], (), ["S"], 8192)
+    dma("act", T.MX[:, 2048:2056], T.mix[:, 0:8], (), [("MX", 2048, 2056)], 4096)
+    for (a, b) in ((0, 1536), (1536, 3072), (3072, 4096)):
+        dma("sync", T.MU[:, a:b], T.mu[:, a:b], (), [("MU", a, b)], 256 * (b - a))
+    dma("sync", T.MX[:, 0:2048], T.mix[:], (), [("MX", 0, 2048)], 1048576)
+    dma("sync", T.FR[:, 256:1024], T.fr[:, 256:1024], (), [("FR", 256, 1024)], 196608)
+    for a in range(0, 4256, 480):
+        b = min(a + 480, 4256)
+        dma("sync", T.JJ[:, a:b], T.ZR[:, 0:b - a], ["ZR"], [rg("JJ", a, b)], 256 * (b - a))
+    for k in range(8):
+        dma("sync", T.VP[:, 2 * k:2 * k + 2, :], T.ZR[:], ["ZR"], [rg("VP", 2 * k, 2 * k + 2)], 122880)
+    now["seq"] = None
 
-    ms(T.ZR[:], 0.0, ["ZR"])
-    ms(T.ONE[:], 1.0, ["ONE"])
-    ms(T.NEG[:], -1.0, ["NEG"])
-    ms(T.L[:], 0.0, ["L"])
-
-    def xr_names(t):
-        return ["XR%d#%d" % (t, i) for i in range(16)]
-
-    for k in range(VACT):
-        act(T.VP[:, 2 * k:2 * k + 2, :], T.ZR[:], F.Identity, ["ZR"], [rg("VP", 2 * k, 2 * k + 2)])
-    for i in range(16 - XACT, 16):
-        act(XR[0][:, i:4096:16], T.FR[:, 0:256], F.Identity, [("FR", 0, 256)], [xr_names(0)[i]])
-    ts(T.IP[:, 1:2], T.IP[:, 0:1], 15, None, A.bitwise_and, None, [("IP", 0, 1)], [("IP", 1, 2)])
+    now["seq"] = "main"
+    iota(T.IP[:, 0:1], [[0, 1]], 0, 1, [("IP", 0, 1)], 1, flt=False)
+    iota(T.SLI[:], [[128, 8]], 0, 1, ["SLI"], 8, flt=False)
+    iota(T.K16[:], [[128, 2], [2, 8]], 0, 0, ["K16"], 16)
+    ip = [("IP", 0, 1)]
+    ms(T.LN[:], 0.0, ["LN"], vec(512))
+    ts(T.IP[:, 1:2], T.IP[:, 0:1], 15, None, A.bitwise_and, None, ip, [("IP", 1, 2)])
+    ts(T.IP[:, 2:3], T.IP[:, 0:1], 7, None, A.bitwise_and, None, ip, [("IP", 2, 3)])
+    ts(T.IP[:, 3:4], T.IP[:, 0:1], 3, 1, A.logical_shift_right, A.bitwise_and, ip, [("IP", 3, 4)])
     cp(T.SL[:], T.SLI[:], ["SLI"], ["SL"])
     ts(T.SLB[:], T.SLI[:, 4:8], -512.0, None, A.add, None, ["SLI"], ["SLB"])
-    cp(T.PC[:, 0:2], T.IP[:, 0:2], [("IP", 0, 2)], [("PC", 0, 2)])
     ms(T.Q64[:], 1.0 / 64, ["Q64"])
+    cp(T.PC[:, 0:4], T.IP[:, 0:4], ["IP"], [("PC", 0, 4)])
     ms(T.BL[0:2, :], 1.0 / 128, ["BL"])
-    PF, PM = T.PC[:, 0:1], T.PC[:, 1:2]
-    col = lambda k: T.PC[:, k:k + 1]
-    pr = [("PC", 0, 2)]
-    pc = [("PC", 0, 10)]
-    ts(T.I16[:], T.CI[:, 0:16], PM, 64.0, A.is_equal, A.mult, pr + ["CI"], ["I16"])
-    ms(T.BR[0:2, :], 1.0, ["BR"])
+    ms(T.BR[0:2, :], 1.0, ["BR"], vec(256))
+    PF, PM = col(0), col(1)
+    ts(col(10), col(2), 16.0, col(3), A.mult, A.add, pc(2, 3), pc(10))
     ms(T.BL[0:1, :], 192.0, ["BL"])
-    ts(col(3), PM, -1.0, 15.0, A.mult, A.add, pr, [("PC", 3, 4)])
-    ts(col(7), PM, 15.0, 8192.0, A.is_equal, A.mult, pr, [("PC", 7, 8)])
-    ts(col(2), PM, -1.0, 31.0, A.mult, A.add, pr, [("PC", 2, 3)])
-    tt(col(9), PF, col(3), A.add, pr + [("PC", 3, 4)], [("PC", 9, 10)])
-    ms(T.ONF[:], 1.0, ["ONF"])
+    ms(T.ONE[:], 1.0, ["ONE"])
+    ms(T.NEG[:], -1.0, ["NEG"])
+    ts(T.PL[:], T.K16[:], col(10), None, A.add, None, pc(10) + ["K16"], ["PL"])
+    now["seq"] = None
+    iota(T.CI[:], [[1, 144]], 0, 0, ["CI"], 144)
+    ts(T.I16[:], T.CI[:, 0:16], PM, 64.0, A.is_equal, A.mult, pc(1) + ["CI"], ["I16"])
 
-    def masks(k):
-        if k == 0:
-            ts(col(4), PM, 1.0, None, A.add, None, pr, [("PC", 4, 5)])
-            ts(col(5), PM, -512.0, 2048.5, A.mult, A.add, pr, [("PC", 5, 6)])
-            ts(col(8), col(7), -6144.0, None, A.add, None, [("PC", 7, 8)], [("PC", 8, 9)])
-            ts(T.SC2[:], T.C16[:], PM, -1.0e9, A.is_equal, A.mult, pc + ["C16"], ["SC2"])
-            ts(T.SC3[:], T.C16[:], col(4), 8192.0, A.is_equal, A.mult, pc + ["C16"], ["SC3"])
-        else:
-            ts(T.J[:, 0:32], T.CI[:, 0:32], col(2), None, A.is_equal, None, pc + ["CI"], [("J", 0, 32)])
-            ts(T.J[:, 32:64], T.CI[:, 0:32], col(3), None, A.is_equal, None, pc + ["CI"], [("J", 32, 64)])
-            cp(T.BH[:], T.BF[:], ["BF"], ["BH"])
-            tt(T.SC2[:], T.SC2[:], T.SC3[:], A.add, ["SC2", "SC3"], ["SC2"])
+    def lin(k, src, scale, bias, r=()):
+        act(col(k), col(src), F.Identity, pc(src, *r), pc(k), 1, bias=bias, scale=scale)
 
-    def xrep(t, i0, i1):
-        for i in range(i0, i1):
-            sel(XR[t][:, i:4096:16], T.FR[:, 256 * t:256 * t + 256], [[0, 256]], A.is_equal, 0.0, 0, 0,
-                [("FR", 256 * t, 256 * t + 256)], [xr_names(t)[i]])
+    lin(11, 1, -1.0, 15.0)
+    lin(5, 1, -512.0, 2048.5)
+    lin(6, 1, 128.0, 2191.0)
+    lin(9, 0, 1.0, col(11), (11,))
+    ts(col(7), PM, 15.0, 8192.0, A.is_equal, A.mult, pc(1), pc(7))
+    lin(8, 7, 1.0, -6144.0)
+    ts(T.WB[:], T.CI[:], col(9), -4096.0, A.is_equal, A.mult, pc(9) + ["CI"], ["WB"], vec(144))
+    for hf in range(2):
+        a = 4112 * hf + 2048
+        iota(T.D[:, a:a + 16], [[0, 16]], 0, 0, [rg("D", a, a + 16)], 16)
+    sel(T.ID[:], T.ONE[:, 0:128], [[-1, 128]], A.is_equal, 0.0, 0, 1, ["ONE"], ["ID"], 128)
+    sel(T.NID[:], T.NEG[:, 0:128], [[-1, 128]], A.is_equal, 0.0, 0, 1, ["NEG"], ["NID"], 128)
+    iota(T.C16[:], [[0, 8], [1, 16]], 0, 0, ["C16"], 128)
+    ts(T.JJ[:, 2064:2192], T.C16[:], PM, None, A.is_equal, None, pc(1) + ["C16"], [rg("JJ", 1920, 2400)], vec(128))
+    act(T.SC2[:], T.JJ[:, 2064:2192], F.Identity, [rg("JJ", 1920, 2400)], ["SC2"], 128, scale=-1.0e9)
+    act(T.SC3[:], T.JJ[:, 2063:2191], F.Identity, [rg("JJ", 1920, 2400)], ["SC3"], 128, scale=8192.0)
+    tt(T.SC2[:], T.SC2[:], T.SC3[:], A.add, ["SC2", "SC3"], ["SC2"], vec(256))
+    iota(T.SC1[:], [[0, 256]], 1, 0, ["SC1"], 256)
+    iota(T.SC1[:, 0:256:32], [[0, 8]], -16000000, 0, ["SC1"], 8)
+    iota(T.SC1[:, 16:256:32], [[0, 8]], 2049, 0, ["SC1"], 8)
+    iota(T.JB[0:1, :], [[-16, 8], [0, 32]], 112, 0, ["JB"], 256)
+    sel(T.BT[:], T.ONE[:, 0:128], [[-16, 8], [0, 16]], A.is_ge, 0.0, 0, 1, ["ONE"], ["BT"], 128)
+    sel(T.BF[:], T.BT[:], [[16, 8], [0, 16]], A.is_ge, 0.0, 15, -1, ["BT"], ["BF"], 128)
+    cp(T.BH[:], T.BF[:], ["BF"], ["BH"], vec(128))
+    for (buf, src) in (("E1", "NEG"), ("E3", "ONE")):
+        sel(T[buf][:], T[src][:], [[-16, 8], [-1, 17]], A.is_equal, 0.0, 0, 1, [src], [buf], 136)
+        iota(T[buf][:, 16:136:17], [[0, 8]], 0, 0, [buf], 8)
+    sel(T.E2[:], T.ONE[:], [[-16, 8], [0, 17]], A.is_equal, 0.0, 0, 1, ["ONE"], ["E2"], 136)
+    for (buf, up) in (("LOC", 0), ("HIC", 1)):
+        iota(T[buf][:, 0:64:4], [[0, 16]], 8 * up, 0, [(buf, 0, 1)], 16)
+        iota(T[buf][:, 1:64:4], [[0, 2], [4, 2], [0, 4]], 4 * up, 0, [(buf, 1, 2)], 16)
+        iota(T[buf][:, 2:64:4], [[0, 2], [2, 4], [0, 2]], 2 * up, 0, [(buf, 2, 3)], 16)
+        iota(T[buf][:, 3:64:4], [[0, 2], [1, 8]], up, 0, [(buf, 3, 4)], 16)
+    ts(T.KA[:], T.LOC[:], PM, 256.0, A.is_equal, A.mult, pc(1) + ["LOC"], ["KA"])
+    ts(T.KB[:], T.HIC[:], PM, 256.0, A.is_equal, A.mult, pc(1) + ["HIC"], ["KB"])
+    tt(T.KA[:], T.KA[:], T.KB[:], A.subtract, ["KA", "KB"], ["KA"], vec(128))
+    lin(4, 1, -1.0, 0.0)
+    act(T.VC[:, 0:32], T.LOC[:, 0:32], F.Identity, pc(1) + ["LOC"], [("VC", 0, 32)], 32, scale=16.0, bias=PM)
+    act(T.VC[:, 32:64], T.HIC[:, 32:64], F.Identity, pc(4) + ["HIC"], [("VC", 32, 64)], 32, scale=-16.0, bias=col(4))
+    iota(T.SCS[:], [[0, 64]], 0, 0, ["SCS"], 64)
+    iota(T.SCS[:, 0:64:4], [[0, 16]], -16000000, 0, ["SCS"], 16)
+    iota(T.CUM[:, 128:144], [[0, 16]], n * 128, 0, [("CUM", 128, 144)], 16)
+    for t in range(R):
+        a, b = 256 * t, 256 * t + 256
+        now["seq"] = None if t else "main"
+        act(T.FP[:, a:b], T.FR[:, a:b].indirect(T.PL[:, 0:16]), F.Identity, [rg("FR", a, b), "PL"], [rg("FP", a, b)],
+            256, bias=192.0, gather=True)
+        now["seq"] = None
+        act(T.FX[:, a:b], T.FR[:, a:b], F.Identity, [rg("FR", a, b)], [rg("FX", a, b)], 256, bias=192.0)
+        for hf in range(2):
+            a, b = 256 * t + 128 * hf, 256 * t + 128 * hf + 128
+            sel(T.XZ[:, a:b], T.FX[:, a:b], [[0, 8], [-1, 16]], A.is_ge, 0.0, RAW[hf] - 1, 0, [rg("FX", a, b)],
+                [rg("XZ", a, b)], 128)
 
-    def spread(hv, src, name):
+    def xrep(t, u0, u1, q, after=(), slots=range(16)):
+        a, b, k = 256 * t + u0, 256 * t + u1, u1 - u0
+        for i in slots:
+            out, w = T.XR[:, 16 * a + i:16 * b:16], [("XR%d#%d" % (t, h), i, i + 1) for h in range(u0 // 128, u1 // 128)]
+            if q == "dve":
+                cp(out, T.FP[:, a:b], [("FP", a, b)], w, vec(k // 2))
+            elif q == "act":
+                act(out, T.FP[:, a:b], F.Identity, [("FP", a, b)], w, k, after=after)
+            else:
+                sel(out, T.FP[:, a:b], [[0, k]], A.is_equal, 0.0, 0, 0, [("FP", a, b)], w, k, after=after)
+
+    def spread(hv, src, name, dst="L"):
         lst, ln = (T.SL[:, 0:4], "SL") if hv == 0 else (T.SLB[:, 0:4], "SLB")
-        tt(T.L[:, 512 * hv:512 * hv + 512].indirect(lst), src[:, 64 * hv:64 * hv + 64], T.Q64[:], A.mult,
-           [rg(name, 64 * hv, 64 * hv + 64), ln, "Q64"], [rg("L", 512 * hv, 512 * hv + 512)])
+        tt(T[dst][:, 512 * hv:512 * hv + 512].indirect(lst), src[:, 64 * hv:64 * hv + 64], T.Q64[:], A.mult,
+           [rg(name, 64 * hv, 64 * hv + 64), ln, "Q64"], [rg(dst, 512 * hv, 512 * hv + 512)], 0.05 + 64 * SCA * CYC)
 
-    def preload():
+    def preload(after=()):
         for c in VCLS:
-            mm(P[c][:], T.BL[0:2, :], T.BR[0:2, :], True, False, ["BL", "BR"], ["P%d" % c])
+            mm(P[c][:], T.BL[0:2, :], T.BR[0:2, :], True, False, ["BL", "BR"], [pn(c)], 512, after)
 
-    def turn(c, bank):
-        mm(P[bank][:, 16 * c:16 * c + 16], T.L[:, 128 * c:128 * c + 128], T.I16[:], True, True,
-           [rg("L", 128 * c, 128 * c + 128), "I16"], ["P%d" % bank])
-
-    sel(T.ID[:], T.ONE[:, 0:128], [[-1, 128]], A.is_equal, 0.0, 0, 1, ["ONE"], ["ID"])
-    sel(T.NID[:], T.NEG[:, 0:128], [[-1, 128]], A.is_equal, 0.0, 0, 1, ["NEG"], ["NID"])
-    iota(T.C16[:], [[0, 8], [1, 16]], 0, 0, ["C16"])
-    xrep(0, 0, XPOOL)
-    sel(T.SC1[:], T.ONF[:], [[0, 4], [1, 32]], A.not_equal, -1.0e9, 0, 0, ["ONF"], ["SC1"])
-    sel(T.BT[:], T.ONF[:], [[-16, 8], [0, 16]], A.is_ge, 0.0, 0, 1, ["ONF"], ["BT"])
-    sel(T.E1[:], T.NEG[:], [[-16, 8], [-1, 17]], A.is_equal, 0.0, 0, 1, ["NEG"], ["E1"])
-    sel(T.BF[:], T.BT[:], [[16, 8], [0, 16]], A.is_ge, 0.0, 15, -1, ["BT"], ["BF"])
-    sel(T.E2[:], T.ONE[:], [[-16, 8], [0, 17]], A.is_equal, 0.0, 0, 1, ["ONE"], ["E2"])
-    iota(T.E1[:, 16:136:17], [[0, 8]], 0, 0, ["E1"])
-    for k in range(VACT, 8):
-        iota(T.VP[:, 2 * k:2 * k + 2, :], [[0, 2], [0, 240]], 0, 0, [rg("VP", 2 * k, 2 * k + 2)])
-    iota(T.LOC[:, 0:16], [[0, 2], [1, 8]], 0, 0, [("LOC", 0, 16)])
-    iota(T.LOC[:, 16:32], [[0, 2], [2, 4], [0, 2]], 0, 0, [("LOC", 16, 32)])
-    iota(T.LOC[:, 32:48], [[0, 2], [4, 2], [0, 4]], 0, 0, [("LOC", 32, 48)])
-    xrep(1, 0, 16 - XLATE)
+    def turn(src, bank):
+        for c in range(8):
+            mm(P[bank][:, 16 * c:16 * c + 16], T[src][:, 128 * c:128 * c + 128], T.I16[:], True, True,
+               [rg(src, 128 * c, 128 * c + 128), "I16"], [pn(bank)], 16)
+        act(T.AB[:], P[bank][:, 0:128], F.Identity, [pn(bank)], ["AB"], 128)
 
     def lists():
         cp(T.S2[:, 0:16], T.S[:], ["S"], [("S2", 0, 16)])
         ts(T.S2[:, 16:32], T.S[:], 1.0, None, A.add, None, ["S"], [("S2", 16, 32)])
 
+    def cands(first):
+        k = 128 if first else 256
+        for a in range(0, 512, k):
+            lst = T.S2[:, a // 16:(a + k) // 16]
+            if first:
+                ts(T.CF[:, a:a + k], T.MX[:, 0:2056].indirect(lst), -2048.0, None, A.add, None, ["MX", "S2"],
+                   [rg("CF", a, a + k)], gat(k))
+            else:
+                act(T.CF[:, a:a + k], T.MXF[:, 0:2056].indirect(lst), F.Identity, ["MXF", "S2"], [rg("CF", a, a + k)],
+                    k, bias=-2048.0, gather=True)
+            ts(T.CL[:, a:a + k], T.CF[:, a:a + k].indirect(T.PL[:, 0:k // 16]), 2048.0, None, A.add, None,
+               [rg("CF", a, a + k), "PL"], [rg("CL", a, a + k)], gat(k))
+
     preload()
+    now["seq"] = "main"
     for hv in range(2):
-        spread(hv, T.AN, "AN")
-        for c in range(4 * hv, 4 * hv + 4):
-            turn(c, 6 + hv)
-    cp(T.AB[:, 0:64], P[6][:, 0:64], ["P6"], [rg("AB", 0, 64)])
+        spread(hv, T.AN, "AN", "LN")
+        a, b = 512 * hv, 512 * hv + 512
+        op("dve", lambda a=a, b=b: V.transpose(T.L[:, a:b], T.LN[:, a:b]), vec(256), [rg("LN", a, b)], [rg("L", a, b)])
+    xrep(0, 0, 128, "act", slots=range(X0))
+    xrep(0, 0, 128, "dve", slots=range(X0, 16))
     lists()
-    cp(T.AB[:, 64:128], P[7][:, 64:128], ["P7"], [rg("AB", 64, 128)])
-    for hv in range(2):
-        spread(hv, T.AB, "AB")
-    ts(T.WB[:], T.CI[:], col(9), -32.0, A.is_equal, A.mult, pc + ["CI"], ["WB"])
-
-    def cands():
-        op("dve", lambda: V.tensor_copy(T.CL[:], T.MX[:, 0:2056].indirect(T.S2[:, 0:32])), ["MX", "S2"], ["CL"])
-
-    def cands_f(k):
-        a, b = 128 * k, 128 * k + 128
-        ts(T.CF[:, a:b], T.CL[:, a:b], -2048.0, None, A.add, None, ["CL"], [rg("CF", a, b)])
-
-    def tree_consts():
-        ms(T.CUM[:, 128:144], float(n * 128), [("CUM", 128, 144)])
-        ts(col(10), PM, 1.0, None, A.subtract, None, pr, [("PC", 10, 11)])
-        ts(col(11), PM, 2.0, None, A.subtract, None, pr, [("PC", 11, 12)])
-        ts(col(12), PM, 4.0, None, A.subtract, None, pr, [("PC", 12, 13)])
-        ts(col(13), PM, 128.0, None, A.add, None, pr, [("PC", 13, 14)])
-        ts(T.KA[:], T.LOC[:], PM, None, A.is_equal, None, pr + ["LOC"], ["KA"])
-        for l in range(3):
-            ts(T.KB[:, 16 * l:16 * l + 16], T.LOC[:, 16 * l:16 * l + 16], col(10 + l), None, A.is_equal, None,
-               [("PC", 10, 13), "LOC"], [("KB", 16 * l, 16 * l + 16)])
-        for l in range(3):
-            ts(T.VC[:, 16 * l:16 * l + 8], T.LOC[:, 16 * l:16 * l + 8], 16.0, None, A.mult, None,
-               ["LOC"], [("VC", 16 * l, 16 * l + 8)])
-            if l == 0:
-                tt(T.KA[:], T.KA[:], T.KB[:], A.subtract, ["KA", "KB"], ["KA"])
-            ts(T.VC[:, 16 * l + 8:16 * l + 16], T.LOC[:, 16 * l + 8:16 * l + 16], -16.0, 128.0 - 16.0 * (1 << l),
-               A.mult, A.add, ["LOC"], [("VC", 16 * l + 8, 16 * l + 16)])
-
-    for i in range(XPOOL, 16 - XACT):
-        cp(XR[0][:, i:4096:16], T.FR[:, 0:256], [("FR", 0, 256)], [xr_names(0)[i]])
+    now["seq"] = None
+    xrep(0, 128, 256, "pool")
+    cands(True)
+    for a in range(0, 2056, 514):
+        sel(T.MXF[:, a:a + 514], T.MX[:, a:a + 514], [[0, 514]], A.is_equal, 0.0, 0, 0, ["MX"], [rg("MXF", a, a + 514)], 514)
     BIAS = 192.0 + 1.0 / 128
     win = T.MW[:, 0:4096]
 
     for t in range(R):
-        xr = xr_names(t)
+        last = t == R - 1
+        now["tag"], now["seq"] = "%d means" % t, "main"
         for c in range(8):
             mm(P[c][:], T.L[:, 128 * c:128 * c + 128], T.MU[:, 512 * c:512 * c + 512], c not in VCLS, True,
-               [rg("L", 128 * c, 128 * c + 128), rg("MU", 512 * c, 512 * c + 512)], ["P%d" % c])
-        toks = MORDER.split()
-        for tok in toks:
+               [rg("L", 128 * c, 128 * c + 128), rg("MU", 512 * c, 512 * c + 512)], [pn(c)], 512)
+        for tok in MORDER.split():
             lo, hi = [256 * int(v) for v in tok[1:].split(":")]
             c = lo // 512
             a, b = lo - 512 * c, hi - 512 * c
             if tok[0] == "A":
-                act(T.MW[:, lo:hi], P[c][:, a:b], F.Identity, ["P%d" % c], [rg("MW", lo, hi)],
+                act(T.MW[:, lo:hi], P[c][:, a:b], F.Identity, [pn(c)], [rg("MW", lo, hi)], hi - lo,
                     bias=0.0 if c in VCLS else BIAS)
             elif tok[0] == "D":
-                ts(T.MW[:, lo:hi], P[c][:, a:b], 184.0, 199.0, A.max, A.min, ["P%d" % c], [rg("MW", lo, hi)])
+                ts(T.MW[:, lo:hi], P[c][:, a:b], 184.0, 199.0, A.max, A.min, [pn(c)], [rg("MW", lo, hi)], vec(hi - lo))
             else:
-                ts(T.MW[:, lo:hi], T.MW[:, lo:hi], 184.0, 199.0, A.max, A.min, [rg("MW", lo, hi)], [rg("MW", lo, hi)])
+                ts(T.MW[:, lo:hi], T.MW[:, lo:hi], 184.0, 199.0, A.max, A.min, [rg("MW", lo, hi)], [rg("MW", lo, hi)],
+                   vec((hi - lo) // 2))
+        now["seq"] = None
         if t == 0:
-            act(T.XO[:, 0:256], T.FR[:, 0:256], F.Identity, [("FR", 0, 256)], [("XO", 0, 256)], bias=192.0)
-            cands()
+            turn("LN", 4)
+        if last:
+            turn("L", 4)
 
         slot = {}
-
-        def d2(j, h, p0=0, p1=16):
-            return rg("D2", 32 * j + 16 * h + p0, 32 * j + 16 * h + p1)
-
-        def cgath(h, j0, j1):
-            for j in range(j0, j1):
-                slot.setdefault(j, len(slot))
-            a = 1024 * h + 256 * slot[j0]
-            b = a + 256 * (j1 - j0)
-            act(T.MG[:, a:b], win.indirect(T.CL[:, 256 * h + 16 * j0:256 * h + 16 * j1]), F.Identity,
-                ["MW", "CL"], [rg("MG", a, b)])
-            for j in range(j0, j1):
-                bank = CBANK[slot[j]]
-                o = P[bank][:, 256 * h:256 * h + 256]
-                m0 = 1024 * h + 256 * slot[j]
-                mm(o, T.NID[:], XR[t][:, 256 * j:256 * j + 256], True, False, ["NID"] + xr, ["P%d" % bank])
-                mm(o, T.ID[:], T.MG[:, m0:m0 + 256], False, True, ["ID", rg("MG", m0, m0 + 256)], ["P%d" % bank])
-
-        def csq(j):
-            bank = CBANK[slot[j]]
-            act(T.D2[:, 2 * j:2 * j + 2, :], P[bank][:], F.Square, ["P%d" % bank], [d2(j, 0), d2(j, 1)], bias=-192.0)
-
-        def gath(h, j0, j1, p0=0, p1=16):
-            e0, e1 = 16 * j0 + p0, 16 * (j1 - 1) + p1
-            a, b = 4096 * h + 16 * e0, 4096 * h + 16 * e1
-            tt(T.D[:, a:b], win.indirect(T.CL[:, 256 * h + e0:256 * h + e1]), XR[t][:, 16 * e0:16 * e1],
-               A.subtract, ["MW", "CL"] + xr, [rg("D", a, b)])
-
-        def sq(h, j0, j1, p0=0, p1=16):
-            e0, e1 = 16 * j0 + p0, 16 * (j1 - 1) + p1
-            a, b = 4096 * h + 16 * e0, 4096 * h + 16 * e1
-            act(T.D2[:, 2 * j0 + h:2 * j1:2, 16 * p0:16 * p1], T.D[:, a:b], F.Square, [rg("D", a, b)],
-                [d2(j, h, p0, p1) for j in range(j0, j1)], bias=-192.0)
-
-        def score(bank, j0, j1, p0=0, p1=16):
-            for p in range(p0, p1):
-                mm(P[bank][:, 0:32 * (j1 - j0)], T.WB[:, 15 - p:143 - p], T.D2[:, 2 * j0:2 * j1, 16 * p:16 * p + 16],
-                   p == 0, p == 15, ["WB"] + [d2(j, h, p, p + 1) for j in range(j0, j1) for h in range(2)],
-                   ["P%d" % bank])
-
-        def scan(bank, j0, j1):
-            w = 32 * (j1 - j0)
-            op("dve", lambda: V.tensor_tensor_scan(T.SK[:, 32 * j0:32 * j1], T.SC1[:, 0:w], P[bank][:, 0:w], 0.0,
-                                                   A.add, A.max),
-               ["SC1", "P%d" % bank], [rg("SK", 32 * j0, 32 * j1)])
-
+        scored = [0, 0]
+        mark = {}
+        nar = []
         tn = lambda k: ("TT", k, k + 1)
         nown = rg("NL", 16 * t + 8, 16 * t + 10)
 
-        def step(hf, k):
+        def run(h, r0, r1):
+            a, k = 4112 * (r0 // 16) + 2064 * h + 128 * (r0 % 16), 128 * (r1 - r0)
+            return (a, a + k, 256 * h + 8 * r0, 256 * h + 8 * r1, T.XR[:, 4096 * t + 128 * r0:4096 * t + 128 * r1],
+                    "XR%d#%d" % (t, r0 // 16), T.D2[:, 16 * r0 + h:16 * r1:2, :], rg("D2#%d" % h, r0, r1))
+
+        def cgath(h, r0, r1):
+            a, b, e0, e1, x, xn, _, _ = run(h, r0, r1)
+            bank = slot[h, r0] = CBANK[len(slot)]
+            act(T.D[:, a:b], win.indirect(T.CL[:, e0:e1]), F.Identity, ["MW", rg("CL", e0, e1)], [rg("D", a, b)],
+                b - a, gather=True)
+            mm(P[bank][:, 0:b - a], T.NID[:], x, True, False, ["NID", xn], [pn(bank)], b - a)
+            mm(P[bank][:, 0:b - a], T.ID[:], T.D[:, a:b], False, True, ["ID", rg("D", a, b)], [pn(bank)], b - a)
+
+        def csq(h, r0, r1):
+            a, b, _, _, _, _, d2, dn = run(h, r0, r1)
+            act(d2, P[slot[h, r0]][:, 0:b - a], F.Square, [pn(slot[h, r0])], [dn], b - a)
+
+        def gath(h, r0, r1):
+            a, b, e0, e1, x, xn, _, _ = run(h, r0, r1)
+            tt(T.D[:, a:b], win.indirect(T.CL[:, e0:e1]), x, A.subtract, ["MW", rg("CL", e0, e1), xn], [rg("D", a, b)],
+               gat(b - a))
+
+        def sq(h, r0, r1):
+            a, b, _, _, _, _, d2, dn = run(h, r0, r1)
+            act(d2, T.D[:, a:b], F.Square, [rg("D", a, b)], [dn], b - a)
+
+        def vsq(h, r0, r1):
+            a, b, _, _, _, _, d2, dn = run(h, r0, r1)
+            tt(d2, T.D[:, a:b], T.D[:, a:b], A.mult, [rg("D", a, b)], [dn], vec(b - a))
+
+        def score(r0, r1):
+            hf = r0 // 16
+            bank = HBANK[hf][0]
+            if scored[hf] == 0:
+                mm(P[bank][:, 0:256], T.ONE[0:1, 0:128], T.JB[0:1, :], True, False, ["ONE", "JB"], [pn(bank)], 256)
+            for r in range(r0, r1):
+                scored[hf] += 1
+                mm(P[bank][:, 0:256], T.WB[:, 15 - r % 16:143 - r % 16], T.D2[:, 16 * r:16 * r + 16, :], False,
+                   scored[hf] == 16, ["WB", rg("D2#0", r, r + 1), rg("D2#1", r, r + 1)], [pn(bank)], 256)
+
+        def half(hf):
+            now["tag"], now["seq"] = "%d%s" % (t, "ab"[hf]), None
             j0, j1 = 8 * hf, 8 * hf + 8
             u0, u1 = 128 * hf, 128 * hf + 128
-            bx, by, bv = (4, 5, 2) if hf == 0 else (0, 1, 3)
-            px, py = "P%d" % bx, "P%d" % by
-            if k == 1:
-                ts(T.RI[:, j0:j1], T.SK[:, 32 * j0 + 31:32 * j1:32], 31, None, A.bitwise_and, None,
-                   [rg("SK", 32 * j0, 32 * j1)], [rg("RI", j0, j1)])
-                if t == 0 and hf == 0:
-                    masks(0)
-                    masks(1)
-            elif k == 2:
-                cp(T.RL[:, j0:j1], T.RI[:, j0:j1], [rg("RI", j0, j1)], [rg("RL", j0, j1)])
-            elif k in (3, 4):
-                h = k - 3
+            bk, bx, by, bv = HBANK[hf]
+            mark["Z"] = scan(T.SK[:, 32 * j0:32 * j1], T.SC1[:], P[bk][:, 0:256], ["SC1", pn(bk)],
+                             [rg("SK", 32 * j0, 32 * j1)], 256)
+            ts(T.RO[:, j0:j1], T.SK[:, 32 * j0 + 31:32 * j1:32], 4095, None, A.bitwise_and, None,
+               [rg("SK", 32 * j0, 32 * j1)], [rg("RO", j0, j1)])
+            mark["L"] = ts(T.RL[:, j0:j1], T.RO[:, j0:j1], -1.0, 2191.0, A.mult, A.add, [rg("RO", j0, j1)],
+                           [rg("RL", j0, j1)])
+            ts(T.OF[:, j0:j1], T.RO[:, j0:j1], -1.0, col(6), A.mult, A.add, [rg("RO", j0, j1)] + pc(6), [rg("OF", j0, j1)])
+            for h in range(2):
                 a, b = 256 * h + u0, 256 * h + u1
-                tt(T.CM[:, a:b], T.J[:, 32 * h:32 * h + 32].indirect(T.RL[:, j0:j1]), T.CF[:, a:b], A.mult,
-                   ["J", rg("RL", j0, j1), rg("CF", a, b)], [rg("CM", a, b)])
-                for bank in (bx, by):
-                    mm(P[bank][:, 0:128], T.BH[:], T.CM[:, a:b], h == 0, h == 1, ["BH", rg("CM", a, b)],
-                       ["P%d" % bank])
-            elif k == 5:
-                op("dve", lambda: V.tensor_tensor_scan(T.SW[:, u0:u1], T.SC2[:], P[bx][:, 0:128], 0.0, A.add, A.max),
-                   ["SC2", px], [rg("SW", u0, u1)])
-            elif k == 6:
-                act(T.CS[:, u0:u1], P[by][:, 0:128], F.Identity, [py], [rg("CS", u0, u1)],
-                    bias=6144.0 + 128.0 - 255.5 / 16, scale=1.0 / 16)
-                mm(P[bx][:, 0:136], T.CS[:, u0:u1], T.E2[:], True, False, [rg("CS", u0, u1), "E2"], [px])
-            elif k == 7:
-                act(T.SG[:, u0:u1], P[by][:, 0:128], F.Sign, [py] + pc,
-                    [rg("SG", u0, u1), rg("NL", 16 * t + 8 + hf, 16 * t + 9 + hf)], bias=col(5),
-                    acc=T.NL[:, 16 * t + 8 + hf:16 * t + 9 + hf])
-                if t == 0:
-                    send(T.NL[:, 8 + hf:9 + hf], [T.NL[:, 2 * k2 + hf:2 * k2 + hf + 1] for k2 in range(1, n)], "nar0",
-                         [rg("NL", 8 + hf, 9 + hf)])
-                elif hf == 1:
-                    send(T.NL[:, 16 * t + 8:16 * t + 10],
-                         [T.NL[:, 16 * t + 2 * k2:16 * t + 2 * k2 + 2] for k2 in range(1, n)], "nar%d" % t, [nown])
-            elif k == 8:
-                a = 256 * t + u0
-                act(T.YW[:, a:a + 128], P[by][:, 0:128], F.Identity, [py], [rg("YW", a, a + 128)], bias=2048.0)
-                if hf == 1:
-                    dma("sync", T.yw[:, 256 * t:256 * t + 256], T.YW[0:128:16, 256 * t:256 * t + 256],
-                        [rg("YW", 256 * t, 256 * t + 256)], ())
-            elif k == 9:
-                ts(T.WL[:, j0:j1], T.SW[:, u0 + 15:u1:16], col(8), None, A.add, None, [rg("SW", u0, u1)] + pc,
-                   [rg("WL", j0, j1)])
-            elif k == 10:
-                act(T.VG[:, u0:u1], T.MU[:, 0:4096].indirect(T.WL[:, j0:j1]), F.Identity, ["MU", rg("WL", j0, j1)],
-                    [rg("VG", u0, u1)])
-                mm(P[bv][:, 0:128], T.VG[:, u0:u1], T.ID[:], True, True, [rg("VG", u0, u1), "ID"], ["P%d" % bv])
-            elif k == 11:
-                tt(T.EG[:, u0:u1], win.indirect(T.WL[:, j0:j1]), T.XO[:, 256 * t + u0:256 * t + u1], A.subtract,
-                   ["MW", rg("WL", j0, j1), rg("XO", 256 * t, 256 * t + 256)], [rg("EG", u0, u1)])
-                mm(P[bx][:, 0:136], T.EG[:, u0:u1], T.E1[:], False, True, [rg("EG", u0, u1), "E1"], [px])
-            elif k == 12:
-                if (hf, k) in ONACT:
-                    act(T.TT[:, j0, :], P[bx][:, 0:136], F.Identity, [px], [tn(j0)], bias=16.0 - 6144.0)
+                mark["C"] = tt(T.CM[:, a:b], T.JJ[:, 2064 - 2064 * h:4256 - 2064 * h].indirect(T.RL[:, j0:j1]),
+                               T.CF[:, a:b], A.mult, ["JJ", rg("RL", j0, j1), rg("CF", a, b)], [rg("CM", a, b)], gat(128))
+            for bank in (bx, by):
+                for h in range(2):
+                    a, b = 256 * h + u0, 256 * h + u1
+                    mark["B"] = mm(P[bank][:, 0:128], T.BH[:], T.CM[:, a:b], h == 0, h == 1, ["BH", rg("CM", a, b)],
+                                   [pn(bank)], 128)
+            scan(T.SW[:, u0:u1], T.SC2[:], P[bx][:, 0:128], ["SC2", pn(bx)], [rg("SW", u0, u1)], 128)
+            mark["W"] = ts(T.WL[:, j0:j1], T.SW[:, u0 + 15:u1:16], col(8), None, A.add, None,
+                           [rg("SW", u0, u1)] + pc(8), [rg("WL", j0, j1)])
+            mark["S"] = act(T.SG[:, u0:u1], P[by][:, 0:128], F.Sign, [pn(by)] + pc(5),
+                            [rg("SG", u0, u1), rg("NL", 16 * t + 8 + hf, 16 * t + 9 + hf)], 150, bias=col(5),
+                            acc=T.NL[:, 16 * t + 8 + hf:16 * t + 9 + hf])
+            if t == 0:
+                nar.append(send(T.NL[:, 8 + hf:9 + hf], [T.NL[:, 2 * k + hf:2 * k + hf + 1] for k in range(1, n)],
+                                "nar0", [rg("NL", 8 + hf, 9 + hf)]))
+            elif hf == 1:
+                nar.append(send(T.NL[:, 16 * t + 8:16 * t + 10],
+                                [T.NL[:, 16 * t + 2 * k:16 * t + 2 * k + 2] for k in range(1, n)], "nar%d" % t, [nown]))
+            def affine(step, out, in_, r, w, k, scale=1.0, bias=0.0, gather=False):
+                if step in ON_VECTOR[hf]:
+                    ts(out, in_, scale, bias, A.mult, A.add, r, w, gat(k) if gather else vec(k))
                 else:
-                    ts(T.TT[:, j0, :], P[bx][:, 0:136], 16.0 - 6144.0, None, A.add, None, [px], [tn(j0)])
-            elif k == 13:
-                act(T.VP[:, j0:j1, 112:128], P[bv][:, 0:128], F.Identity, ["P%d" % bv], [rg("VP", j0, j1)])
-            elif k in (14, 15, 16):
-                for c in ((1, 2, 3), (4, 5), (6, 7))[k - 14]:
-                    if (hf, k) in ONACT:
-                        act(T.TT[:, j0 + c, :], T.TT[:, j0, :], F.Relu, [tn(j0)], [tn(j0 + c)], bias=-32.0 * c)
-                    else:
-                        ts(T.TT[:, j0 + c, :], T.TT[:, j0, :], -32.0 * c, 0.0, A.add, A.max, [tn(j0)], [tn(j0 + c)])
-            elif k in (17, 18):
-                cv = k - 17
+                    act(out, in_, F.Identity, r, w, k, bias=bias, scale=scale, gather=gather)
+
+            bc = bx if "C" in ON_VECTOR[hf] else by
+            affine("C", T.CS[:, u0:u1], P[bc][:, 0:128], [pn(bc)], [rg("CS", u0, u1)], 128, 1.0 / 16,
+                   6144.0 + 128.0 - 255.5 / 16)
+            affine("E", T.EG[:, u0:u1], T.D[:, 4112 * hf:4112 * hf + 4112].indirect(T.OF[:, j0:j1]),
+                   [rg("D", 4112 * hf, 4112 * hf + 4112), rg("OF", j0, j1)], [rg("EG", u0, u1)], 128, 1.0, 0.0, True)
+            affine("V", T.VG[:, u0:u1], T.MU[:, 0:4096].indirect(T.WL[:, j0:j1]), ["MU", rg("WL", j0, j1)],
+                   [rg("VG", u0, u1)], 128, -1.0 if last else 1.0, 0.0, True)
+            xz, xn = T.XZ[:, 256 * t + u0:256 * t + u1], rg("XZ", 256 * t + u0, 256 * t + u1)
+            eg, vg = T.EG[:, u0:u1], T.VG[:, u0:u1]
+            if last:
+                mm(P[bv][:, 0:128], xz, T.ID[:], True, False, [xn, "ID"], [pn(bv)], 128)
+                mm(P[bv][:, 0:128], eg, T.NID[:], False, True, [rg("EG", u0, u1), "NID"], [pn(bv)], 128)
+                mm(P[bk][:, 0:136], T.CS[:, u0:u1], T.E2[:], True, False, [rg("CS", u0, u1), "E2"], [pn(bk)], 136)
+                mm(P[bk][:, 0:136], vg, T.E1[:], False, True, [rg("VG", u0, u1), "E1"], [pn(bk)], 136)
+            else:
+                mm(P[bk][:, 0:136], xz, T.E3[:], True, False, [xn, "E3"], [pn(bk)], 136)
+                mm(P[bk][:, 0:136], eg, T.E1[:], False, False, [rg("EG", u0, u1), "E1"], [pn(bk)], 136)
+                mm(P[bk][:, 0:136], T.CS[:, u0:u1], T.E2[:], False, True, [rg("CS", u0, u1), "E2"], [pn(bk)], 136)
+                mm(P[bv][:, 0:128], vg, T.ID[:], True, True, [rg("VG", u0, u1), "ID"], [pn(bv)], 128)
+            affine("P", T.VP[:, j0:j1, 112:128], P[bv][:, 0:128], [pn(bv)], [rg("VP", j0, j1)], 128)
+            affine("T", T.TT[:, j0, :], P[bk][:, 0:136], [pn(bk)], [tn(j0)], 136, 1.0, 16.0 - 6144.0)
+            for c in range(1, 8):
+                if c in RELU_ACT[hf]:
+                    act(T.TT[:, j0 + c, :], T.TT[:, j0, :], F.Relu, [tn(j0)], [tn(j0 + c)], 136, bias=-32.0 * c)
+                else:
+                    mark["R"] = ts(T.TT[:, j0 + c, :], T.TT[:, j0, :], -32.0 * c, 0.0, A.add, A.max, [tn(j0)],
+                                   [tn(j0 + c)], vec(68))
+            a = 256 * t + u0
+            act(T.YW[:, a:a + 128], P[by][:, 0:128], F.Identity, [pn(by)], [rg("YW", a, a + 128)], 128, bias=2048.0)
+
+        def sums(hf):
+            now["tag"], now["seq"] = "%d%s" % (t, "ab"[hf]), None
+            j0, j1 = 8 * hf, 8 * hf + 8
+            prev = []
+            for cv in range(len(CUT) - 1):
                 c0, c1 = CUT[cv], CUT[cv + 1]
                 for s in range(8):
-                    mm(P[6 + cv][:, 0:17 * (c1 - c0)], T.VP[:, j0 + s, 112 - 16 * s:240 - 16 * s],
-                       T.TT[:, j0 + c0:j0 + c1, 17 * s:17 * s + 17], hf == 0 and s == 0,
-                       hf == 1 and s == 7, [rg("VP", j0, j1), rg("TT", j0 + c0, j0 + c1)], ["P%d" % (6 + cv)])
+                    prev = [mm(P[6 + cv][:, 0:17 * (c1 - c0)], T.VP[:, j0 + s, 112 - 16 * s:240 - 16 * s],
+                               T.TT[:, j0 + c0:j0 + c1, 17 * s:17 * s + 17], hf == 0 and s == 0, hf == 1 and s == 7,
+                               [rg("VP", j0, j1), rg("TT", j0 + c0, j0 + c1)], [pn(6 + cv)], 17 * (c1 - c0), prev)]
 
-        def state(k):
-            if k == 0:
-                ts(T.HS[:], T.RI[:], 16.0, None, A.is_lt, None, ["RI"], ["HS"])
-            elif k == 1:
-                tt(T.S[:], T.S[:], T.HS[:], A.add, ["S", "HS"], ["S"])
-            else:
-                lists()
-
-        def pack(cv):
-            for c in range(CUT[cv], CUT[cv + 1]):
-                a = 128 * t + 16 * c
-                bank, c0 = 6 + cv, 17 * (c - CUT[cv])
-                ts(T.GS[:, a:a + 16], P[bank][:, c0:c0 + 16], P[bank][:, c0 + 16:c0 + 17], 32768.0,
-                   A.subtract, A.add, ["P%d" % bank], [rg("GS", a, a + 16)])
-
-        def part(k):
-            if t < R - 1:
-                op("dve", lambda: V.tensor_copy(T.CL[:, 128 * k:128 * k + 128],
-                                                T.MX[:, 0:2056].indirect(T.S2[:, 8 * k:8 * k + 8])),
-                   ["MX", "S2"], [rg("CL", 128 * k, 128 * k + 128)])
-
-        def bounds(k):
-            if k == 0:
-                ts(P[4][:, 0:128], T.AB[:], -2.0, -127.0, A.add, A.max, ["AB"], [("P4", 0, 128)])
-            else:
-                ts(P[4][:, 128:256], T.AB[:], 2.0, 127.0, A.add, A.min, ["AB"], [("P4", 128, 256)])
-
-        calls = {"k": part, "l": bounds, "c": cgath, "q": csq, "g": gath, "s": sq, "m": score, "z": scan, "a": lambda k: step(0, k),
-                 "b": lambda k: step(1, k), "h": state, "p": pack, "f": cands_f}
-        for tok in (PLAN0 if t == 0 else PLAN).replace("\n", "").split("|"):
+        steps = {"c": cgath, "q": csq, "g": gath, "s": sq, "v": vsq, "m": score, "w": half, "u": sums}
+        for tok in (PLAN if t else PLAN0).replace("\n", "").split("|"):
             f = tok.split()
-            calls[f[0]](*[int(v) for v in f[1:]])
+            now["tag"], now["seq"] = "%d%s" % (t, f[0]), "main"
+            if f[0] in mark:
+                now["gate"] = [mark[f[0]]]
+            else:
+                steps[f[0]](*[int(v) for v in f[1:]])
+        now["tag"], now["seq"] = "%dp" % t, None
+        for cv in range(len(CUT) - 1):
+            for c in range(CUT[cv], CUT[cv + 1]):
+                a, c0 = 128 * t + 16 * c, 17 * (c - CUT[cv])
+                ts(T.GS[:, a:a + 16], P[6 + cv][:, c0:c0 + 16], P[6 + cv][:, c0 + 16:c0 + 17], 32768.0,
+                   A.subtract, A.add, [pn(6 + cv)], [rg("GS", a, a + 16)])
         gs = rg("GS", 128 * t, 128 * t + 128)
-        send(T.GS[:, 128 * t:128 * t + 128],
-             [T.GL[:, 384 * t + 128 * k:384 * t + 128 * k + 128] for k in range(n - 1)], "gar%d" % t, [gs])
-        if t == 0:
-            xrep(1, 16 - XLATE, 16)
-        if t + 2 < R:
-            xrep(t + 2, 0, 16)
+        gar = send(T.GS[:, 128 * t:128 * t + 128],
+                   [T.GL[:, 384 * t + 128 * k:384 * t + 128 * k + 128] for k in range(n - 1)], "gar%d" % t, [gs])
+        now["tag"] = "%dx" % t
+        if not last and XENG[t] == "act":
+            xrep(t + 1, 0, 256, "act", nar)
+        if t + 2 < R and XENG[t + 1] == "pool":
+            xrep(t + 2, 0, 256, "pool", [gar])
         if t == 2:
-            iota(T.IW[:, 0:2048], [[1, 2048]], 0, 0, [("IW", 0, 2048)])
-            iota(T.IW[:, 2048:2056], [[1, 8]], 0, 0, [("IW", 2048, 2056)])
+            iota(T.IW[:, 0:2048], [[1, 2048]], 0, 0, [("IW", 0, 2048)], 2048, after=[gar])
+            iota(T.IW[:, 2048:2056], [[1, 8]], 0, 0, [("IW", 2048, 2056)], 8, after=[gar])
 
-        if t == 0:
-            tree_consts()
-            act(T.XO[:, 256:1024], T.FR[:, 256:1024], F.Identity, ["FR"], [("XO", 256, 1024)], bias=192.0)
-        act(T.AM[:], T.AB[:], F.Identity, ["AB"], ["AM"], bias=-127.5 / 256)
-        if t < R - 1:
-            preload()
-        act(T.NJ[:], T.NL[:, 16 * t + 2:16 * t + 10], F.Identity, [nown], ["NJ", "NS"], acc=T.NS[:, 0:1],
-            ext=("nar%d" % t, neng * (n - 1) * (2 if t == 0 else 1)))
-        act(T.RK[:], T.KA[:], F.Identity, ["KA", "NS"], ["RK"], scale=T.NS[:, 0:1])
-        mm(P[2][:, 0:48], T.BF[:], T.RK[:], True, True, ["BF", "RK"], ["P2"])
-        if t == R - 1:
-            act(T.YS[:], T.IW[:, 0:2056].indirect(T.S2[:, 0:16]), F.Identity, ["IW", "S2"], ["YS"])
-            dma("sync", T.ys[:], T.YS[0:128:16, :], ["YS"], ())
-        ts(T.OWN[:, 0:128], T.GS[:, 128 * t:128 * t + 128], 1.0 / 256, None, A.mult, None, [gs], [("OWN", 0, 128)])
-        fill = [k for k in range(4) if ("k %d" % k) not in (PLAN0 if t == 0 else PLAN)]
+        now["tag"] = "%dh" % t
+        dma("sync", T.yw[:, 256 * t:256 * t + 256], T.YW[0:128:16, 256 * t:256 * t + 256],
+            [rg("YW", 256 * t, 256 * t + 256)], (), 8192)
+        ts(T.HS[:], T.RO[:], 1024.0, None, A.is_lt, None, ["RO"], ["HS"])
+        tt(T.S[:], T.S[:], T.HS[:], A.add, ["S", "HS"], ["S"])
+        lists()
+        if not last:
+            cands(False)
+        else:
+            act(T.YS[:], T.IW[:, 0:2056].indirect(T.S2[:, 0:16]), F.Identity, ["IW", "S2"], ["YS"], 256, gather=True)
+            dma("sync", T.ys[:], T.YS[0:128:16, :], ["YS"], (), 8192)
 
-        def more():
-            if fill:
-                part(fill.pop(0))
+        now["tag"] = "%dtree" % t
+        act(T.AM[:], T.AB[:], F.Identity, ["AB"], ["AM"], 128, bias=-127.5 / 256)
+        ts(P[4][:, 0:128], T.AB[:], -2.0, -127.0, A.add, A.max, ["AB"], [pn(4, 0, 128)], vec(128))
+        ts(P[4][:, 128:256], T.AB[:], 2.0, 127.0, A.add, A.min, ["AB"], [pn(4, 128, 256)], vec(128))
+        if not last:
+            preload([gar])
+        act(T.NJ[:, 0:8], T.NL[:, 16 * t + 2:16 * t + 10], F.Identity, [nown], ["NJ"], 30, acc=T.NJ[:, 8:9],
+            ext=("nar%d" % t, neng * (n - 1) * (2 if t == 0 else 1)), after=nar)
+        act(T.RK[:], T.KA[:], F.Identity, ["KA", "NJ"], ["RK"], 64, scale=T.NJ[:, 8:9], bias=-519.0 * 16)
+        mm(P[2][:, 0:64], T.BF[:], T.RK[:], True, True, ["BF", "RK"], [pn(2)], 256)
+        tt(T.OK[:], P[2][:, 0:64], T.VC[:], A.min, [pn(2), "VC"], ["OK"])
+        scan(T.SM[:], T.SCS[:], T.OK[:], ["SCS", "OK"], ["SM"], 64)
+        ts(T.LH[:, 8:16], T.SM[:, 35:64:4], -1.0, None, A.mult, None, ["SM"], [("LH", 8, 16)])
+        cp(T.LH[:, 0:8], T.SM[:, 3:32:4], ["SM"], [("LH", 0, 8)])
+        ts(T.OWN[:], T.GS[:, 128 * t:128 * t + 128], 1.0 / 256, None, A.mult, None, [gs], ["OWN"], vec(128))
 
-        more()
-        ts(T.OK[:], P[2][:, 0:48], 519.0, None, A.is_ge, None, ["P2"], ["OK"])
-        more()
-        tt(T.OK[:], T.OK[:], T.VC[:], A.mult, ["OK", "VC"], ["OK"])
-        more()
-        tt(T.M1[:], T.OK[:, 0:16], T.OK[:, 16:32], A.max, ["OK"], ["M1"])
-        more()
-        tt(T.M2[:], T.M1[:], T.OK[:, 32:48], A.max, ["OK", "M1"], ["M2"])
-
-        def late(k):
-            if k == 0:
-                ts(T.LH[:, 8:16], T.M2[:, 8:16], -1.0, col(13), A.mult, A.add, ["M2", "PC"], [("LH", 8, 16)])
-            elif k == 1:
-                ts(T.LH[:, 0:8], T.M2[:, 0:8], PM, None, A.add, None, ["M2", "PC"], [("LH", 0, 8)])
-
-        ts(P[0][:, 0:256], T.GL[:, 384 * t:384 * t + 256], 1.0 / 256, None, A.mult, None, [], [rg("P0", 0, 256)],
-           ext=("gar%d" % t, neng * (n - 1)))
-        late(0)
-        ts(T.C2[:], T.GL[:, 384 * t + 256:384 * t + 384], 1.0 / 256, None, A.mult, None, [], ["C2"])
-        late(1)
-        tt(T.C1[:], P[0][:, 0:128], T.OWN[:, 0:128], A.add, [rg("P0", 0, 128), "OWN"], ["C1"])
+        now["tag"] = "%dupd" % t
+        landed = dict(ext=("gar%d" % t, neng * (n - 1)), after=[gar])
+        ts(P[0][:, 0:256], T.GL[:, 384 * t:384 * t + 256], 1.0 / 256, None, A.mult, None, [], [pn(0, 0, 256)],
+           vec(256), **landed)
+        ts(T.C2[:], T.GL[:, 384 * t + 256:384 * t + 384], 1.0 / 256, None, A.mult, None, [], ["C2"], vec(128), **landed)
+        tt(T.C1[:], P[0][:, 0:128], T.OWN[:], A.add, [pn(0, 0, 128), "OWN"], ["C1"], vec(128))
         hv2 = [(0, 64), (64, 128)]
         for (a, b) in hv2:
             tt(P[0][:, 256 + a:256 + b], P[0][:, 128 + a:128 + b], T.C2[:, a:b], A.add,
-               [rg("P0", 128 + a, 128 + b), "C2"], [rg("P0", 256 + a, 256 + b)])
-        late(2)
+               [pn(0, 128 + a, 128 + b), "C2"], [pn(0, 256 + a, 256 + b)])
         for (a, b) in hv2:
-            tt(T.CUM[:, a:b], P[0][:, 256 + a:256 + b], T.C1[:, a:b], A.add, [rg("P0", 256 + a, 256 + b), "C1"],
+            tt(T.CUM[:, a:b], P[0][:, 256 + a:256 + b], T.C1[:, a:b], A.add, [pn(0, 256 + a, 256 + b), "C1"],
                [rg("CUM", a, b)])
         cw = T.CUM[:, 0:144]
         for hv, (a, b) in enumerate(hv2):
             tt(T.H[:, a:b], cw.indirect(T.LH[:, 8 + 4 * hv:12 + 4 * hv]), T.AM[:, a:b], A.subtract,
-               ["CUM", "LH", "AM"], [rg("H", a, b)])
+               ["CUM", "LH", "AM"], [rg("H", a, b)], gat(64))
         for hv, (a, b) in enumerate(hv2):
             tt(T.TI[:, a:b], cw.indirect(T.LH[:, 4 * hv:4 * hv + 4]), T.H[:, a:b], A.subtract,
-               ["CUM", "LH", rg("H", a, b)], [rg("TI", a, b)])
+               ["CUM", "LH", rg("H", a, b)], [rg("TI", a, b)], gat(64))
         for (a, b) in hv2:
-            tt(T.T2[:, a:b], T.TI[:, a:b], P[4][:, a:b], A.max, [rg("TI", a, b), "P4"], [rg("T2", a, b)])
+            tt(T.T2[:, a:b], T.TI[:, a:b], P[4][:, a:b], A.max, [rg("TI", a, b), pn(4, a, b)], [rg("T2", a, b)])
+        new = "YA" if last else "AB"
         for (a, b) in hv2:
-            tt(T.AB[:, a:b], T.T2[:, a:b], P[4][:, 128 + a:128 + b], A.min, [rg("T2", a, b), "P4"], [rg("AB", a, b)])
-        for hv in range(2):
-            spread(hv, T.AB, "AB")
+            tt(T[new][:, a:b], T.T2[:, a:b], P[4][:, 128 + a:128 + b], A.min, [rg("T2", a, b), pn(4, 128 + a, 128 + b)],
+               [rg(new, a, b)])
+        if not last:
+            for hv in range(2):
+                spread(hv, T.AB, "AB")
 
-    for c in range(8):
-        turn(c, 4 + c // 4)
-    act(T.YA[:, 0:64], P[4][:, 0:64], F.Identity, ["P4"], [rg("YA", 0, 64)])
-    cp(T.YA[:, 64:128], P[5][:, 64:128], ["P5"], [rg("YA", 64, 128)])
-    dma("sync", T.ya[:], T.YA[:], ["YA"], ())
+    dma("sync", T.ya[:], T.YA[:], ["YA"], (), 65536)
+    issue(g, T, calls)
     g.wait_ge(T.sem.sent, sends[0])
-    finish("sync")

from concourse.bass import DstId, RemoteDMATransfer
from concourse.mybir import AluOpType, ActivationFunctionType

R = 4
_B = {
    "bfloat16": dict(MU=4096, FR=1024, FP=1024, FX=1024, XZ=1024, XR=16384, AN=128, AB=128, L=1024, LN=1024, MW=4096, D=8224,
                     JB=256, JJ=4256, CS=256, SG=256, VG=256, EG=256, ZR=480, I16=16, WB=144,
                     ONE=136, NEG=136, ID=128, NID=128, E1=136, E2=136, E3=136, Q64=64, BL=128, BR=512),
    "float32": dict(AM=128, SW=256, NL=64, NJ=16, RK=64, OK=64, SM=64, OWN=128, C1=128, CF=512, MXF=2056,
                    C2=128, CUM=144, H=128, T2=128, YW=1024, YS=256, YA=128, PC=16, CI=144, C16=128, LOC=64, HIC=64,
                    KA=64, KB=64, VC=64, SCS=64, SC1=256, SC2=128, SC3=128, BT=128, BF=128, IW=2056, K16=16),
    "int32": dict(MX=2056, S=16, SK=512, RO=16, HS=16, TI=128, IP=4, SLI=8),
    "uint16": dict(S2=32, CL=512, RL=16, OF=16, WL=16, GS=512, GL=1536, LH=16, SL=8, SLB=4, PL=16),
    "float16": dict(CM=512, BH=128),
}
SCRATCH = {}
for _d in _B:
    for _n in _B[_d]:
        SCRATCH[_n] = ("sbuf", [128, _B[_d][_n]], _d)
SCRATCH["D2"] = ("sbuf", [128, 512, 16], "bfloat16")
SCRATCH["TT"] = ("sbuf", [128, 16, 136], "bfloat16")
SCRATCH["VP"] = ("sbuf", [128, 16, 240], "bfloat16")
for _k in range(8):
    SCRATCH["P%d" % _k] = ("psum", [128, 512], "float32")

NDMA = 48
SEMAPHORES = (["pe", "dve", "act", "pool", "sent"] + ["d%d" % k for k in range(NDMA)]
              + ["nar%d" % t for t in range(R)] + ["gar%d" % t for t in range(R)])

A = AluOpType
F = ActivationFunctionType

MORDER = "A0:2 D2:4 A4:6 D6:8 A8:10 C0:2 D10:12 C4:6 A12:14 C8:10 A14:15 C12:14 A15:16 C14:15 C15:16"
VCLS = (1, 3, 5)
PLAN = """c 0 0 4|c 1 0 4|c 0 4 8|c 1 4 8|g 0 8 11|g 1 8 11|g 0 11 14|v 0 8 11|v 1 8 11|m 8 11|q 0 0 4|q 1 0 4|m 0 4|
g 1 11 14|g 0 14 16|v 0 11 14|v 1 11 14|m 11 14|q 0 4 8|q 1 4 8|m 4 8|g 1 14 16|v 0 14 16|s 1 14 16|m 14 16|
c 0 16 19|c 1 16 19|c 0 19 22|g 0 22 26|w 0|g 1 22 26|q 0 16 19|c 1 19 22|g 0 26 29|v 0 22 26|q 1 16 19|m 16 19|
s 1 22 26|m 22 26|g 1 26 29|q 0 19 22|v 0 26 29|q 1 19 22|m 19 22|g 0 29 32|u 0|s 1 26 29|m 26 29|g 1 29 31|
s 0 29 32|g 1 31 32|v 1 29 31|m 29 31|s 1 31 32|m 31 32|w 1|u 1"""
RAW = (8, 6)
PLAN0 = PLAN
for _g, _c in (("Z", "g 1 22 26"), ("L", "g 0 26 29"), ("C", "g 1 26 29"), ("B", "m 22 26"), ("S", "q 0 19 22")):
    PLAN0 = PLAN0.replace(_c, _g + "|" + _c)
X0 = 6
CBANK = (0, 1, 4, 5, 0, 1, 7, 0)
HBANK = ((2, 4, 5, 6), (3, 1, 2, 0))
CUT = (0, 4, 8)
RELU_ACT = ((6, 7), (7,))
ON_VECTOR = ("", "VT")
XENG = ("act", "pool", "pool")
CYC, GAT, SCA, PEC, PE0, SEM, ACT0, DMA0, BPU = 0.0009, 1.4, 3.5, 0.00055, 0.0, 0.13, 0.015, 1.2, 550e3
CALL1, CALL, FLY = 4.0, 0.5, 1.7
PASSES = 2


def _norm(rs):
    return [(r, 0, 1 << 30) if isinstance(r, str) else r for r in rs]


def link(calls):
    hist, bank_last, seq_last = {}, {}, {}
    for i, c in enumerate(calls):
        pre = {}
        for (regs, writing) in ((c["r"], False), (c["w"], True)):
            for (name, lo, hi) in regs:
                for (plo, phi, pw, k) in hist.get(name, ()):
                    if plo < hi and lo < phi and (pw or writing):
                        pre[k] = True
                if name[0] == "P" and name[1:].isdigit() and name in bank_last:
                    k = bank_last[name]
                    pre[k] = pre.get(k, False) or calls[k]["q"] != c["q"]
        if c["seq"] is not None:
            if c["seq"] in seq_last:
                pre.setdefault(seq_last[c["seq"]], False)
            seq_last[c["seq"]] = i
        for k in c["after"]:
            pre.setdefault(k, False)
        pre.pop(i, None)
        c["pre"] = [(k, s and not (c["q"] == "pe" and calls[k]["q"] == "pe")) for k, s in pre.items()]
        for (regs, writing) in ((c["r"], False), (c["w"], True)):
            for (name, lo, hi) in regs:
                lst = hist.setdefault(name, [])
                if writing:
                    lst[:] = [e for e in lst if not (lo <= e[0] and e[1] <= hi)]
                lst.append((lo, hi, writing, i))
                if name[0] == "P" and name[1:].isdigit():
                    bank_last[name] = i


def order(calls):
    n = len(calls)
    wire = 0.0
    for c in calls:
        if c["bytes"]:
            wire = (wire if c["seq"] else 0.0) + c["bytes"] / BPU
            c["late"] = DMA0 + wire
    succ = [[] for _ in range(n)]
    pred = [[] for _ in range(n)]
    for i, c in enumerate(calls):
        for (k, s) in c["pre"]:
            d = (SEM + calls[k]["late"]) if s else 0.0
            if c["ext"] is not None and calls[k]["send"]:
                d = FLY
            succ[k].append((i, d))
            pred[i].append((k, d))

    def place(before, after, rank, first):
        left = [len(b) for b in before]
        ready = sorted((rank[i], i) for i in range(n) if left[i] == 0)
        busy = {}
        end = [0.0] * n
        while ready:
            i = ready.pop(0)[1]
            at = max([first[i]] + [end[k] + d for (k, d) in before[i]])
            lst = busy.setdefault(calls[i]["q"], [])
            k = len(lst)
            while k > 0 and lst[k - 1][1] > at:
                k -= 1
            while k < len(lst) and lst[k][0] < at + calls[i]["us"] - 1e-9:
                at = max(at, lst[k][1])
                k += 1
            end[i] = at + calls[i]["us"]
            lst.insert(k, (at, end[i]))
            for (j, d) in after[i]:
                left[j] -= 1
                if left[j] == 0:
                    ready.append((rank[j], j))
            ready.sort()
        return end

    late = [c["late"] for c in calls]
    way = [0.0] * n
    left = [len(s) for s in succ]
    chain = [i for i in range(n) if left[i] == 0]
    for i in chain:
        way[i] = calls[i]["us"] + max([d + way[j] for (j, d) in succ[i]] + [late[i]])
        for (k, d) in pred[i]:
            left[k] -= 1
            if left[k] == 0:
                chain.append(k)
    end = place(pred, succ, [-way[i] - calls[i]["lead"] for i in range(n)], [0.0] * n)
    best = (max(end[i] + late[i] for i in range(n)), end)
    for _ in range(PASSES):
        back = place(succ, pred, [-end[i] - late[i] for i in range(n)], late)
        end = place(pred, succ, [-back[i] for i in range(n)], [0.0] * n)
        span = max(end[i] + late[i] for i in range(n))
        if span < best[0]:
            best = (span, end)
    end = best[1]
    return sorted(range(n), key=lambda i: (end[i] - calls[i]["us"], end[i]))


def issue(g, T, calls):
    queues = {"pe": g.tensor, "dve": g.vector, "act": g.scalar, "pool": g, "sync": g.sync}
    known = {q: {} for q in queues}
    count = {}
    ndma = 0

    def wait_for(q, src, n, clock):
        if known[q].get(src, 0) >= n:
            return
        queues[q].wait_ge(T.sem[src], n)
        known[q][src] = n
        for k, v in clock.items():
            if known[q].get(k, 0) < v:
                known[q][k] = v

    link(calls)
    for i in order(calls):
        c = calls[i]
        q = c["q"]
        tag = c["tag"]
        need = {}
        for (k, s) in c["pre"]:
            if s:
                src, n, clock = calls[k]["done"]
                if need.get(src, (0, None))[0] < n:
                    need[src] = (n, clock)
        for src in sorted(need):
            if not any(o != src and need[o][1].get(src, 0) >= need[src][0] for o in need):
                wait_for(q, src, need[src][0], need[src][1])
        if c["ext"] is not None:
            wait_for(q, c["ext"][0], c["ext"][1], {})
        ins = c["fn"]()
        if c["send"]:
            continue
        src, step = q, 1
        if c["bytes"]:
            src, step = "d%d" % ndma, 16
            ndma += 1
        ins.then_inc(T.sem[src], step)
        count[src] = count.get(src, 0) + step
        clock = dict(known[q])
        clock[src] = count[src]
        c["done"] = (src, count[src], clock)
    for src in count:
        wait_for("sync", src, count[src], {})


def rank_program(g, core, T, topo):
    rank = T.rank_of(core)
    if rank is None:
        return
    cores = list(T.cores)
    n = len(cores)
    V, S_, PE = g.vector, g.scalar, g.tensor
    calls = []
    now = {"tag": "init", "seq": None, "lead": 0.0}

    def op(q, fn, us, r=(), w=(), ext=None, after=(), nbytes=0, send=False, late=0.0):
        seq = now["seq"] and q != "pe" and (now["seq"], q) or None
        calls.append(dict(q=q, fn=fn, us=us, r=_norm(r), w=_norm(w), ext=ext, after=list(after) + now.pop("gate", []),
                          bytes=nbytes, send=send, late=late, seq=seq, tag=now["tag"], lead=now["lead"]))
        return len(calls) - 1

    def vec(cyc):
        return max(64, cyc) * CYC

    def gat(k):
        return 0.05 + k * GAT * CYC

    def ts(out, in0, s1, s2, o0, o1, r, w, us=vec(0), ext=None, after=()):
        if o1 is None:
            return op("dve", lambda: V.tensor_scalar(out, in0, s1, None, o0), us, r, w, ext, after)
        return op("dve", lambda: V.tensor_scalar(out, in0, s1, s2, o0, o1), us, r, w, ext, after)

    def tt(out, in0, in1, o, r, w, us=vec(0)):
        return op("dve", lambda: V.tensor_tensor(out, in0, in1, o), us, r, w)

    def cp(out, in_, r, w, us=vec(0)):
        return op("dve", lambda: V.tensor_copy(out, in_), us, r, w)

    def ms(ap, c, w, us=vec(0)):
        return op("dve", lambda: V.memset(ap, c), us, (), w)

    def scan(out, d0, d1, r, w, k):
        return op("dve", lambda: V.tensor_tensor_scan(out, d0, d1, 0.0, A.add, A.max), vec(k), r, w)

    def act(out, in_, f, r, w, k, bias=0.0, scale=1.0, acc=None, ext=None, after=(), gather=False):
        us = gat(k) if gather else ACT0 + k * CYC
        return op("act", lambda: S_.activation(out, in_, f, bias=bias, scale=scale, accum_out=acc), us, r, w, ext, after)

    def mm(out, lhsT, rhs, st, sp, r, w, k, after=()):
        return op("pe", lambda: PE.matmul(out, lhsT, rhs, st, sp), PE0 + max(64, k) * PEC, r, w, late=0.05, after=after)

    def dma(q, out, in_, r, w, nbytes):
        eng = g.sync if q == "sync" else g.scalar
        return op(q, lambda: eng.dma_start(out, in_), 0.06, r, w, nbytes=nbytes)

    def iota(out, pat, base, cm, w, k, flt=True, after=()):
        us = 0.13 + 2 * k * CYC
        if flt:
            op("pool", lambda: g.iota(out, pat, base, cm, allow_small_or_imprecise_dtypes=True), us, (), w, after=after)
        else:
            op("pool", lambda: g.iota(out, pat, base, cm), us, (), w, after=after)

    def sel(out, in_, pat, cmp, fill, base, cm, r, w, k, after=()):
        op("pool", lambda: g.affine_select(out, in_, pat, cmp, fill, base, cm), 0.17 + 2 * k * CYC, r, w, after=after)

    peers = [cores[(rank + k) % n] for k in range(1, n)]
    mask = topo.mask(core, peers[0])
    for c in peers[1:]:
        mask &= topo.mask(core, c)
    neng = bin(mask).count("1")
    ids = [DstId(rid=topo.addr(c)[0], pnc=topo.addr(c)[1]) for c in peers]
    sends = [0]

    def send(src, dsts, sem, r):
        def fn():
            tr = RemoteDMATransfer(dst_ids=ids, dma_engine_mask=mask, remote_sem=T.sem[sem], src=src, dsts=dsts)
            return g.remote_dma_fused([tr], local_sem=T.sem.sent)
        sends[0] += neng
        return op("pool", fn, CALL if sends[0] > neng else CALL1, r, (), send=True)

    def col(k):
        return T.PC[:, k:k + 1]

    def pc(*ks):
        return [("PC", k, k + 1) for k in ks]

    def rg(name, a, b):
        return (name, a, b)

    P = [T["P%d" % k] for k in range(8)]
    pn = lambda k, a=0, b=512: ("P%d" % k, a, b)

    ms(T.ZR[:], 0.0, ["ZR"], vec(240))
    now["seq"] = "load"
    dma("sync", T.AN[:], T.a0[:], (), ["AN"], 32768)
    dma("act", T.FR[:, 0:256], T.fr[:, 0:256], (), [("FR", 0, 256)], 65536)
    dma("act", T.S[:], T.s0[:], (), ["S"], 8192)
    dma("act", T.MX[:, 2048:2056], T.mix[:, 0:8], (), [("MX", 2048, 2056)], 4096)
    for (a, b) in ((0, 1536), (1536, 3072), (3072, 4096)):
        dma("sync", T.MU[:, a:b], T.mu[:, a:b], (), [("MU", a, b)], 256 * (b - a))
    dma("sync", T.MX[:, 0:2048], T.mix[:], (), [("MX", 0, 2048)], 1048576)
    dma("sync", T.FR[:, 256:1024], T.fr[:, 256:1024], (), [("FR", 256, 1024)], 196608)
    for a in range(0, 4256, 480):
        b = min(a + 480, 4256)
        dma("sync", T.JJ[:, a:b], T.ZR[:, 0:b - a], ["ZR"], [rg("JJ", a, b)], 256 * (b - a))
    for k in range(8):
        dma("sync", T.VP[:, 2 * k:2 * k + 2, :], T.ZR[:], ["ZR"], [rg("VP", 2 * k, 2 * k + 2)], 122880)
    now["seq"] = None

    now["seq"] = "main"
    iota(T.IP[:, 0:1], [[0, 1]], 0, 1, [("IP", 0, 1)], 1, flt=False)
    iota(T.SLI[:], [[128, 8]], 0, 1, ["SLI"], 8, flt=False)
    iota(T.K16[:], [[128, 2], [2, 8]], 0, 0, ["K16"], 16)
    ip = [("IP", 0, 1)]
    ms(T.LN[:], 0.0, ["LN"], vec(512))
    ts(T.IP[:, 1:2], T.IP[:, 0:1], 15, None, A.bitwise_and, None, ip, [("IP", 1, 2)])
    ts(T.IP[:, 2:3], T.IP[:, 0:1], 7, None, A.bitwise_and, None, ip, [("IP", 2, 3)])
    ts(T.IP[:, 3:4], T.IP[:, 0:1], 3, 1, A.logical_shift_right, A.bitwise_and, ip, [("IP", 3, 4)])
    cp(T.SL[:], T.SLI[:], ["SLI"], ["SL"])
    ts(T.SLB[:], T.SLI[:, 4:8], -512.0, None, A.add, None, ["SLI"], ["SLB"])
    ms(T.Q64[:], 1.0 / 64, ["Q64"])
    cp(T.PC[:, 0:4], T.IP[:, 0:4], ["IP"], [("PC", 0, 4)])
    ms(T.BL[0:2, :], 1.0 / 128, ["BL"])
    ms(T.BR[0:2, :], 1.0, ["BR"], vec(256))
    PF, PM = col(0), col(1)
    ts(col(10), col(2), 16.0, col(3), A.mult, A.add, pc(2, 3), pc(10))
    ms(T.BL[0:1, :], 192.0, ["BL"])
    ms(T.ONE[:], 1.0, ["ONE"])
    ms(T.NEG[:], -1.0, ["NEG"])
    ts(T.PL[:], T.K16[:], col(10), None, A.add, None, pc(10) + ["K16"], ["PL"])
    now["seq"] = None
    iota(T.CI[:], [[1, 144]], 0, 0, ["CI"], 144)
    ts(T.I16[:], T.CI[:, 0:16], PM, 64.0, A.is_equal, A.mult, pc(1) + ["CI"], ["I16"])

    def lin(k, src, scale, bias, r=()):
        act(col(k), col(src), F.Identity, pc(src, *r), pc(k), 1, bias=bias, scale=scale)

    lin(11, 1, -1.0, 15.0)
    lin(5, 1, -512.0, 2048.5)
    lin(6, 1, 128.0, 2191.0)
    lin(9, 0, 1.0, col(11), (11,))
    ts(col(7), PM, 15.0, 8192.0, A.is_equal, A.mult, pc(1), pc(7))
    lin(8, 7, 1.0, -6144.0)
    ts(T.WB[:], T.CI[:], col(9), -4096.0, A.is_equal, A.mult, pc(9) + ["CI"], ["WB"], vec(144))
    for hf in range(2):
        a = 4112 * hf + 2048
        iota(T.D[:, a:a + 16], [[0, 16]], 0, 0, [rg("D", a, a + 16)], 16)
    sel(T.ID[:], T.ONE[:, 0:128], [[-1, 128]], A.is_equal, 0.0, 0, 1, ["ONE"], ["ID"], 128)
    sel(T.NID[:], T.NEG[:, 0:128], [[-1, 128]], A.is_equal, 0.0, 0, 1, ["NEG"], ["NID"], 128)
    iota(T.C16[:], [[0, 8], [1, 16]], 0, 0, ["C16"], 128)
    ts(T.JJ[:, 2064:2192], T.C16[:], PM, None, A.is_equal, None, pc(1) + ["C16"], [rg("JJ", 1920, 2400)], vec(128))
    act(T.SC2[:], T.JJ[:, 2064:2192], F.Identity, [rg("JJ", 1920, 2400)], ["SC2"], 128, scale=-1.0e9)
    act(T.SC3[:], T.JJ[:, 2063:2191], F.Identity, [rg("JJ", 1920, 2400)], ["SC3"], 128, scale=8192.0)
    tt(T.SC2[:], T.SC2[:], T.SC3[:], A.add, ["SC2", "SC3"], ["SC2"], vec(256))
    iota(T.SC1[:], [[0, 256]], 1, 0, ["SC1"], 256)
    iota(T.SC1[:, 0:256:32], [[0, 8]], -16000000, 0, ["SC1"], 8)
    iota(T.SC1[:, 16:256:32], [[0, 8]], 2049, 0, ["SC1"], 8)
    iota(T.JB[0:1, :], [[-16, 8], [0, 32]], 112, 0, ["JB"], 256)
    sel(T.BT[:], T.ONE[:, 0:128], [[-16, 8], [0, 16]], A.is_ge, 0.0, 0, 1, ["ONE"], ["BT"], 128)
    sel(T.BF[:], T.BT[:], [[16, 8], [0, 16]], A.is_ge, 0.0, 15, -1, ["BT"], ["BF"], 128)
    cp(T.BH[:], T.BF[:], ["BF"], ["BH"], vec(128))
    for (buf, src) in (("E1", "NEG"), ("E3", "ONE")):
        sel(T[buf][:], T[src][:], [[-16, 8], [-1, 17]], A.is_equal, 0.0, 0, 1, [src], [buf], 136)
        iota(T[buf][:, 16:136:17], [[0, 8]], 0, 0, [buf], 8)
    sel(T.E2[:], T.ONE[:], [[-16, 8], [0, 17]], A.is_equal, 0.0, 0, 1, ["ONE"], ["E2"], 136)
    for (buf, up) in (("LOC", 0), ("HIC", 1)):
        iota(T[buf][:, 0:64:4], [[0, 16]], 8 * up, 0, [(buf, 0, 1)], 16)
        iota(T[buf][:, 1:64:4], [[0, 2], [4, 2], [0, 4]], 4 * up, 0, [(buf, 1, 2)], 16)
        iota(T[buf][:, 2:64:4], [[0, 2], [2, 4], [0, 2]], 2 * up, 0, [(buf, 2, 3)], 16)
        iota(T[buf][:, 3:64:4], [[0, 2], [1, 8]], up, 0, [(buf, 3, 4)], 16)
    ts(T.KA[:], T.LOC[:], PM, 256.0, A.is_equal, A.mult, pc(1) + ["LOC"], ["KA"])
    ts(T.KB[:], T.HIC[:], PM, 256.0, A.is_equal, A.mult, pc(1) + ["HIC"], ["KB"])
    tt(T.KA[:], T.KA[:], T.KB[:], A.subtract, ["KA", "KB"], ["KA"], vec(128))
    lin(4, 1, -1.0, 0.0)
    act(T.VC[:, 0:32], T.LOC[:, 0:32], F.Identity, pc(1) + ["LOC"], [("VC", 0, 32)], 32, scale=16.0, bias=PM)
    act(T.VC[:, 32:64], T.HIC[:, 32:64], F.Identity, pc(4) + ["HIC"], [("VC", 32, 64)], 32, scale=-16.0, bias=col(4))
    iota(T.SCS[:], [[0, 64]], 0, 0, ["SCS"], 64)
    iota(T.SCS[:, 0:64:4], [[0, 16]], -16000000, 0, ["SCS"], 16)
    iota(T.CUM[:, 128:144], [[0, 16]], n * 128, 0, [("CUM", 128, 144)], 16)
    for t in range(R):
        a, b = 256 * t, 256 * t + 256
        now["seq"] = None if t else "main"
        act(T.FP[:, a:b], T.FR[:, a:b].indirect(T.PL[:, 0:16]), F.Identity, [rg("FR", a, b), "PL"], [rg("FP", a, b)],
            256, bias=192.0, gather=True)
        now["seq"] = None
        act(T.FX[:, a:b], T.FR[:, a:b], F.Identity, [rg("FR", a, b)], [rg("FX", a, b)], 256, bias=192.0)
        for hf in range(2):
            a, b = 256 * t + 128 * hf, 256 * t + 128 * hf + 128
            sel(T.XZ[:, a:b], T.FX[:, a:b], [[0, 8], [-1, 16]], A.is_ge, 0.0, RAW[hf] - 1, 0, [rg("FX", a, b)],
                [rg("XZ", a, b)], 128)

    def xrep(t, u0, u1, q, after=(), slots=range(16)):
        a, b, k = 256 * t + u0, 256 * t + u1, u1 - u0
        for i in slots:
            out, w = T.XR[:, 16 * a + i:16 * b:16], [("XR%d#%d" % (t, h), i, i + 1) for h in range(u0 // 128, u1 // 128)]
            if q == "dve":
                cp(out, T.FP[:, a:b], [("FP", a, b)], w, vec(k // 2))
            elif q == "act":
                act(out, T.FP[:, a:b], F.Identity, [("FP", a, b)], w, k, after=after)
            else:
                sel(out, T.FP[:, a:b], [[0, k]], A.is_equal, 0.0, 0, 0, [("FP", a, b)], w, k, after=after)

    def spread(hv, src, name, dst="L"):
        lst, ln = (T.SL[:, 0:4], "SL") if hv == 0 else (T.SLB[:, 0:4], "SLB")
        tt(T[dst][:, 512 * hv:512 * hv + 512].indirect(lst), src[:, 64 * hv:64 * hv + 64], T.Q64[:], A.mult,
           [rg(name, 64 * hv, 64 * hv + 64), ln, "Q64"], [rg(dst, 512 * hv, 512 * hv + 512)], 0.05 + 64 * SCA * CYC)

    def preload(after=()):
        for c in VCLS:
            mm(P[c][:], T.BL[0:2, :], T.BR[0:2, :], True, False, ["BL", "BR"], [pn(c)], 512, after)

    def turn(src, bank):
        for c in range(8):
            mm(P[bank][:, 16 * c:16 * c + 16], T[src][:, 128 * c:128 * c + 128], T.I16[:], True, True,
               [rg(src, 128 * c, 128 * c + 128), "I16"], [pn(bank)], 16)
        act(T.AB[:], P[bank][:, 0:128], F.Identity, [pn(bank)], ["AB"], 128)

    def lists():
        cp(T.S2[:, 0:16], T.S[:], ["S"], [("S2", 0, 16)])
        ts(T.S2[:, 16:32], T.S[:], 1.0, None, A.add, None, ["S"], [("S2", 16, 32)])

    def cands(first):
        k = 128 if first else 256
        for a in range(0, 512, k):
            lst = T.S2[:, a // 16:(a + k) // 16]
            if first:
                ts(T.CF[:, a:a + k], T.MX[:, 0:2056].indirect(lst), -2048.0, None, A.add, None, ["MX", "S2"],
                   [rg("CF", a, a + k)], gat(k))
            else:
                act(T.CF[:, a:a + k], T.MXF[:, 0:2056].indirect(lst), F.Identity, ["MXF", "S2"], [rg("CF", a, a + k)],
                    k, bias=-2048.0, gather=True)
            ts(T.CL[:, a:a + k], T.CF[:, a:a + k].indirect(T.PL[:, 0:k // 16]), 2048.0, None, A.add, None,
               [rg("CF", a, a + k), "PL"], [rg("CL", a, a + k)], gat(k))

    preload()
    now["seq"] = "main"
    for hv in range(2):
        spread(hv, T.AN, "AN", "LN")
        a, b = 512 * hv, 512 * hv + 512
        op("dve", lambda a=a, b=b: V.transpose(T.L[:, a:b], T.LN[:, a:b]), vec(256), [rg("LN", a, b)], [rg("L", a, b)])
    xrep(0, 0, 128, "act", slots=range(X0))
    xrep(0, 0, 128, "dve", slots=range(X0, 16))
    lists()
    now["seq"] = None
    xrep(0, 128, 256, "pool")
    cands(True)
    for a in range(0, 2056, 514):
        sel(T.MXF[:, a:a + 514], T.MX[:, a:a + 514], [[0, 514]], A.is_equal, 0.0, 0, 0, ["MX"], [rg("MXF", a, a + 514)], 514)
    BIAS = 192.0 + 1.0 / 128
    win = T.MW[:, 0:4096]

    for t in range(R):
        last = t == R - 1
        now["tag"], now["seq"] = "%d means" % t, "main"
        for c in range(8):
            mm(P[c][:], T.L[:, 128 * c:128 * c + 128], T.MU[:, 512 * c:512 * c + 512], c not in VCLS, True,
               [rg("L", 128 * c, 128 * c + 128), rg("MU", 512 * c, 512 * c + 512)], [pn(c)], 512)
        for tok in MORDER.split():
            lo, hi = [256 * int(v) for v in tok[1:].split(":")]
            c = lo // 512
            a, b = lo - 512 * c, hi - 512 * c
            if tok[0] == "A":
                act(T.MW[:, lo:hi], P[c][:, a:b], F.Identity, [pn(c)], [rg("MW", lo, hi)], hi - lo,
                    bias=0.0 if c in VCLS else BIAS)
            elif tok[0] == "D":
                ts(T.MW[:, lo:hi], P[c][:, a:b], 184.0, 199.0, A.max, A.min, [pn(c)], [rg("MW", lo, hi)], vec(hi - lo))
            else:
                ts(T.MW[:, lo:hi], T.MW[:, lo:hi], 184.0, 199.0, A.max, A.min, [rg("MW", lo, hi)], [rg("MW", lo, hi)],
                   vec((hi - lo) // 2))
        now["seq"] = None
        if t == 0:
            turn("LN", 4)
        if last:
            turn("L", 4)

        slot = {}
        scored = [0, 0]
        mark = {}
        nar = []
        tn = lambda k: ("TT", k, k + 1)
        nown = rg("NL", 16 * t + 8, 16 * t + 10)

        def run(h, r0, r1):
            a, k = 4112 * (r0 // 16) + 2064 * h + 128 * (r0 % 16), 128 * (r1 - r0)
            return (a, a + k, 256 * h + 8 * r0, 256 * h + 8 * r1, T.XR[:, 4096 * t + 128 * r0:4096 * t + 128 * r1],
                    "XR%d#%d" % (t, r0 // 16), T.D2[:, 16 * r0 + h:16 * r1:2, :], rg("D2#%d" % h, r0, r1))

        def cgath(h, r0, r1):
            a, b, e0, e1, x, xn, _, _ = run(h, r0, r1)
            bank = slot[h, r0] = CBANK[len(slot)]
            act(T.D[:, a:b], win.indirect(T.CL[:, e0:e1]), F.Identity, ["MW", rg("CL", e0, e1)], [rg("D", a, b)],
                b - a, gather=True)
            mm(P[bank][:, 0:b - a], T.NID[:], x, True, False, ["NID", xn], [pn(bank)], b - a)
            mm(P[bank][:, 0:b - a], T.ID[:], T.D[:, a:b], False, True, ["ID", rg("D", a, b)], [pn(bank)], b - a)

        def csq(h, r0, r1):
            a, b, _, _, _, _, d2, dn = run(h, r0, r1)
            act(d2, P[slot[h, r0]][:, 0:b - a], F.Square, [pn(slot[h, r0])], [dn], b - a)

        def gath(h, r0, r1):
            a, b, e0, e1, x, xn, _, _ = run(h, r0, r1)
            tt(T.D[:, a:b], win.indirect(T.CL[:, e0:e1]), x, A.subtract, ["MW", rg("CL", e0, e1), xn], [rg("D", a, b)],
               gat(b - a))

        def sq(h, r0, r1):
            a, b, _, _, _, _, d2, dn = run(h, r0, r1)
            act(d2, T.D[:, a:b], F.Square, [rg("D", a, b)], [dn], b - a)

        def vsq(h, r0, r1):
            a, b, _, _, _, _, d2, dn = run(h, r0, r1)
            tt(d2, T.D[:, a:b], T.D[:, a:b], A.mult, [rg("D", a, b)], [dn], vec(b - a))

        def score(r0, r1):
            hf = r0 // 16
            bank = HBANK[hf][0]
            if scored[hf] == 0:
                mm(P[bank][:, 0:256], T.ONE[0:1, 0:128], T.JB[0:1, :], True, False, ["ONE", "JB"], [pn(bank)], 256)
            for r in range(r0, r1):
                scored[hf] += 1
                mm(P[bank][:, 0:256], T.WB[:, 15 - r % 16:143 - r % 16], T.D2[:, 16 * r:16 * r + 16, :], False,
                   scored[hf] == 16, ["WB", rg("D2#0", r, r + 1), rg("D2#1", r, r + 1)], [pn(bank)], 256)

        def half(hf):
            now["tag"], now["seq"] = "%d%s" % (t, "ab"[hf]), None
            j0, j1 = 8 * hf, 8 * hf + 8
            u0, u1 = 128 * hf, 128 * hf + 128
            bk, bx, by, bv = HBANK[hf]
            mark["Z"] = scan(T.SK[:, 32 * j0:32 * j1], T.SC1[:], P[bk][:, 0:256], ["SC1", pn(bk)],
                             [rg("SK", 32 * j0, 32 * j1)], 256)
            ts(T.RO[:, j0:j1], T.SK[:, 32 * j0 + 31:32 * j1:32], 4095, None, A.bitwise_and, None,
               [rg("SK", 32 * j0, 32 * j1)], [rg("RO", j0, j1)])
            mark["L"] = ts(T.RL[:, j0:j1], T.RO[:, j0:j1], -1.0, 2191.0, A.mult, A.add, [rg("RO", j0, j1)],
                           [rg("RL", j0, j1)])
            ts(T.OF[:, j0:j1], T.RO[:, j0:j1], -1.0, col(6), A.mult, A.add, [rg("RO", j0, j1)] + pc(6), [rg("OF", j0, j1)])
            for h in range(2):
                a, b = 256 * h + u0, 256 * h + u1
                mark["C"] = tt(T.CM[:, a:b], T.JJ[:, 2064 - 2064 * h:4256 - 2064 * h].indirect(T.RL[:, j0:j1]),
                               T.CF[:, a:b], A.mult, ["JJ", rg("RL", j0, j1), rg("CF", a, b)], [rg("CM", a, b)], gat(128))
            for bank in (bx, by):
                for h in range(2):
                    a, b = 256 * h + u0, 256 * h + u1
                    mark["B"] = mm(P[bank][:, 0:128], T.BH[:], T.CM[:, a:b], h == 0, h == 1, ["BH", rg("CM", a, b)],
                                   [pn(bank)], 128)
            scan(T.SW[:, u0:u1], T.SC2[:], P[bx][:, 0:128], ["SC2", pn(bx)], [rg("SW", u0, u1)], 128)
            mark["W"] = ts(T.WL[:, j0:j1], T.SW[:, u0 + 15:u1:16], col(8), None, A.add, None,
                           [rg("SW", u0, u1)] + pc(8), [rg("WL", j0, j1)])
            mark["S"] = act(T.SG[:, u0:u1], P[by][:, 0:128], F.Sign, [pn(by)] + pc(5),
                            [rg("SG", u0, u1), rg("NL", 16 * t + 8 + hf, 16 * t + 9 + hf)], 150, bias=col(5),
                            acc=T.NL[:, 16 * t + 8 + hf:16 * t + 9 + hf])
            if t == 0:
                nar.append(send(T.NL[:, 8 + hf:9 + hf], [T.NL[:, 2 * k + hf:2 * k + hf + 1] for k in range(1, n)],
                                "nar0", [rg("NL", 8 + hf, 9 + hf)]))
            elif hf == 1:
                nar.append(send(T.NL[:, 16 * t + 8:16 * t + 10],
                                [T.NL[:, 16 * t + 2 * k:16 * t + 2 * k + 2] for k in range(1, n)], "nar%d" % t, [nown]))
            def affine(step, out, in_, r, w, k, scale=1.0, bias=0.0, gather=False):
                if step in ON_VECTOR[hf]:
                    ts(out, in_, scale, bias, A.mult, A.add, r, w, gat(k) if gather else vec(k))
                else:
                    act(out, in_, F.Identity, r, w, k, bias=bias, scale=scale, gather=gather)

            bc = bx if "C" in ON_VECTOR[hf] else by
            affine("C", T.CS[:, u0:u1], P[bc][:, 0:128], [pn(bc)], [rg("CS", u0, u1)], 128, 1.0 / 16,
                   6144.0 + 128.0 - 255.5 / 16)
            affine("E", T.EG[:, u0:u1], T.D[:, 4112 * hf:4112 * hf + 4112].indirect(T.OF[:, j0:j1]),
                   [rg("D", 4112 * hf, 4112 * hf + 4112), rg("OF", j0, j1)], [rg("EG", u0, u1)], 128, 1.0, 0.0, True)
            affine("V", T.VG[:, u0:u1], T.MU[:, 0:4096].indirect(T.WL[:, j0:j1]), ["MU", rg("WL", j0, j1)],
                   [rg("VG", u0, u1)], 128, -1.0 if last else 1.0, 0.0, True)
            xz, xn = T.XZ[:, 256 * t + u0:256 * t + u1], rg("XZ", 256 * t + u0, 256 * t + u1)
            eg, vg = T.EG[:, u0:u1], T.VG[:, u0:u1]
            if last:
                mm(P[bv][:, 0:128], xz, T.ID[:], True, False, [xn, "ID"], [pn(bv)], 128)
                mm(P[bv][:, 0:128], eg, T.NID[:], False, True, [rg("EG", u0, u1), "NID"], [pn(bv)], 128)
                mm(P[bk][:, 0:136], T.CS[:, u0:u1], T.E2[:], True, False, [rg("CS", u0, u1), "E2"], [pn(bk)], 136)
                mm(P[bk][:, 0:136], vg, T.E1[:], False, True, [rg("VG", u0, u1), "E1"], [pn(bk)], 136)
            else:
                mm(P[bk][:, 0:136], xz, T.E3[:], True, False, [xn, "E3"], [pn(bk)], 136)
                mm(P[bk][:, 0:136], eg, T.E1[:], False, False, [rg("EG", u0, u1), "E1"], [pn(bk)], 136)
                mm(P[bk][:, 0:136], T.CS[:, u0:u1], T.E2[:], False, True, [rg("CS", u0, u1), "E2"], [pn(bk)], 136)
                mm(P[bv][:, 0:128], vg, T.ID[:], True, True, [rg("VG", u0, u1), "ID"], [pn(bv)], 128)
            affine("P", T.VP[:, j0:j1, 112:128], P[bv][:, 0:128], [pn(bv)], [rg("VP", j0, j1)], 128)
            affine("T", T.TT[:, j0, :], P[bk][:, 0:136], [pn(bk)], [tn(j0)], 136, 1.0, 16.0 - 6144.0)
            for c in range(1, 8):
                if c in RELU_ACT[hf]:
                    act(T.TT[:, j0 + c, :], T.TT[:, j0, :], F.Relu, [tn(j0)], [tn(j0 + c)], 136, bias=-32.0 * c)
                else:
                    mark["R"] = ts(T.TT[:, j0 + c, :], T.TT[:, j0, :], -32.0 * c, 0.0, A.add, A.max, [tn(j0)],
                                   [tn(j0 + c)], vec(68))
            a = 256 * t + u0
            act(T.YW[:, a:a + 128], P[by][:, 0:128], F.Identity, [pn(by)], [rg("YW", a, a + 128)], 128, bias=2048.0)

        def sums(hf):
            now["tag"], now["seq"] = "%d%s" % (t, "ab"[hf]), None
            j0, j1 = 8 * hf, 8 * hf + 8
            prev = []
            for cv in range(len(CUT) - 1):
                c0, c1 = CUT[cv], CUT[cv + 1]
                for s in range(8):
                    prev = [mm(P[6 + cv][:, 0:17 * (c1 - c0)], T.VP[:, j0 + s, 112 - 16 * s:240 - 16 * s],
                               T.TT[:, j0 + c0:j0 + c1, 17 * s:17 * s + 17], hf == 0 and s == 0, hf == 1 and s == 7,
                               [rg("VP", j0, j1), rg("TT", j0 + c0, j0 + c1)], [pn(6 + cv)], 17 * (c1 - c0), prev)]

        steps = {"c": cgath, "q": csq, "g": gath, "s": sq, "v": vsq, "m": score, "w": half, "u": sums}
        for tok in (PLAN if t else PLAN0).replace("\n", "").split("|"):
            f = tok.split()
            now["tag"], now["seq"] = "%d%s" % (t, f[0]), "main"
            if f[0] in mark:
                now["gate"] = [mark[f[0]]]
            else:
                steps[f[0]](*[int(v) for v in f[1:]])
        now["tag"], now["seq"] = "%dp" % t, None
        for cv in range(len(CUT) - 1):
            for c in range(CUT[cv], CUT[cv + 1]):
                a, c0 = 128 * t + 16 * c, 17 * (c - CUT[cv])
                ts(T.GS[:, a:a + 16], P[6 + cv][:, c0:c0 + 16], P[6 + cv][:, c0 + 16:c0 + 17], 32768.0,
                   A.subtract, A.add, [pn(6 + cv)], [rg("GS", a, a + 16)])
        gs = rg("GS", 128 * t, 128 * t + 128)
        gar = send(T.GS[:, 128 * t:128 * t + 128],
                   [T.GL[:, 384 * t + 128 * k:384 * t + 128 * k + 128] for k in range(n - 1)], "gar%d" % t, [gs])
        now["tag"] = "%dx" % t
        if not last and XENG[t] == "act":
            xrep(t + 1, 0, 256, "act", nar)
        if t + 2 < R and XENG[t + 1] == "pool":
            xrep(t + 2, 0, 256, "pool", [gar])
        if t == 2:
            iota(T.IW[:, 0:2048], [[1, 2048]], 0, 0, [("IW", 0, 2048)], 2048, after=[gar])
            iota(T.IW[:, 2048:2056], [[1, 8]], 0, 0, [("IW", 2048, 2056)], 8, after=[gar])

        now["tag"] = "%dh" % t
        dma("sync", T.yw[:, 256 * t:256 * t + 256], T.YW[0:128:16, 256 * t:256 * t + 256],
            [rg("YW", 256 * t, 256 * t + 256)], (), 8192)
        ts(T.HS[:], T.RO[:], 1024.0, None, A.is_lt, None, ["RO"], ["HS"])
        tt(T.S[:], T.S[:], T.HS[:], A.add, ["S", "HS"], ["S"])
        lists()
        if not last:
            cands(False)
        else:
            act(T.YS[:], T.IW[:, 0:2056].indirect(T.S2[:, 0:16]), F.Identity, ["IW", "S2"], ["YS"], 256, gather=True)
            dma("sync", T.ys[:], T.YS[0:128:16, :], ["YS"], (), 8192)

        now["tag"] = "%dtree" % t
        act(T.AM[:], T.AB[:], F.Identity, ["AB"], ["AM"], 128, bias=-127.5 / 256)
        ts(P[4][:, 0:128], T.AB[:], -2.0, -127.0, A.add, A.max, ["AB"], [pn(4, 0, 128)], vec(128))
        ts(P[4][:, 128:256], T.AB[:], 2.0, 127.0, A.add, A.min, ["AB"], [pn(4, 128, 256)], vec(128))
        if not last:
            preload([gar])
        act(T.NJ[:, 0:8], T.NL[:, 16 * t + 2:16 * t + 10], F.Identity, [nown], ["NJ"], 30, acc=T.NJ[:, 8:9],
            ext=("nar%d" % t, neng * (n - 1) * (2 if t == 0 else 1)), after=nar)
        act(T.RK[:], T.KA[:], F.Identity, ["KA", "NJ"], ["RK"], 64, scale=T.NJ[:, 8:9], bias=-519.0 * 16)
        mm(P[2][:, 0:64], T.BF[:], T.RK[:], True, True, ["BF", "RK"], [pn(2)], 256)
        tt(T.OK[:], P[2][:, 0:64], T.VC[:], A.min, [pn(2), "VC"], ["OK"])
        scan(T.SM[:], T.SCS[:], T.OK[:], ["SCS", "OK"], ["SM"], 64)
        ts(T.LH[:, 8:16], T.SM[:, 35:64:4], -1.0, None, A.mult, None, ["SM"], [("LH", 8, 16)])
        cp(T.LH[:, 0:8], T.SM[:, 3:32:4], ["SM"], [("LH", 0, 8)])
        ts(T.OWN[:], T.GS[:, 128 * t:128 * t + 128], 1.0 / 256, None, A.mult, None, [gs], ["OWN"], vec(128))

        now["tag"] = "%dupd" % t
        landed = dict(ext=("gar%d" % t, neng * (n - 1)), after=[gar])
        ts(P[0][:, 0:256], T.GL[:, 384 * t:384 * t + 256], 1.0 / 256, None, A.mult, None, [], [pn(0, 0, 256)],
           vec(256), **landed)
        ts(T.C2[:], T.GL[:, 384 * t + 256:384 * t + 384], 1.0 / 256, None, A.mult, None, [], ["C2"], vec(128), **landed)
        tt(T.C1[:], P[0][:, 0:128], T.OWN[:], A.add, [pn(0, 0, 128), "OWN"], ["C1"], vec(128))
        hv2 = [(0, 64), (64, 128)]
        for (a, b) in hv2:
            tt(P[0][:, 256 + a:256 + b], P[0][:, 128 + a:128 + b], T.C2[:, a:b], A.add,
               [pn(0, 128 + a, 128 + b), "C2"], [pn(0, 256 + a, 256 + b)])
        for (a, b) in hv2:
            tt(T.CUM[:, a:b], P[0][:, 256 + a:256 + b], T.C1[:, a:b], A.add, [pn(0, 256 + a, 256 + b), "C1"],
               [rg("CUM", a, b)])
        cw = T.CUM[:, 0:144]
        for hv, (a, b) in enumerate(hv2):
            tt(T.H[:, a:b], cw.indirect(T.LH[:, 8 + 4 * hv:12 + 4 * hv]), T.AM[:, a:b], A.subtract,
               ["CUM", "LH", "AM"], [rg("H", a, b)], gat(64))
        for hv, (a, b) in enumerate(hv2):
            tt(T.TI[:, a:b], cw.indirect(T.LH[:, 4 * hv:4 * hv + 4]), T.H[:, a:b], A.subtract,
               ["CUM", "LH", rg("H", a, b)], [rg("TI", a, b)], gat(64))
        for (a, b) in hv2:
            tt(T.T2[:, a:b], T.TI[:, a:b], P[4][:, a:b], A.max, [rg("TI", a, b), pn(4, a, b)], [rg("T2", a, b)])
        new = "YA" if last else "AB"
        for (a, b) in hv2:
            tt(T[new][:, a:b], T.T2[:, a:b], P[4][:, 128 + a:128 + b], A.min, [rg("T2", a, b), pn(4, 128 + a, 128 + b)],
               [rg(new, a, b)])
        if not last:
            for hv in range(2):
                spread(hv, T.AB, "AB")

    dma("sync", T.ya[:], T.YA[:], ["YA"], (), 65536)
    issue(g, T, calls)
    g.wait_ge(T.sem.sent, sends[0])
